import numpy as np
import ml_dtypes


def mxq(x, axis, fmt="e4m3"):
    dtype, down = {"e4m3": (ml_dtypes.float8_e4m3fn, 7), "e5m2": (ml_dtypes.float8_e5m2, 14)}[fmt]
    v = np.moveaxis(np.asarray(x, np.float32).astype(ml_dtypes.bfloat16).astype(np.float64), axis, -1)
    blocks = v.reshape(v.shape[:-1] + (-1, 32))
    amax = np.abs(blocks).max(-1, keepdims=True)
    byte = np.maximum(np.where(amax > 0, np.frexp(amax)[1] - 1 + 127, 0) - down, 1)
    scale = np.exp2(byte - 127.0)
    codes = (blocks / scale).astype(np.float32).astype(dtype).astype(np.float64)
    return np.moveaxis((codes * scale).reshape(v.shape), -1, axis)


WIDE = False


def mx_kscale(k):
    if not WIDE:
        return np.ones(k)
    levels = np.array([10, -10, 5, -5, 0])
    if k % 512:
        return np.exp2(np.random.permutation(np.resize(levels, k // 32))).repeat(32)
    a = np.empty((k // 512, 16))
    for p in range(k // 512):
        a[p, :8] = np.random.permutation(np.resize(levels, 8))
        for g in range(8):
            far = levels[np.abs(levels - a[p, g]) >= 10]
            a[p, g + 8] = far[np.random.randint(len(far))]
    return np.exp2(a.ravel()).repeat(32)


def f64(x):
    return np.asarray(x).astype(np.float64)


def striped(idx):
    return np.tile(idx.reshape(-1, 16).T, (8, 1)).astype(np.uint16)


def unstriped(offs):
    return offs[:16].T.reshape(-1).astype(np.int64)


def striped8(idx):
    return np.concatenate([x.reshape(-1, 16).T for x in idx]).astype(np.uint16)


def runs(offs, k):
    lists = np.stack([offs[16 * r : 16 * r + 16].T.reshape(-1) for r in range(8)]).astype(np.int64)
    return lists[np.arange(k) % 512 // 64]


def pack_weight(w):
    k, n = w.shape
    w = f64(np.asarray(w, np.float32).astype(ml_dtypes.bfloat16)).reshape(k // 32, 32, n)
    amax = np.abs(w).max(1)
    byte = np.clip(np.where(amax > 0, np.frexp(amax)[1] - 1 + 127 - 7, 1), 1, 254)
    scaled = (w * np.exp2(127.0 - byte)[:, None, :]).reshape(k, n).astype(np.float32)
    words = np.ascontiguousarray(scaled.reshape(k // 512, 128, 4, n).transpose(0, 1, 3, 2)).astype(ml_dtypes.float8_e4m3fn).view(np.uint8)
    return words, np.ascontiguousarray(byte.astype(np.uint8).reshape(k // 512, 16, n))


def unpack_weight(words, scales):
    g, p, n, _ = words.shape
    vals = np.ascontiguousarray(words).view(ml_dtypes.float8_e4m3fn).astype(np.float64) * np.repeat(np.exp2(scales.astype(np.float64) - 127.0), 8, axis=1)[..., None]
    return vals.transpose(0, 1, 3, 2).reshape(g * 512, n)

def planes(y):
    n, m = y.shape
    v = y.astype(np.float32).astype(ml_dtypes.bfloat16).astype(np.float64).reshape(n // 32, 32, m)
    top = np.abs(v).max(1)
    byte = np.clip(np.where(top > 0, np.frexp(top)[1] - 1 + 127 - 7, 1), 1, 254)
    codes = (v * np.exp2(127.0 - byte)[:, None, :]).reshape(n, m).astype(np.float32).astype(ml_dtypes.float8_e4m3fn).view(np.uint8)
    words = codes.reshape(n // 512, 128, 4, m).transpose(0, 1, 3, 2)
    return np.ascontiguousarray(words), np.ascontiguousarray(byte.astype(np.uint8).reshape(n // 512, 16, m))


K, T, S, V, N = 512, 2048, 512, 512, 512
P = 2 ** 7


def setup_inputs():
    n = np.random.standard_normal
    s = mx_kscale(K)[:, None]
    packed_xT = pack_weight(n((K, T)) * s)
    return {
        "x_words": packed_xT[0],
        "x_scales": packed_xT[1],
        "w1": (n((K, N)) / np.sqrt(K) / s).astype(np.float32),
        "w2": (n((K, N)) / np.sqrt(K) / s).astype(np.float32),
        "dn": np.tile(np.random.uniform(4.0, 9.0, S), (P, 1)).astype(np.float32),
        "qn": (0.5 * n((N, 1))).astype(np.float32),
        "offs": striped8(np.random.randint(0, T, (8, S))),
        "cent": striped(np.random.permutation(T)[:V]),
        "own": striped(np.random.randint(0, V, S)),
    }


def reference(x_words, x_scales, w1, w2, dn, qn, offs, cent, own):
    xq = unpack_weight(x_words, x_scales)[np.arange(K)[:, None], runs(offs, K)]
    x_cent = unpack_weight(x_words, x_scales)[:, unstriped(cent)]
    c = mxq(f64(w1), 0, "e4m3").T @ x_cent
    o = f64(dn)[:1] - (2.0 * ((mxq(f64(w2), 0, "e4m3").T @ xq) + c[:, unstriped(own)]))
    out_0 = o + f64(qn)
    return (out_0,) + planes(out_0)

@@ -1,0 +1,170 @@
+from contextlib import ExitStack
+
+import concourse.mybir as mybir
+
+K, T, S, V, N = 512, 2048, 512, 512, 512
+FLOPS = 2 * K * N * (V + S)
+
+F32 = mybir.dt.float32
+BF16 = mybir.dt.bfloat16
+I32 = mybir.dt.int32
+U32 = mybir.dt.uint32
+U16 = mybir.dt.uint16
+U8 = mybir.dt.uint8
+FP8X4 = mybir.dt.float8_e4m3fn_x4
+ALU = mybir.AluOpType
+ACT = mybir.ActivationFunctionType
+
+P = 128
+PACK = 4
+HALF = N // 2
+BANK = 512
+CHUNKS = ((0, 256), (256, 128), (384, 128))
+
+
+def tile_picked_ivfpq_none_po_kernel(
+    tc, x_words, x_scales, w1, w2, dn, qn, offs, cent, own, out_0, out_1, out_2
+):
+    nc = tc.nc
+    with ExitStack() as ctx:
+        keep = ctx.enter_context(tc.tile_pool(name="keep", bufs=1))
+        psum = ctx.enter_context(tc.psum_pool(name="psum", bufs=1))
+
+        cent_sb = keep.tile([P, V // 16], U16, name="cent_sb")
+        offs_sb = keep.tile([P, S // 16], U16, name="offs_sb")
+        own_sb = keep.tile([P, S // 16], U16, name="own_sb")
+        xs = keep.tile([P, T], U8, name="xs", tag="xs_dn", align_bytes=64)
+        xw = keep.tile([P, T], I32, name="xw", align_bytes=64)
+        qn_sb = keep.tile([P, PACK], F32, name="qn_sb")
+        warm = keep.tile([P, 2], F32, name="warm")
+        placed = keep.tile([P, V + S], U8, name="placed", align_bytes=64)
+
+        nc.gpsimd.memset(warm[:, 0:1], 0.0)
+        nc.scalar.activation(out=warm[:, 1:2], in_=warm[:, 0:1], func=ACT.Identity, bias=warm[:, 0:1], scale=-2.0)
+        nc.gpsimd.memset(placed[:].bitcast(I32), 0)
+        nc.gpsimd.dma_start(out=qn_sb[:], in_=qn.rearrange("(p t) o -> p (t o)", t=PACK))
+
+        nc.sync.dma_start(cent_sb[:], cent)
+        nc.sync.dma_start(
+            out=xs[:].bitcast(I32),
+            in_=x_scales[0].bitcast(I32).unsqueeze(1).broadcast_to([16, 8, T // 4]),
+        )
+        nc.sync.dma_start(offs_sb[:], offs)
+        nc.sync.dma_start(out=xw[:], in_=x_words[0].rearrange("p n t -> p (n t)").bitcast(I32))
+        raw = {}
+        for name, w in (("w1", w1), ("w2", w2)):
+            for h in range(2):
+                raw[name, h] = keep.tile([P, PACK, HALF], F32, name="raw_%s_%d" % (name, h))
+                nc.sync.dma_start(
+                    out=raw[name, h][:],
+                    in_=w[:, h * HALF : (h + 1) * HALF].rearrange("(p j) c -> p j c", j=PACK),
+                )
+        nc.sync.dma_start(own_sb[:], own)
+
+        picked_bytes = keep.tile([P, V + S], U8, name="picked_bytes", align_bytes=64)
+        nc.vector.tensor_copy(picked_bytes[:, 0:V], xs[:].indirect(cent_sb[:]))
+        nc.vector.tensor_copy(picked_bytes[:, V : V + S], xs[:].indirect(offs_sb[:]))
+        for r in range(4):
+            nc.scalar.dma_start(
+                out=placed[r:P:32, :].bitcast(I32), in_=picked_bytes[8 * r : P : 32, :].bitcast(I32)
+            )
+        dn_sb = keep.tile([P, S], F32, name="dn_sb", tag="xs_dn", align_bytes=64)
+        nc.sync.dma_start(out=dn_sb[:], in_=dn)
+
+        cent_words = keep.tile([P, V], U32, name="cent_words", align_bytes=64)
+        vec_words = keep.tile([P, S], U32, name="vec_words", align_bytes=64)
+        nc.vector.tensor_copy(cent_words[:], xw[:].bitcast(U32).indirect(cent_sb[:]))
+        nc.vector.tensor_copy(vec_words[:], xw[:].bitcast(U32).indirect(offs_sb[:]))
+
+        grouped, codes, scales = {}, {}, {}
+        for name in ("w1", "w2"):
+            grouped[name] = keep.tile([P, PACK, P, PACK], BF16, name="grouped_" + name, align_bytes=64)
+            codes[name] = keep.tile([P, N], U32, name="codes_" + name, align_bytes=64)
+            scales[name] = keep.tile([P, N], U8, name="scales_" + name, align_bytes=64)
+
+        def round_half(copy, name, h):
+            rows = slice(h * HALF // PACK, (h + 1) * HALF // PACK)
+            copy(
+                out=grouped[name][:, :, rows, :].rearrange("p t m j -> p m t j"),
+                in_=raw[name, h][:].rearrange("p j (m t) -> p m t j", t=PACK),
+            )
+
+        def quantize_w(name, t0, t1):
+            nc.vector.quantize_mx(
+                out=codes[name][:, t0 * P : t1 * P].bitcast(FP8X4),
+                scales=scales[name][:, t0 * P : t1 * P],
+                in_=grouped[name][:, t0:t1, :, :].rearrange("p t m j -> p (t m j)"),
+            )
+
+        def product(acc, name, t, words, first, cols):
+            nc.tensor.matmul_mx(
+                out=acc,
+                lhsT=codes[name][:, t * P : (t + 1) * P].bitcast(FP8X4),
+                lhsT_scale=scales[name][:, t * P : (t + 1) * P],
+                rhs=words[:, cols].bitcast(FP8X4),
+                rhs_scale=placed[:, first + cols.start : first + cols.stop],
+                start=True,
+                stop=True,
+            )
+
+        round_half(nc.scalar.copy, "w1", 0)
+        round_half(nc.vector.tensor_copy, "w1", 1)
+        for t in range(PACK):
+            quantize_w("w1", t, t + 1)
+        round_half(nc.scalar.copy, "w2", 0)
+        c_rows = []
+        for t in range(PACK):
+            c_ps = psum.tile([P, V], F32, name="c_ps%d" % t)
+            product(c_ps[:], "w1", t, cent_words, 0, slice(0, V))
+            c_t = keep.tile([P, V], F32, name="c_%d" % t)
+            nc.scalar.activation(out=c_t[:], in_=c_ps[:], func=ACT.Identity, bias=qn_sb[:, t : t + 1], scale=-2.0)
+            c_rows.append(c_t)
+        round_half(nc.vector.tensor_copy, "w2", 1)
+        quantize_w("w2", 0, PACK)
+
+        y_words = keep.tile([P, S], I32, name="y_words", align_bytes=64)
+        y_scales = keep.tile([P, S], U8, name="y_scales", align_bytes=64)
+        out_rows = out_0.rearrange("(p t) j -> p t j", t=PACK)
+        out_words = out_1[0].rearrange("p n t -> p (n t)").bitcast(I32)
+
+        for start, width in CHUNKS:
+            cols = slice(start, start + width)
+            per_bank = BANK // width
+            banks = []
+            for b in range(PACK // per_bank):
+                acc = psum.tile([P, per_bank, width], F32, name="rest_%d_%d" % (start, b))
+                for u in range(per_bank):
+                    product(acc[:, u, :], "w2", b * per_bank + u, vec_words, V, cols)
+                banks.append(acc)
+            near = keep.tile([P, PACK, width], F32, name="near_%d" % start)
+            for t in range(PACK):
+                nc.vector.tensor_tensor(
+                    near[:, t, :],
+                    c_rows[t][:].indirect(own_sb[:, start // 16 : (start + width) // 16]),
+                    dn_sb[:, cols],
+                    ALU.add,
+                )
+            y = keep.tile([P, PACK, width], F32, name="y_%d" % start)
+            for b, acc in enumerate(banks):
+                rows = slice(b * per_bank, (b + 1) * per_bank)
+                nc.vector.scalar_tensor_tensor(
+                    out=y[:, rows, :], in0=acc[:], scalar=-2.0, in1=near[:, rows, :], op0=ALU.mult, op1=ALU.add
+                )
+            nc.sync.dma_start(out=out_rows[:, :, cols], in_=y[:])
+            y_bf = keep.tile([P, width, PACK], BF16, name="y_bf_%d" % start, align_bytes=64)
+            nc.scalar.copy(
+                out=y_bf[:].rearrange("p (c i) t -> p c t i", i=4),
+                in_=y[:].rearrange("p t (c i) -> p c t i", i=4),
+            )
+            nc.vector.quantize_mx(
+                out=y_words[:, cols].bitcast(FP8X4),
+                scales=y_scales[:, cols],
+                in_=y_bf[:].rearrange("p c t -> p (c t)"),
+            )
+            nc.sync.dma_start(out=out_words[:, cols], in_=y_words[:, cols])
+        for q in range(4):
+            engine = nc.scalar if q % 2 else nc.sync
+            engine.dma_start(
+                out=out_2[0][4 * q : 4 * q + 4, :].bitcast(I32),
+                in_=y_scales[32 * q : 32 * q + 4, :].bitcast(I32),
+            )

@@ -33,7 +33,7 @@ def tile_picked_ivfpq_none_po_kernel(
         cent_sb = keep.tile([P, V // 16], U16, name="cent_sb")
         offs_sb = keep.tile([P, S // 16], U16, name="offs_sb")
         own_sb = keep.tile([P, S // 16], U16, name="own_sb")
-        xs = keep.tile([P, T], U8, name="xs", tag="xs_dn", align_bytes=64)
+        xs = keep.tile([P, T], U8, name="xs", tag="xs_then_late", align_bytes=64)
         xw = keep.tile([P, T], I32, name="xw", align_bytes=64)
         qn_sb = keep.tile([P, PACK], F32, name="qn_sb")
         warm = keep.tile([P, 2], F32, name="warm")
@@ -42,23 +42,25 @@ def tile_picked_ivfpq_none_po_kernel(
         nc.gpsimd.memset(warm[:, 0:1], 0.0)
         nc.scalar.activation(out=warm[:, 1:2], in_=warm[:, 0:1], func=ACT.Identity, bias=warm[:, 0:1], scale=-2.0)
         nc.gpsimd.memset(placed[:].bitcast(I32), 0)
-        nc.gpsimd.dma_start(out=qn_sb[:], in_=qn.rearrange("(p t) o -> p (t o)", t=PACK))
 
-        nc.sync.dma_start(cent_sb[:], cent)
         nc.sync.dma_start(
             out=xs[:].bitcast(I32),
             in_=x_scales[0].bitcast(I32).unsqueeze(1).broadcast_to([16, 8, T // 4]),
         )
+        nc.sync.dma_start(cent_sb[:], cent)
         nc.sync.dma_start(offs_sb[:], offs)
         nc.sync.dma_start(out=xw[:], in_=x_words[0].rearrange("p n t -> p (n t)").bitcast(I32))
         raw = {}
-        for name, w in (("w1", w1), ("w2", w2)):
-            for h in range(2):
-                raw[name, h] = keep.tile([P, PACK, HALF], F32, name="raw_%s_%d" % (name, h))
-                nc.sync.dma_start(
-                    out=raw[name, h][:],
-                    in_=w[:, h * HALF : (h + 1) * HALF].rearrange("(p j) c -> p j c", j=PACK),
-                )
+
+        def load_half(name, w, h):
+            nc.sync.dma_start(
+                out=raw[name, h], in_=w[:, h * HALF : (h + 1) * HALF].rearrange("(p j) c -> p j c", j=PACK)
+            )
+
+        for h in range(2):
+            raw["w1", h] = keep.tile([P, PACK, HALF], F32, name="raw_w1", tag="stage_%d" % h)[:]
+            load_half("w1", w1, h)
+        nc.sync.dma_start(out=qn_sb[:], in_=qn.rearrange("(p t) o -> p (t o)", t=PACK))
         nc.sync.dma_start(own_sb[:], own)
 
         picked_bytes = keep.tile([P, V + S], U8, name="picked_bytes", align_bytes=64)
@@ -68,8 +70,11 @@ def tile_picked_ivfpq_none_po_kernel(
             nc.scalar.dma_start(
                 out=placed[r:P:32, :].bitcast(I32), in_=picked_bytes[8 * r : P : 32, :].bitcast(I32)
             )
-        dn_sb = keep.tile([P, S], F32, name="dn_sb", tag="xs_dn", align_bytes=64)
-        nc.sync.dma_start(out=dn_sb[:], in_=dn)
+        late = keep.tile([P, PACK * HALF + S], F32, name="late", tag="xs_then_late", align_bytes=64)
+        raw["w2", 0] = late[:, : PACK * HALF].rearrange("p (j c) -> p j c", j=PACK)
+        dn_sb = late[:, PACK * HALF :]
+        load_half("w2", w2, 0)
+        nc.sync.dma_start(out=dn_sb, in_=dn)
 
         cent_words = keep.tile([P, V], U32, name="cent_words", align_bytes=64)
         vec_words = keep.tile([P, S], U32, name="vec_words", align_bytes=64)
@@ -78,15 +83,15 @@ def tile_picked_ivfpq_none_po_kernel(
 
         grouped, codes, scales = {}, {}, {}
         for name in ("w1", "w2"):
-            grouped[name] = keep.tile([P, PACK, P, PACK], BF16, name="grouped_" + name, align_bytes=64)
+            grouped[name] = keep.tile([P, PACK, P, PACK], BF16, name="grouped", tag="near_0" if name == "w2" else "grouped_w1", align_bytes=64)
             codes[name] = keep.tile([P, N], U32, name="codes_" + name, align_bytes=64)
             scales[name] = keep.tile([P, N], U8, name="scales_" + name, align_bytes=64)
 
-        def round_half(copy, name, h):
-            rows = slice(h * HALF // PACK, (h + 1) * HALF // PACK)
+        def round_half(copy, name, h, m0=0, m1=HALF // PACK):
+            first = h * HALF // PACK
             copy(
-                out=grouped[name][:, :, rows, :].rearrange("p t m j -> p m t j"),
-                in_=raw[name, h][:].rearrange("p j (m t) -> p m t j", t=PACK),
+                out=grouped[name][:, :, first + m0 : first + m1, :].rearrange("p t m j -> p m t j"),
+                in_=raw[name, h].rearrange("p j (m t) -> p m t j", t=PACK)[:, m0:m1, :, :],
             )
 
         def quantize_w(name, t0, t1):
@@ -108,18 +113,21 @@ def tile_picked_ivfpq_none_po_kernel(
             )
 
         round_half(nc.scalar.copy, "w1", 0)
-        round_half(nc.vector.tensor_copy, "w1", 1)
+        raw["w2", 1] = keep.tile([P, PACK, HALF], F32, name="raw_w2", tag="stage_0")[:]
+        load_half("w2", w2, 1)
+        round_half(nc.scalar.copy, "w1", 1, 0, 24)
+        round_half(nc.vector.tensor_copy, "w1", 1, 24)
         for t in range(PACK):
             quantize_w("w1", t, t + 1)
-        round_half(nc.scalar.copy, "w2", 0)
+        round_half(nc.vector.tensor_copy, "w2", 0)
+        round_half(nc.scalar.copy, "w2", 1)
         c_rows = []
         for t in range(PACK):
             c_ps = psum.tile([P, V], F32, name="c_ps%d" % t)
             product(c_ps[:], "w1", t, cent_words, 0, slice(0, V))
-            c_t = keep.tile([P, V], F32, name="c_%d" % t)
+            c_t = keep.tile([P, V], F32, name="c_t", tag="stage_0" if t == 2 else "c_%d" % t)
             nc.scalar.activation(out=c_t[:], in_=c_ps[:], func=ACT.Identity, bias=qn_sb[:, t : t + 1], scale=-2.0)
             c_rows.append(c_t)
-        round_half(nc.vector.tensor_copy, "w2", 1)
         quantize_w("w2", 0, PACK)
 
         y_words = keep.tile([P, S], I32, name="y_words", align_bytes=64)
@@ -127,7 +135,7 @@ def tile_picked_ivfpq_none_po_kernel(
         out_rows = out_0.rearrange("(p t) j -> p t j", t=PACK)
         out_words = out_1[0].rearrange("p n t -> p (n t)").bitcast(I32)
 
-        for start, width in CHUNKS:
+        for index, (start, width) in enumerate(CHUNKS):
             cols = slice(start, start + width)
             per_bank = BANK // width
             banks = []
@@ -136,19 +144,27 @@ def tile_picked_ivfpq_none_po_kernel(
                 for u in range(per_bank):
                     product(acc[:, u, :], "w2", b * per_bank + u, vec_words, V, cols)
                 banks.append(acc)
-            near = keep.tile([P, PACK, width], F32, name="near_%d" % start)
+            near = [
+                keep.tile([P, 2, width], F32, name="near", tag="near_%d" % (index + 1 - pair), align_bytes=64) if pair == 0 or index == 0 else keep.tile([P, 2, width], F32, name="near", tag="near_%d" % index, align_bytes=64)
+                for pair in range(2)
+            ]
             for t in range(PACK):
                 nc.vector.tensor_tensor(
-                    near[:, t, :],
+                    near[t // 2][:, t % 2, :],
                     c_rows[t][:].indirect(own_sb[:, start // 16 : (start + width) // 16]),
                     dn_sb[:, cols],
                     ALU.add,
                 )
             y = keep.tile([P, PACK, width], F32, name="y_%d" % start)
-            for b, acc in enumerate(banks):
-                rows = slice(b * per_bank, (b + 1) * per_bank)
+            for pair in range(2):
+                first = 2 * pair % per_bank
                 nc.vector.scalar_tensor_tensor(
-                    out=y[:, rows, :], in0=acc[:], scalar=-2.0, in1=near[:, rows, :], op0=ALU.mult, op1=ALU.add
+                    out=y[:, 2 * pair : 2 * pair + 2, :],
+                    in0=banks[2 * pair // per_bank][:, first : first + 2, :],
+                    scalar=-2.0,
+                    in1=near[pair][:],
+                    op0=ALU.mult,
+                    op1=ALU.add,
                 )
             nc.sync.dma_start(out=out_rows[:, :, cols], in_=y[:])
             y_bf = keep.tile([P, width, PACK], BF16, name="y_bf_%d" % start, align_bytes=64)

@@ -60,7 +60,8 @@ def tile_picked_ivfpq_none_po_kernel(
         for h in range(2):
             raw["w1", h] = keep.tile([P, PACK, HALF], F32, name="raw_w1", tag="stage_%d" % h)[:]
             load_half("w1", w1, h)
-        nc.sync.dma_start(out=qn_sb[:], in_=qn.rearrange("(p t) o -> p (t o)", t=PACK))
+            if h == 0:
+                nc.sync.dma_start(out=qn_sb[:], in_=qn.rearrange("(p t) o -> p (t o)", t=PACK))
         nc.sync.dma_start(own_sb[:], own)
 
         picked_bytes = keep.tile([P, V + S], U8, name="picked_bytes", align_bytes=64)
@@ -115,8 +116,7 @@ def tile_picked_ivfpq_none_po_kernel(
         round_half(nc.scalar.copy, "w1", 0)
         raw["w2", 1] = keep.tile([P, PACK, HALF], F32, name="raw_w2", tag="stage_0")[:]
         load_half("w2", w2, 1)
-        round_half(nc.scalar.copy, "w1", 1, 0, 24)
-        round_half(nc.vector.tensor_copy, "w1", 1, 24)
+        round_half(nc.vector.tensor_copy, "w1", 1)
         for t in range(PACK):
             quantize_w("w1", t, t + 1)
         round_half(nc.vector.tensor_copy, "w2", 0)
@@ -144,40 +144,39 @@ def tile_picked_ivfpq_none_po_kernel(
                 for u in range(per_bank):
                     product(acc[:, u, :], "w2", b * per_bank + u, vec_words, V, cols)
                 banks.append(acc)
-            near = [
-                keep.tile([P, 2, width], F32, name="near", tag="near_%d" % (index + 1 - pair), align_bytes=64) if pair == 0 or index == 0 else keep.tile([P, 2, width], F32, name="near", tag="near_%d" % index, align_bytes=64)
-                for pair in range(2)
-            ]
-            for t in range(PACK):
-                nc.vector.tensor_tensor(
-                    near[t // 2][:, t % 2, :],
-                    c_rows[t][:].indirect(own_sb[:, start // 16 : (start + width) // 16]),
-                    dn_sb[:, cols],
-                    ALU.add,
-                )
             y = keep.tile([P, PACK, width], F32, name="y_%d" % start)
+            entries = own_sb[:, start // 16 : (start + width) // 16]
+            near = []
             for pair in range(2):
-                first = 2 * pair % per_bank
+                slot = index + 1 - pair if pair == 0 or index == 0 else index
+                near.append(keep.tile([P, 2, width], F32, name="near", tag="near_%d" % slot, align_bytes=64))
+                for u in range(2):
+                    nc.vector.tensor_tensor(
+                        near[pair][:, u, :], c_rows[2 * pair + u][:].indirect(entries), dn_sb[:, cols], ALU.add
+                    )
+            for pair in range(2):
+                rest = banks[2 * pair // per_bank][:, 2 * pair % per_bank : 2 * pair % per_bank + 2, :]
+                y_pair = y[:, 2 * pair : 2 * pair + 2, :]
                 nc.vector.scalar_tensor_tensor(
-                    out=y[:, 2 * pair : 2 * pair + 2, :],
-                    in0=banks[2 * pair // per_bank][:, first : first + 2, :],
-                    scalar=-2.0,
-                    in1=near[pair][:],
-                    op0=ALU.mult,
-                    op1=ALU.add,
+                    out=y_pair, in0=rest, scalar=-2.0, in1=near[pair][:], op0=ALU.mult, op1=ALU.add
                 )
-            nc.sync.dma_start(out=out_rows[:, :, cols], in_=y[:])
+                nc.sync.dma_start(out=out_rows[:, 2 * pair : 2 * pair + 2, cols], in_=y_pair)
             y_bf = keep.tile([P, width, PACK], BF16, name="y_bf_%d" % start, align_bytes=64)
-            nc.scalar.copy(
-                out=y_bf[:].rearrange("p (c i) t -> p c t i", i=4),
-                in_=y[:].rearrange("p t (c i) -> p c t i", i=4),
-            )
+            if index < len(CHUNKS) - 1:
+                nc.scalar.copy(
+                    out=y_bf[:].rearrange("p (c i) t -> p c t i", i=4),
+                    in_=y[:].rearrange("p t (c i) -> p c t i", i=4),
+                )
+            else:
+                nc.vector.tensor_copy(out=y_bf[:], in_=y[:].rearrange("p t c -> p c t"))
             nc.vector.quantize_mx(
                 out=y_words[:, cols].bitcast(FP8X4),
                 scales=y_scales[:, cols],
                 in_=y_bf[:].rearrange("p c t -> p (c t)"),
             )
-            nc.sync.dma_start(out=out_words[:, cols], in_=y_words[:, cols])
+        last = CHUNKS[-1][0]
+        nc.sync.dma_start(out=out_words[:, :last], in_=y_words[:, :last])
+        nc.scalar.dma_start(out=out_words[:, last:], in_=y_words[:, last:])
         for q in range(4):
             engine = nc.scalar if q % 2 else nc.sync
             engine.dma_start(

@@ -1,6 +1,7 @@
 from contextlib import ExitStack
 
 import concourse.mybir as mybir
+from concourse.masks import make_identity
 
 K, T, S, V, N = 512, 2048, 512, 512, 512
 FLOPS = 2 * K * N * (V + S)
@@ -18,8 +19,7 @@ ACT = mybir.ActivationFunctionType
 P = 128
 PACK = 4
 HALF = N // 2
-BANK = 512
-CHUNKS = ((0, 256), (256, 128), (384, 128))
+NEAR = S - P
 
 
 def tile_picked_ivfpq_none_po_kernel(
@@ -33,150 +33,205 @@ def tile_picked_ivfpq_none_po_kernel(
         cent_sb = keep.tile([P, V // 16], U16, name="cent_sb")
         offs_sb = keep.tile([P, S // 16], U16, name="offs_sb")
         own_sb = keep.tile([P, S // 16], U16, name="own_sb")
-        xs = keep.tile([P, T], U8, name="xs", tag="xs_then_late", align_bytes=64)
+        xs = keep.tile([P, T], U8, name="xs", tag="xs_then_w1", align_bytes=64)
         xw = keep.tile([P, T], I32, name="xw", align_bytes=64)
         qn_sb = keep.tile([P, PACK], F32, name="qn_sb")
-        warm = keep.tile([P, 2], F32, name="warm")
+        dn_col = keep.tile([P, PACK], F32, name="dn_col")
+        dn_sb = keep.tile([P, S], F32, name="dn_sb")
+        ident = keep.tile([P, P], F32, name="ident")
         placed = keep.tile([P, V + S], U8, name="placed", align_bytes=64)
-
-        nc.gpsimd.memset(warm[:, 0:1], 0.0)
-        nc.scalar.activation(out=warm[:, 1:2], in_=warm[:, 0:1], func=ACT.Identity, bias=warm[:, 0:1], scale=-2.0)
-        nc.gpsimd.memset(placed[:].bitcast(I32), 0)
-
-        nc.sync.dma_start(
-            out=xs[:].bitcast(I32),
-            in_=x_scales[0].bitcast(I32).unsqueeze(1).broadcast_to([16, 8, T // 4]),
-        )
-        nc.sync.dma_start(cent_sb[:], cent)
-        nc.sync.dma_start(offs_sb[:], offs)
-        nc.sync.dma_start(out=xw[:], in_=x_words[0].rearrange("p n t -> p (n t)").bitcast(I32))
-        raw = {}
+        raw = {key: keep.tile([P, PACK, HALF], F32, name="raw_%s_%d" % key)[:] for key in (("w2", 0), ("w2", 1), ("w1", 0))}
 
         def load_half(name, w, h):
             nc.sync.dma_start(
                 out=raw[name, h], in_=w[:, h * HALF : (h + 1) * HALF].rearrange("(p j) c -> p j c", j=PACK)
             )
 
-        for h in range(2):
-            raw["w1", h] = keep.tile([P, PACK, HALF], F32, name="raw_w1", tag="stage_%d" % h)[:]
-            load_half("w1", w1, h)
-            if h == 0:
-                nc.sync.dma_start(out=qn_sb[:], in_=qn.rearrange("(p t) o -> p (t o)", t=PACK))
+        nc.sync.dma_start(
+            out=xs[:].bitcast(I32),
+            in_=x_scales[0].bitcast(I32).unsqueeze(1).broadcast_to([16, 8, T // 4]),
+        )
+        nc.scalar.dma_start(out=dn_col[:], in_=dn[0:1, :].rearrange("o (p u) -> p (o u)", u=PACK))
+        nc.sync.dma_start(offs_sb[:], offs)
+        nc.scalar.dma_start(out=qn_sb[:], in_=qn.rearrange("(p t) o -> p (t o)", t=PACK))
+        nc.sync.dma_start(cent_sb[:], cent)
+        nc.sync.dma_start(out=xw[:], in_=x_words[0].rearrange("p n t -> p (n t)").bitcast(I32))
+        load_half("w2", w2, 0)
+        load_half("w2", w2, 1)
+        load_half("w1", w1, 0)
         nc.sync.dma_start(own_sb[:], own)
 
+        make_identity(nc, ident[:])
+        nc.gpsimd.memset(placed[:].bitcast(I32), 0)
+
+        dn_ps = psum.tile([P, PACK, P], F32, name="dn_ps", tag="bank_7")
+        for u in range(PACK):
+            nc.tensor.transpose(dn_ps[:, u, :], dn_col[:, u : u + 1].to_broadcast([P, P]), ident[:])
+        nc.scalar.activation(
+            out=dn_sb[:].rearrange("m (p u) -> m p u", u=PACK),
+            in_=dn_ps[:].rearrange("m u p -> m p u"),
+            func=ACT.Identity,
+        )
+        dn_turned = psum.tile([P, P], F32, name="dn_turned", tag="bank_6")
+        nc.tensor.transpose(dn_turned[:], dn_sb[:, NEAR:], ident[:])
+        dn_last = keep.tile([P, 1], F32, name="dn_last")
+        nc.scalar.copy(out=dn_last[:], in_=dn_turned[:, 0:1])
+
         picked_bytes = keep.tile([P, V + S], U8, name="picked_bytes", align_bytes=64)
-        nc.vector.tensor_copy(picked_bytes[:, 0:V], xs[:].indirect(cent_sb[:]))
         nc.vector.tensor_copy(picked_bytes[:, V : V + S], xs[:].indirect(offs_sb[:]))
+        nc.vector.tensor_copy(picked_bytes[:, 0:V], xs[:].indirect(cent_sb[:]))
         for r in range(4):
-            nc.scalar.dma_start(
+            nc.sync.dma_start(
                 out=placed[r:P:32, :].bitcast(I32), in_=picked_bytes[8 * r : P : 32, :].bitcast(I32)
             )
-        late = keep.tile([P, PACK * HALF + S], F32, name="late", tag="xs_then_late", align_bytes=64)
-        raw["w2", 0] = late[:, : PACK * HALF].rearrange("p (j c) -> p j c", j=PACK)
-        dn_sb = late[:, PACK * HALF :]
-        load_half("w2", w2, 0)
-        nc.sync.dma_start(out=dn_sb, in_=dn)
+        raw["w1", 1] = keep.tile([P, PACK, HALF], F32, name="raw_w1_1", tag="xs_then_w1", align_bytes=64)[:]
+        load_half("w1", w1, 1)
 
         cent_words = keep.tile([P, V], U32, name="cent_words", align_bytes=64)
         vec_words = keep.tile([P, S], U32, name="vec_words", align_bytes=64)
-        nc.vector.tensor_copy(cent_words[:], xw[:].bitcast(U32).indirect(cent_sb[:]))
         nc.vector.tensor_copy(vec_words[:], xw[:].bitcast(U32).indirect(offs_sb[:]))
+        nc.vector.tensor_copy(cent_words[:], xw[:].bitcast(U32).indirect(cent_sb[:]))
 
         grouped, codes, scales = {}, {}, {}
-        for name in ("w1", "w2"):
-            grouped[name] = keep.tile([P, PACK, P, PACK], BF16, name="grouped", tag="near_0" if name == "w2" else "grouped_w1", align_bytes=64)
+        for name in ("w2", "w1"):
+            grouped[name] = keep.tile([P, PACK, P, PACK], BF16, name="grouped", tag="grouped_" + name, align_bytes=64)
             codes[name] = keep.tile([P, N], U32, name="codes_" + name, align_bytes=64)
             scales[name] = keep.tile([P, N], U8, name="scales_" + name, align_bytes=64)
 
-        def round_half(copy, name, h, m0=0, m1=HALF // PACK):
-            first = h * HALF // PACK
+        def round_part(copy, name, h, first, last):
+            rows = slice(h * P // 2, (h + 1) * P // 2)
             copy(
-                out=grouped[name][:, :, first + m0 : first + m1, :].rearrange("p t m j -> p m t j"),
-                in_=raw[name, h].rearrange("p j (m t) -> p m t j", t=PACK)[:, m0:m1, :, :],
+                out=grouped[name][:, first:last, rows, :].rearrange("p t m j -> p m j t"),
+                in_=raw[name, h].rearrange("p j (m t) -> p m j t", t=PACK)[:, :, :, first:last],
             )
 
-        def quantize_w(name, t0, t1):
-            nc.vector.quantize_mx(
-                out=codes[name][:, t0 * P : t1 * P].bitcast(FP8X4),
-                scales=scales[name][:, t0 * P : t1 * P],
-                in_=grouped[name][:, t0:t1, :, :].rearrange("p t m j -> p (t m j)"),
-            )
+        def round_weights(name, urgent_copy):
+            round_part(nc.scalar.copy, name, 0, 0, PACK)
+            round_part(urgent_copy, name, 1, 0, 2)
+            round_part(nc.scalar.copy, name, 1, 2, PACK)
+
+        def quantize_weights(name):
+            for first, last in ((0, 1), (1, 2), (2, PACK)):
+                nc.vector.quantize_mx(
+                    out=codes[name][:, first * P : last * P].bitcast(FP8X4),
+                    scales=scales[name][:, first * P : last * P],
+                    in_=grouped[name][:, first:last, :, :].rearrange("p t m j -> p (t m j)"),
+                )
 
         def product(acc, name, t, words, first, cols):
+            deal = slice(t * P, (t + 1) * P)
             nc.tensor.matmul_mx(
                 out=acc,
-                lhsT=codes[name][:, t * P : (t + 1) * P].bitcast(FP8X4),
-                lhsT_scale=scales[name][:, t * P : (t + 1) * P],
+                lhsT=codes[name][:, deal].bitcast(FP8X4),
+                lhsT_scale=scales[name][:, deal],
                 rhs=words[:, cols].bitcast(FP8X4),
                 rhs_scale=placed[:, first + cols.start : first + cols.stop],
                 start=True,
                 stop=True,
             )
 
-        round_half(nc.scalar.copy, "w1", 0)
-        raw["w2", 1] = keep.tile([P, PACK, HALF], F32, name="raw_w2", tag="stage_0")[:]
-        load_half("w2", w2, 1)
-        round_half(nc.vector.tensor_copy, "w1", 1)
-        for t in range(PACK):
-            quantize_w("w1", t, t + 1)
-        round_half(nc.vector.tensor_copy, "w2", 0)
-        round_half(nc.scalar.copy, "w2", 1)
+        halves = [slice(0, S // 2), slice(S // 2, S)]
+        stretches = [slice(0, S // 2), slice(S // 2, NEAR), slice(NEAR, S)]
+        rest = {}
+
+        def add_norms(t, tag):
+            rest[t] = keep.tile([P, NEAR], F32, name="rest", tag=tag, align_bytes=64)
+            groups = [stretches[0:1], stretches[1:2]] if t == 0 else [stretches[0:2]]
+            for index, group in enumerate(groups):
+                cols = slice(group[0].start, group[-1].stop)
+                acc = psum.tile([P, cols.stop - cols.start], F32, name="acc", tag="bank_%d" % (t + 4 * index))
+                for part in group:
+                    product(acc[:, part.start - cols.start : part.stop - cols.start], "w2", t, vec_words, V, part)
+                nc.vector.scalar_tensor_tensor(
+                    out=rest[t][:, cols], in0=acc[:], scalar=-2.0, in1=dn_sb[:, cols], op0=ALU.mult, op1=ALU.add
+                )
+
+        round_weights("w2", nc.vector.tensor_copy)
+        quantize_weights("w2")
+        add_norms(0, "rest_0")
+        round_weights("w1", nc.scalar.copy)
+        add_norms(1, "rest_1")
+        quantize_weights("w1")
+        add_norms(2, "xs_then_w1")
+        add_norms(3, "grouped_w1")
         c_rows = []
         for t in range(PACK):
-            c_ps = psum.tile([P, V], F32, name="c_ps%d" % t)
-            product(c_ps[:], "w1", t, cent_words, 0, slice(0, V))
-            c_t = keep.tile([P, V], F32, name="c_t", tag="stage_0" if t == 2 else "c_%d" % t)
-            nc.scalar.activation(out=c_t[:], in_=c_ps[:], func=ACT.Identity, bias=qn_sb[:, t : t + 1], scale=-2.0)
+            c_t = keep.tile([P, V], F32, name="c_%d" % t)
+            for index, cols in enumerate(halves if t == 0 else [slice(0, V)]):
+                acc = psum.tile([P, cols.stop - cols.start], F32, name="acc", tag="bank_%d" % (4 + t - 4 * index))
+                product(acc[:], "w1", t, cent_words, 0, cols)
+                nc.scalar.activation(
+                    out=c_t[:, cols], in_=acc[:], func=ACT.Identity, bias=qn_sb[:, t : t + 1], scale=-2.0
+                )
             c_rows.append(c_t)
-        quantize_w("w2", 0, PACK)
+            if t == 1:
+                turned_ps = psum.tile([P, N], F32, name="turned_ps", tag="bank_4")
+                nc.tensor.matmul_mx(
+                    out=turned_ps[:],
+                    lhsT=vec_words[:, NEAR:].bitcast(FP8X4),
+                    lhsT_scale=placed[:, V + NEAR :],
+                    rhs=codes["w2"][:].bitcast(FP8X4),
+                    rhs_scale=scales["w2"][:],
+                    start=True,
+                    stop=True,
+                )
+                turned = keep.tile([P, N], F32, name="turned")
+                nc.scalar.activation(out=turned[:], in_=turned_ps[:], func=ACT.Identity, bias=dn_last[:], scale=-2.0)
+        back = psum.tile([P, PACK, P], F32, name="back", tag="bank_1")
+        for t in range(PACK):
+            nc.tensor.transpose(back[:, t, :], turned[:, t * P : (t + 1) * P], ident[:])
+        rest_last = keep.tile([P, PACK, P], F32, name="rest_last")
+        nc.scalar.copy(out=rest_last[:], in_=back[:])
 
         y_words = keep.tile([P, S], I32, name="y_words", align_bytes=64)
         y_scales = keep.tile([P, S], U8, name="y_scales", align_bytes=64)
         out_rows = out_0.rearrange("(p t) j -> p t j", t=PACK)
         out_words = out_1[0].rearrange("p n t -> p (n t)").bitcast(I32)
+        y = [keep.tile([P, PACK, cols.stop - cols.start], F32, name="y_%d" % cols.start) for cols in stretches]
+        rounded = [
+            keep.tile([P, cols.stop - cols.start, PACK], BF16, name="rounded_%d" % cols.start, align_bytes=64)
+            for cols in stretches
+        ]
 
-        for index, (start, width) in enumerate(CHUNKS):
-            cols = slice(start, start + width)
-            per_bank = BANK // width
-            banks = []
-            for b in range(PACK // per_bank):
-                acc = psum.tile([P, per_bank, width], F32, name="rest_%d_%d" % (start, b))
-                for u in range(per_bank):
-                    product(acc[:, u, :], "w2", b * per_bank + u, vec_words, V, cols)
-                banks.append(acc)
-            y = keep.tile([P, PACK, width], F32, name="y_%d" % start)
-            entries = own_sb[:, start // 16 : (start + width) // 16]
-            near = []
-            for pair in range(2):
-                slot = index + 1 - pair if pair == 0 or index == 0 else index
-                near.append(keep.tile([P, 2, width], F32, name="near", tag="near_%d" % slot, align_bytes=64))
-                for u in range(2):
-                    nc.vector.tensor_tensor(
-                        near[pair][:, u, :], c_rows[2 * pair + u][:].indirect(entries), dn_sb[:, cols], ALU.add
-                    )
-            for pair in range(2):
-                rest = banks[2 * pair // per_bank][:, 2 * pair % per_bank : 2 * pair % per_bank + 2, :]
-                y_pair = y[:, 2 * pair : 2 * pair + 2, :]
-                nc.vector.scalar_tensor_tensor(
-                    out=y_pair, in0=rest, scalar=-2.0, in1=near[pair][:], op0=ALU.mult, op1=ALU.add
-                )
-                nc.sync.dma_start(out=out_rows[:, 2 * pair : 2 * pair + 2, cols], in_=y_pair)
-            y_bf = keep.tile([P, width, PACK], BF16, name="y_bf_%d" % start, align_bytes=64)
-            if index < len(CHUNKS) - 1:
-                nc.scalar.copy(
-                    out=y_bf[:].rearrange("p (c i) t -> p c t i", i=4),
-                    in_=y[:].rearrange("p t (c i) -> p c t i", i=4),
-                )
-            else:
-                nc.vector.tensor_copy(out=y_bf[:], in_=y[:].rearrange("p t c -> p c t"))
+        def look_up(t, index):
+            cols = stretches[index]
+            nc.vector.tensor_tensor(
+                y[index][:, t, :],
+                c_rows[t][:].indirect(own_sb[:, cols.start // 16 : cols.stop // 16]),
+                rest[t][:, cols] if cols.stop <= NEAR else rest_last[:, t, :],
+                ALU.add,
+            )
+
+        def store(index, first, last):
+            nc.sync.dma_start(out=out_rows[:, first:last, stretches[index]], in_=y[index][:, first:last, :])
+
+        def round_y(copy, index):
+            copy(
+                out=rounded[index][:].rearrange("p (c i) t -> p c t i", i=4),
+                in_=y[index][:].rearrange("p t (c i) -> p c t i", i=4),
+            )
+
+        for t in range(PACK):
+            for index in range(2):
+                look_up(t, index)
+            if t % 2:
+                store(0, t - 1, t + 1)
+        store(1, 0, PACK)
+        round_y(nc.scalar.copy, 0)
+        round_y(nc.scalar.copy, 1)
+        for t in range(PACK):
+            look_up(t, 2)
+            if t % 2:
+                store(2, t - 1, t + 1)
+        round_y(nc.vector.tensor_copy, 2)
+        for index, cols in enumerate(stretches):
             nc.vector.quantize_mx(
                 out=y_words[:, cols].bitcast(FP8X4),
                 scales=y_scales[:, cols],
-                in_=y_bf[:].rearrange("p c t -> p (c t)"),
+                in_=rounded[index][:].rearrange("p c t -> p (c t)"),
             )
-        last = CHUNKS[-1][0]
-        nc.sync.dma_start(out=out_words[:, :last], in_=y_words[:, :last])
-        nc.scalar.dma_start(out=out_words[:, last:], in_=y_words[:, last:])
+        nc.sync.dma_start(out=out_words[:, :NEAR], in_=y_words[:, :NEAR])
+        nc.scalar.dma_start(out=out_words[:, NEAR:], in_=y_words[:, NEAR:])
         for q in range(4):
             engine = nc.scalar if q % 2 else nc.sync
             engine.dma_start(

@@ -18,7 +18,6 @@ ACT = mybir.ActivationFunctionType
 
 P = 128
 PACK = 4
-HALF = N // 2
 NEAR = S - P
 
 
@@ -40,12 +39,10 @@ def tile_picked_ivfpq_none_po_kernel(
         dn_sb = keep.tile([P, S], F32, name="dn_sb")
         ident = keep.tile([P, P], F32, name="ident")
         placed = keep.tile([P, V + S], U8, name="placed", align_bytes=64)
-        raw = {key: keep.tile([P, PACK, HALF], F32, name="raw_%s_%d" % key)[:] for key in (("w2", 0), ("w2", 1), ("w1", 0))}
+        raw = {"w2": keep.tile([P, PACK, N], F32, name="raw_w2")}
 
-        def load_half(name, w, h):
-            nc.sync.dma_start(
-                out=raw[name, h], in_=w[:, h * HALF : (h + 1) * HALF].rearrange("(p j) c -> p j c", j=PACK)
-            )
+        def load_weights(name, w):
+            nc.sync.dma_start(out=raw[name][:], in_=w.rearrange("(p j) c -> p j c", j=PACK))
 
         nc.sync.dma_start(
             out=xs[:].bitcast(I32),
@@ -56,9 +53,7 @@ def tile_picked_ivfpq_none_po_kernel(
         nc.scalar.dma_start(out=qn_sb[:], in_=qn.rearrange("(p t) o -> p (t o)", t=PACK))
         nc.sync.dma_start(cent_sb[:], cent)
         nc.sync.dma_start(out=xw[:], in_=x_words[0].rearrange("p n t -> p (n t)").bitcast(I32))
-        load_half("w2", w2, 0)
-        load_half("w2", w2, 1)
-        load_half("w1", w1, 0)
+        load_weights("w2", w2)
         nc.sync.dma_start(own_sb[:], own)
 
         make_identity(nc, ident[:])
@@ -84,8 +79,8 @@ def tile_picked_ivfpq_none_po_kernel(
             nc.sync.dma_start(
                 out=placed[r:P:32, :].bitcast(I32), in_=picked_bytes[8 * r : P : 32, :].bitcast(I32)
             )
-        raw["w1", 1] = keep.tile([P, PACK, HALF], F32, name="raw_w1_1", tag="xs_then_w1", align_bytes=64)[:]
-        load_half("w1", w1, 1)
+        raw["w1"] = keep.tile([P, PACK, N], F32, name="raw_w1", tag="xs_then_w1", align_bytes=64)
+        load_weights("w1", w1)
 
         cent_words = keep.tile([P, V], U32, name="cent_words", align_bytes=64)
         vec_words = keep.tile([P, S], U32, name="vec_words", align_bytes=64)
@@ -98,17 +93,12 @@ def tile_picked_ivfpq_none_po_kernel(
             codes[name] = keep.tile([P, N], U32, name="codes_" + name, align_bytes=64)
             scales[name] = keep.tile([P, N], U8, name="scales_" + name, align_bytes=64)
 
-        def round_part(copy, name, h, first, last):
-            rows = slice(h * P // 2, (h + 1) * P // 2)
-            copy(
-                out=grouped[name][:, first:last, rows, :].rearrange("p t m j -> p m j t"),
-                in_=raw[name, h].rearrange("p j (m t) -> p m j t", t=PACK)[:, :, :, first:last],
-            )
-
-        def round_weights(name, urgent_copy):
-            round_part(nc.scalar.copy, name, 0, 0, PACK)
-            round_part(urgent_copy, name, 1, 0, 2)
-            round_part(nc.scalar.copy, name, 1, 2, PACK)
+        def round_weights(name):
+            for copy, first in ((nc.vector.tensor_copy, 0), (nc.scalar.copy, 2)):
+                copy(
+                    out=grouped[name][:, first : first + 2, :, :].rearrange("p t m j -> p m j t"),
+                    in_=raw[name][:].rearrange("p j (m t) -> p m j t", t=PACK)[:, :, :, first : first + 2],
+                )
 
         def quantize_weights(name):
             for first, last in ((0, 1), (1, 2), (2, PACK)):
@@ -146,11 +136,11 @@ def tile_picked_ivfpq_none_po_kernel(
                     out=rest[t][:, cols], in0=acc[:], scalar=-2.0, in1=dn_sb[:, cols], op0=ALU.mult, op1=ALU.add
                 )
 
-        round_weights("w2", nc.vector.tensor_copy)
+        round_weights("w2")
         quantize_weights("w2")
         add_norms(0, "rest_0")
-        round_weights("w1", nc.scalar.copy)
         add_norms(1, "rest_1")
+        round_weights("w1")
         quantize_weights("w1")
         add_norms(2, "xs_then_w1")
         add_norms(3, "grouped_w1")

@@ -35,14 +35,16 @@ def tile_picked_ivfpq_none_po_kernel(
         xs = keep.tile([P, T], U8, name="xs", tag="xs_then_w1", align_bytes=64)
         xw = keep.tile([P, T], I32, name="xw", align_bytes=64)
         qn_sb = keep.tile([P, PACK], F32, name="qn_sb")
-        dn_col = keep.tile([P, PACK], F32, name="dn_col")
-        dn_sb = keep.tile([P, S], F32, name="dn_sb")
+        dn_col = keep.tile([P, PACK], F32, name="dn_col", tag="grouped_w2_1", align_bytes=64)
+        dn_sb = keep.tile([P, NEAR], F32, name="dn_sb")
+        dn_last = keep.tile([P, 1], F32, name="dn_last")
         ident = keep.tile([P, P], F32, name="ident")
         placed = keep.tile([P, V + S], U8, name="placed", align_bytes=64)
-        raw = {"w2": keep.tile([P, PACK, N], F32, name="raw_w2")}
+        raw_w2 = keep.tile([P, PACK, N], F32, name="raw_w2")
+        raw_w1 = [keep.tile([P, PACK, N // 2], F32, name="raw_w1_0")]
 
-        def load_weights(name, w):
-            nc.sync.dma_start(out=raw[name][:], in_=w.rearrange("(p j) c -> p j c", j=PACK))
+        def load_weights(raw, columns):
+            nc.sync.dma_start(out=raw[:], in_=columns.rearrange("(p j) c -> p j c", j=PACK))
 
         nc.sync.dma_start(
             out=xs[:].bitcast(I32),
@@ -52,25 +54,25 @@ def tile_picked_ivfpq_none_po_kernel(
         nc.sync.dma_start(offs_sb[:], offs)
         nc.scalar.dma_start(out=qn_sb[:], in_=qn.rearrange("(p t) o -> p (t o)", t=PACK))
         nc.sync.dma_start(cent_sb[:], cent)
+        nc.scalar.dma_start(out=dn_last[:], in_=dn[0:1, NEAR:].rearrange("o p -> p o"))
         nc.sync.dma_start(out=xw[:], in_=x_words[0].rearrange("p n t -> p (n t)").bitcast(I32))
-        load_weights("w2", w2)
+        load_weights(raw_w2, w2)
+        load_weights(raw_w1[0], w1[:, : N // 2])
         nc.sync.dma_start(own_sb[:], own)
 
         make_identity(nc, ident[:])
         nc.gpsimd.memset(placed[:].bitcast(I32), 0)
 
-        dn_ps = psum.tile([P, PACK, P], F32, name="dn_ps", tag="bank_7")
-        for u in range(PACK):
-            nc.tensor.transpose(dn_ps[:, u, :], dn_col[:, u : u + 1].to_broadcast([P, P]), ident[:])
-        nc.scalar.activation(
-            out=dn_sb[:].rearrange("m (p u) -> m p u", u=PACK),
-            in_=dn_ps[:].rearrange("m u p -> m p u"),
-            func=ACT.Identity,
-        )
-        dn_turned = psum.tile([P, P], F32, name="dn_turned", tag="bank_6")
-        nc.tensor.transpose(dn_turned[:], dn_sb[:, NEAR:], ident[:])
-        dn_last = keep.tile([P, 1], F32, name="dn_last")
-        nc.scalar.copy(out=dn_last[:], in_=dn_turned[:, 0:1])
+        for pair in range(2):
+            dn_ps = psum.tile([P, 2, P], F32, name="dn_ps", tag="bank_%d" % (6 + pair))
+            for u in range(2):
+                column = dn_col[:, 2 * pair + u : 2 * pair + u + 1]
+                nc.tensor.transpose(dn_ps[:, u, :], column.to_broadcast([P, P]), ident[:])
+            nc.scalar.activation(
+                out=dn_sb[:].rearrange("m (p u) -> m p u", u=PACK)[:, :, 2 * pair : 2 * pair + 2],
+                in_=dn_ps[:, :, : NEAR // PACK].rearrange("m u p -> m p u"),
+                func=ACT.Identity,
+            )
 
         picked_bytes = keep.tile([P, V + S], U8, name="picked_bytes", align_bytes=64)
         nc.vector.tensor_copy(picked_bytes[:, V : V + S], xs[:].indirect(offs_sb[:]))
@@ -79,8 +81,8 @@ def tile_picked_ivfpq_none_po_kernel(
             nc.sync.dma_start(
                 out=placed[r:P:32, :].bitcast(I32), in_=picked_bytes[8 * r : P : 32, :].bitcast(I32)
             )
-        raw["w1"] = keep.tile([P, PACK, N], F32, name="raw_w1", tag="xs_then_w1", align_bytes=64)
-        load_weights("w1", w1)
+        raw_w1.append(keep.tile([P, PACK, N // 2], F32, name="raw_w1_1", tag="xs_then_w1", align_bytes=64))
+        load_weights(raw_w1[1], w1[:, N // 2 :])
 
         cent_words = keep.tile([P, V], U32, name="cent_words", align_bytes=64)
         vec_words = keep.tile([P, S], U32, name="vec_words", align_bytes=64)
@@ -89,23 +91,24 @@ def tile_picked_ivfpq_none_po_kernel(
 
         grouped, codes, scales = {}, {}, {}
         for name in ("w2", "w1"):
-            grouped[name] = keep.tile([P, PACK, P, PACK], BF16, name="grouped", tag="grouped_" + name, align_bytes=64)
+            for pair in range(2):
+                tag = "grouped_%s_%d" % (name, pair)
+                grouped[name, pair] = keep.tile([P, 2, P, PACK], BF16, name="grouped", tag=tag, align_bytes=64)
             codes[name] = keep.tile([P, N], U32, name="codes_" + name, align_bytes=64)
             scales[name] = keep.tile([P, N], U8, name="scales_" + name, align_bytes=64)
 
-        def round_weights(name):
-            for copy, first in ((nc.vector.tensor_copy, 0), (nc.scalar.copy, 2)):
-                copy(
-                    out=grouped[name][:, first : first + 2, :, :].rearrange("p t m j -> p m j t"),
-                    in_=raw[name][:].rearrange("p j (m t) -> p m j t", t=PACK)[:, :, :, first : first + 2],
-                )
+        def round_weights(copy, name, raw, rows, pair):
+            copy(
+                out=grouped[name, pair][:, :, rows, :].rearrange("p t m j -> p m j t"),
+                in_=raw[:].rearrange("p j (m t) -> p m j t", t=PACK)[:, :, :, 2 * pair : 2 * pair + 2],
+            )
 
         def quantize_weights(name):
             for first, last in ((0, 1), (1, 2), (2, PACK)):
                 nc.vector.quantize_mx(
                     out=codes[name][:, first * P : last * P].bitcast(FP8X4),
                     scales=scales[name][:, first * P : last * P],
-                    in_=grouped[name][:, first:last, :, :].rearrange("p t m j -> p (t m j)"),
+                    in_=grouped[name, first // 2][:, first % 2 : (last - 1) % 2 + 1, :, :].rearrange("p t m j -> p (t m j)"),
                 )
 
         def product(acc, name, t, words, first, cols):
@@ -136,14 +139,18 @@ def tile_picked_ivfpq_none_po_kernel(
                     out=rest[t][:, cols], in0=acc[:], scalar=-2.0, in1=dn_sb[:, cols], op0=ALU.mult, op1=ALU.add
                 )
 
-        round_weights("w2")
+        round_weights(nc.vector.tensor_copy, "w2", raw_w2, slice(0, P), 0)
+        round_weights(nc.scalar.copy, "w2", raw_w2, slice(0, P), 1)
         quantize_weights("w2")
         add_norms(0, "rest_0")
         add_norms(1, "rest_1")
-        round_weights("w1")
+        round_weights(nc.scalar.copy, "w1", raw_w1[0], slice(0, P // 2), 0)
+        round_weights(nc.scalar.copy, "w1", raw_w1[0], slice(0, P // 2), 1)
+        round_weights(nc.vector.tensor_copy, "w1", raw_w1[1], slice(P // 2, P), 0)
+        round_weights(nc.scalar.copy, "w1", raw_w1[1], slice(P // 2, P), 1)
         quantize_weights("w1")
         add_norms(2, "xs_then_w1")
-        add_norms(3, "grouped_w1")
+        add_norms(3, "grouped_w1_0")
         c_rows = []
         for t in range(PACK):
             c_t = keep.tile([P, V], F32, name="c_%d" % t)
@@ -177,7 +184,9 @@ def tile_picked_ivfpq_none_po_kernel(
         y_scales = keep.tile([P, S], U8, name="y_scales", align_bytes=64)
         out_rows = out_0.rearrange("(p t) j -> p t j", t=PACK)
         out_words = out_1[0].rearrange("p n t -> p (n t)").bitcast(I32)
-        y = [keep.tile([P, PACK, cols.stop - cols.start], F32, name="y_%d" % cols.start) for cols in stretches]
+        y_near = keep.tile([P, PACK, NEAR], F32, name="y_near")
+        y_last = keep.tile([P, PACK, P], F32, name="y_last")
+        y = [y_near[:, :, stretches[0]], y_near[:, :, stretches[1]], y_last[:]]
         rounded = [
             keep.tile([P, cols.stop - cols.start, PACK], BF16, name="rounded_%d" % cols.start, align_bytes=64)
             for cols in stretches
@@ -192,27 +201,26 @@ def tile_picked_ivfpq_none_po_kernel(
                 ALU.add,
             )
 
-        def store(index, first, last):
-            nc.sync.dma_start(out=out_rows[:, first:last, stretches[index]], in_=y[index][:, first:last, :])
+        def store(values, cols, first, last):
+            nc.sync.dma_start(out=out_rows[:, first:last, cols], in_=values[:, first:last, :])
 
         def round_y(copy, index):
             copy(
                 out=rounded[index][:].rearrange("p (c i) t -> p c t i", i=4),
-                in_=y[index][:].rearrange("p t (c i) -> p c t i", i=4),
+                in_=y[index].rearrange("p t (c i) -> p c t i", i=4),
             )
 
         for t in range(PACK):
             for index in range(2):
                 look_up(t, index)
-            if t % 2:
-                store(0, t - 1, t + 1)
-        store(1, 0, PACK)
+            if t > 0:
+                store(y_near, slice(0, NEAR), 0 if t == 1 else t, t + 1)
         round_y(nc.scalar.copy, 0)
         round_y(nc.scalar.copy, 1)
         for t in range(PACK):
             look_up(t, 2)
             if t % 2:
-                store(2, t - 1, t + 1)
+                store(y_last, stretches[2], t - 1, t + 1)
         round_y(nc.vector.tensor_copy, 2)
         for index, cols in enumerate(stretches):
             nc.vector.quantize_mx(
@@ -220,8 +228,8 @@ def tile_picked_ivfpq_none_po_kernel(
                 scales=y_scales[:, cols],
                 in_=rounded[index][:].rearrange("p c t -> p (c t)"),
             )
-        nc.sync.dma_start(out=out_words[:, :NEAR], in_=y_words[:, :NEAR])
-        nc.scalar.dma_start(out=out_words[:, NEAR:], in_=y_words[:, NEAR:])
+        nc.sync.dma_start(out=out_words[:, halves[0]], in_=y_words[:, halves[0]])
+        nc.scalar.dma_start(out=out_words[:, halves[1]], in_=y_words[:, halves[1]])
         for q in range(4):
             engine = nc.scalar if q % 2 else nc.sync
             engine.dma_start(

@@ -52,9 +52,7 @@ def tile_picked_ivfpq_none_po_kernel(
         )
         nc.scalar.dma_start(out=dn_col[:], in_=dn[0:1, :].rearrange("o (p u) -> p (o u)", u=PACK))
         nc.sync.dma_start(offs_sb[:], offs)
-        nc.scalar.dma_start(out=qn_sb[:], in_=qn.rearrange("(p t) o -> p (t o)", t=PACK))
         nc.sync.dma_start(cent_sb[:], cent)
-        nc.scalar.dma_start(out=dn_last[:], in_=dn[0:1, NEAR:].rearrange("o p -> p o"))
         nc.sync.dma_start(out=xw[:], in_=x_words[0].rearrange("p n t -> p (n t)").bitcast(I32))
         load_weights(raw_w2, w2)
         load_weights(raw_w1[0], w1[:, : N // 2])
@@ -62,6 +60,8 @@ def tile_picked_ivfpq_none_po_kernel(
 
         make_identity(nc, ident[:])
         nc.gpsimd.memset(placed[:].bitcast(I32), 0)
+        nc.gpsimd.dma_start(out=qn_sb[:], in_=qn.rearrange("(p t) o -> p (t o)", t=PACK))
+        nc.gpsimd.dma_start(out=dn_last[:], in_=dn[0:1, NEAR:].rearrange("o p -> p o"))
 
         for pair in range(2):
             dn_ps = psum.tile([P, 2, P], F32, name="dn_ps", tag="bank_%d" % (6 + pair))
@@ -192,10 +192,9 @@ def tile_picked_ivfpq_none_po_kernel(
             for cols in stretches
         ]
 
-        def look_up(t, index):
-            cols = stretches[index]
+        def look_up(t, cols):
             nc.vector.tensor_tensor(
-                y[index][:, t, :],
+                y_near[:, t, cols] if cols.stop <= NEAR else y_last[:, t, :],
                 c_rows[t][:].indirect(own_sb[:, cols.start // 16 : cols.stop // 16]),
                 rest[t][:, cols] if cols.stop <= NEAR else rest_last[:, t, :],
                 ALU.add,
@@ -211,14 +210,14 @@ def tile_picked_ivfpq_none_po_kernel(
             )
 
         for t in range(PACK):
-            for index in range(2):
-                look_up(t, index)
+            for cols in [slice(0, NEAR)] if t < PACK - 1 else stretches[:2]:
+                look_up(t, cols)
             if t > 0:
                 store(y_near, slice(0, NEAR), 0 if t == 1 else t, t + 1)
         round_y(nc.scalar.copy, 0)
         round_y(nc.scalar.copy, 1)
         for t in range(PACK):
-            look_up(t, 2)
+            look_up(t, stretches[2])
             if t % 2:
                 store(y_last, stretches[2], t - 1, t + 1)
         round_y(nc.vector.tensor_copy, 2)

@@ -32,36 +32,103 @@ def tile_picked_ivfpq_none_po_kernel(
         cent_sb = keep.tile([P, V // 16], U16, name="cent_sb")
         offs_sb = keep.tile([P, S // 16], U16, name="offs_sb")
         own_sb = keep.tile([P, S // 16], U16, name="own_sb")
-        xs = keep.tile([P, T], U8, name="xs", tag="xs_then_w1", align_bytes=64)
+        xs = keep.tile([P, T], U8, name="xs", align_bytes=64)
         xw = keep.tile([P, T], I32, name="xw", align_bytes=64)
         qn_sb = keep.tile([P, PACK], F32, name="qn_sb")
-        dn_col = keep.tile([P, PACK], F32, name="dn_col", tag="grouped_w2_1", align_bytes=64)
+        dn_col = keep.tile([P, PACK], F32, name="dn_col")
         dn_sb = keep.tile([P, NEAR], F32, name="dn_sb")
         dn_last = keep.tile([P, 1], F32, name="dn_last")
         ident = keep.tile([P, P], F32, name="ident")
-        placed = keep.tile([P, V + S], U8, name="placed", align_bytes=64)
-        raw_w2 = keep.tile([P, PACK, N], F32, name="raw_w2")
+        placed = {"w2": keep.tile([P, S], U8, name="placed_w2", align_bytes=64)}
+        raw_w2 = [
+            keep.tile([P, PACK, N // 2], F32, name="raw_w2", tag="stage_%d" % h, align_bytes=64) for h in range(2)
+        ]
         raw_w1 = [keep.tile([P, PACK, N // 2], F32, name="raw_w1_0")]
 
         def load_weights(raw, columns):
             nc.sync.dma_start(out=raw[:], in_=columns.rearrange("(p j) c -> p j c", j=PACK))
 
-        nc.sync.dma_start(
-            out=xs[:].bitcast(I32),
-            in_=x_scales[0].bitcast(I32).unsqueeze(1).broadcast_to([16, 8, T // 4]),
-        )
-        nc.scalar.dma_start(out=dn_col[:], in_=dn[0:1, :].rearrange("o (p u) -> p (o u)", u=PACK))
+        nc.vector.memset(xs[:].bitcast(I32), 0)
+        load_weights(raw_w2[0], w2[:, : N // 2])
         nc.sync.dma_start(offs_sb[:], offs)
         nc.sync.dma_start(cent_sb[:], cent)
-        nc.sync.dma_start(out=xw[:], in_=x_words[0].rearrange("p n t -> p (n t)").bitcast(I32))
-        load_weights(raw_w2, w2)
-        load_weights(raw_w1[0], w1[:, : N // 2])
         nc.sync.dma_start(own_sb[:], own)
+        nc.sync.dma_start(out=xs[0:P:8, :].bitcast(I32), in_=x_scales[0].bitcast(I32))
+        nc.scalar.dma_start(out=dn_col[:], in_=dn[0:1, :].rearrange("o (p u) -> p (o u)", u=PACK))
+        load_weights(raw_w2[1], w2[:, N // 2 :])
+        nc.sync.dma_start(out=xw[:], in_=x_words[0].rearrange("p n t -> p (n t)").bitcast(I32))
+        load_weights(raw_w1[0], w1[:, : N // 2])
 
         make_identity(nc, ident[:])
-        nc.gpsimd.memset(placed[:].bitcast(I32), 0)
+        nc.gpsimd.memset(placed["w2"][:].bitcast(I32), 0)
         nc.gpsimd.dma_start(out=qn_sb[:], in_=qn.rearrange("(p t) o -> p (t o)", t=PACK))
         nc.gpsimd.dma_start(out=dn_last[:], in_=dn[0:1, NEAR:].rearrange("o p -> p o"))
+
+        picked = {name: keep.tile([P, S], U8, name="picked_" + name, align_bytes=64) for name in ("w2", "w1")}
+        nc.vector.tensor_copy(picked["w2"][:], xs[:].indirect(offs_sb[:]))
+        nc.vector.tensor_copy(picked["w1"][:], xs[:].indirect(cent_sb[:]))
+
+        def place(name):
+            for r in range(4):
+                nc.sync.dma_start(
+                    out=placed[name][r:P:32, :].bitcast(I32), in_=picked[name][8 * r : P : 32, :].bitcast(I32)
+                )
+
+        place("w2")
+
+        grouped, codes, scales = {}, {}, {}
+        for name in ("w2", "w1"):
+            grouped[name] = keep.tile([P, PACK, P, PACK], BF16, name="grouped", tag="grouped_" + name, align_bytes=64)
+            codes[name] = keep.tile([P, N], U32, name="codes_" + name, align_bytes=64)
+            scales[name] = keep.tile([P, N], U8, name="scales_" + name, align_bytes=64)
+
+        def round_weights(name, raw):
+            for half, deals in ((0, slice(0, PACK)), (1, slice(0, 2)), (1, slice(2, PACK))):
+                rows = slice(half * P // 2, (half + 1) * P // 2)
+                nc.scalar.copy(
+                    out=grouped[name][:, deals, rows, :].rearrange("p t m j -> p m j t"),
+                    in_=raw[half][:].rearrange("p j (m t) -> p m j t", t=PACK)[:, :, :, deals],
+                )
+
+        def quantize_weights(name):
+            for first, last in ((0, 1), (1, 2), (2, PACK)):
+                nc.vector.quantize_mx(
+                    out=codes[name][:, first * P : last * P].bitcast(FP8X4),
+                    scales=scales[name][:, first * P : last * P],
+                    in_=grouped[name][:, first:last, :, :].rearrange("p t m j -> p (t m j)"),
+                )
+
+        def product(acc, name, t, words, cols):
+            deal = slice(t * P, (t + 1) * P)
+            nc.tensor.matmul_mx(
+                out=acc,
+                lhsT=codes[name][:, deal].bitcast(FP8X4),
+                lhsT_scale=scales[name][:, deal],
+                rhs=words[:, cols].bitcast(FP8X4),
+                rhs_scale=placed[name][:, cols],
+                start=True,
+                stop=True,
+            )
+
+        halves = [slice(0, S // 2), slice(S // 2, S)]
+        stretches = [slice(0, S // 2), slice(S // 2, NEAR), slice(NEAR, S)]
+        rest = {}
+
+        def add_norms(t):
+            acc = psum.tile([P, NEAR], F32, name="acc", tag="bank_%d" % t)
+            for part in stretches[:2]:
+                product(acc[:, part], "w2", t, vec_words, part)
+            nc.vector.scalar_tensor_tensor(
+                out=rest[t], in0=acc[:], scalar=-2.0, in1=dn_sb[:], op0=ALU.mult, op1=ALU.add
+            )
+
+        round_weights("w2", raw_w2)
+        quantize_weights("w2")
+        raw_w1.append(keep.tile([P, PACK, N // 2], F32, name="raw_w1_1", tag="stage_0", align_bytes=64))
+        load_weights(raw_w1[1], w1[:, N // 2 :])
+        placed["w1"] = keep.tile([P, V], U8, name="placed_w1", tag="stage_1", align_bytes=64)
+        nc.gpsimd.memset(placed["w1"][:].bitcast(I32), 0)
+        place("w1")
 
         for pair in range(2):
             dn_ps = psum.tile([P, 2, P], F32, name="dn_ps", tag="bank_%d" % (6 + pair))
@@ -74,89 +141,28 @@ def tile_picked_ivfpq_none_po_kernel(
                 func=ACT.Identity,
             )
 
-        picked_bytes = keep.tile([P, V + S], U8, name="picked_bytes", align_bytes=64)
-        nc.vector.tensor_copy(picked_bytes[:, V : V + S], xs[:].indirect(offs_sb[:]))
-        nc.vector.tensor_copy(picked_bytes[:, 0:V], xs[:].indirect(cent_sb[:]))
-        for r in range(4):
-            nc.sync.dma_start(
-                out=placed[r:P:32, :].bitcast(I32), in_=picked_bytes[8 * r : P : 32, :].bitcast(I32)
-            )
-        raw_w1.append(keep.tile([P, PACK, N // 2], F32, name="raw_w1_1", tag="xs_then_w1", align_bytes=64))
-        load_weights(raw_w1[1], w1[:, N // 2 :])
+        picked_words = keep.tile([P, S + V], U32, name="picked_words", tag="grouped_w2", align_bytes=64)
+        vec_words, cent_words = picked_words[:, :S], picked_words[:, S:]
+        nc.vector.tensor_copy(vec_words, xw[:].bitcast(U32).indirect(offs_sb[:]))
+        nc.vector.tensor_copy(cent_words, xw[:].bitcast(U32).indirect(cent_sb[:]))
 
-        cent_words = keep.tile([P, V], U32, name="cent_words", align_bytes=64)
-        vec_words = keep.tile([P, S], U32, name="vec_words", align_bytes=64)
-        nc.vector.tensor_copy(vec_words[:], xw[:].bitcast(U32).indirect(offs_sb[:]))
-        nc.vector.tensor_copy(cent_words[:], xw[:].bitcast(U32).indirect(cent_sb[:]))
-
-        grouped, codes, scales = {}, {}, {}
-        for name in ("w2", "w1"):
-            for pair in range(2):
-                tag = "grouped_%s_%d" % (name, pair)
-                grouped[name, pair] = keep.tile([P, 2, P, PACK], BF16, name="grouped", tag=tag, align_bytes=64)
-            codes[name] = keep.tile([P, N], U32, name="codes_" + name, align_bytes=64)
-            scales[name] = keep.tile([P, N], U8, name="scales_" + name, align_bytes=64)
-
-        def round_weights(copy, name, raw, rows, pair):
-            copy(
-                out=grouped[name, pair][:, :, rows, :].rearrange("p t m j -> p m j t"),
-                in_=raw[:].rearrange("p j (m t) -> p m j t", t=PACK)[:, :, :, 2 * pair : 2 * pair + 2],
-            )
-
-        def quantize_weights(name):
-            for first, last in ((0, 1), (1, 2), (2, PACK)):
-                nc.vector.quantize_mx(
-                    out=codes[name][:, first * P : last * P].bitcast(FP8X4),
-                    scales=scales[name][:, first * P : last * P],
-                    in_=grouped[name, first // 2][:, first % 2 : (last - 1) % 2 + 1, :, :].rearrange("p t m j -> p (t m j)"),
-                )
-
-        def product(acc, name, t, words, first, cols):
-            deal = slice(t * P, (t + 1) * P)
-            nc.tensor.matmul_mx(
-                out=acc,
-                lhsT=codes[name][:, deal].bitcast(FP8X4),
-                lhsT_scale=scales[name][:, deal],
-                rhs=words[:, cols].bitcast(FP8X4),
-                rhs_scale=placed[:, first + cols.start : first + cols.stop],
-                start=True,
-                stop=True,
-            )
-
-        halves = [slice(0, S // 2), slice(S // 2, S)]
-        stretches = [slice(0, S // 2), slice(S // 2, NEAR), slice(NEAR, S)]
-        rest = {}
-
-        def add_norms(t, tag):
-            rest[t] = keep.tile([P, NEAR], F32, name="rest", tag=tag, align_bytes=64)
-            groups = [stretches[0:1], stretches[1:2]] if t == 0 else [stretches[0:2]]
-            for index, group in enumerate(groups):
-                cols = slice(group[0].start, group[-1].stop)
-                acc = psum.tile([P, cols.stop - cols.start], F32, name="acc", tag="bank_%d" % (t + 4 * index))
-                for part in group:
-                    product(acc[:, part.start - cols.start : part.stop - cols.start], "w2", t, vec_words, V, part)
-                nc.vector.scalar_tensor_tensor(
-                    out=rest[t][:, cols], in0=acc[:], scalar=-2.0, in1=dn_sb[:, cols], op0=ALU.mult, op1=ALU.add
-                )
-
-        round_weights(nc.vector.tensor_copy, "w2", raw_w2, slice(0, P), 0)
-        round_weights(nc.scalar.copy, "w2", raw_w2, slice(0, P), 1)
-        quantize_weights("w2")
-        add_norms(0, "rest_0")
-        add_norms(1, "rest_1")
-        round_weights(nc.scalar.copy, "w1", raw_w1[0], slice(0, P // 2), 0)
-        round_weights(nc.scalar.copy, "w1", raw_w1[0], slice(0, P // 2), 1)
-        round_weights(nc.vector.tensor_copy, "w1", raw_w1[1], slice(P // 2, P), 0)
-        round_weights(nc.scalar.copy, "w1", raw_w1[1], slice(P // 2, P), 1)
+        early = keep.tile([P, 2, NEAR], F32, name="early")
+        rest[0], rest[1] = early[:, 0, :], early[:, 1, :]
+        add_norms(0)
+        add_norms(1)
+        round_weights("w1", raw_w1)
         quantize_weights("w1")
-        add_norms(2, "xs_then_w1")
-        add_norms(3, "grouped_w1_0")
+        late = keep.tile([P, 2, NEAR], F32, name="late", tag="stage_0", align_bytes=64)
+        rest[2], rest[3] = late[:, 0, :], late[:, 1, :]
+        turned = keep.tile([P, N], F32, name="turned")
+        add_norms(2)
+        add_norms(3)
         c_rows = []
         for t in range(PACK):
             c_t = keep.tile([P, V], F32, name="c_%d" % t)
             for index, cols in enumerate(halves if t == 0 else [slice(0, V)]):
                 acc = psum.tile([P, cols.stop - cols.start], F32, name="acc", tag="bank_%d" % (4 + t - 4 * index))
-                product(acc[:], "w1", t, cent_words, 0, cols)
+                product(acc[:], "w1", t, cent_words, cols)
                 nc.scalar.activation(
                     out=c_t[:, cols], in_=acc[:], func=ACT.Identity, bias=qn_sb[:, t : t + 1], scale=-2.0
                 )
@@ -166,13 +172,12 @@ def tile_picked_ivfpq_none_po_kernel(
                 nc.tensor.matmul_mx(
                     out=turned_ps[:],
                     lhsT=vec_words[:, NEAR:].bitcast(FP8X4),
-                    lhsT_scale=placed[:, V + NEAR :],
+                    lhsT_scale=placed["w2"][:, NEAR:],
                     rhs=codes["w2"][:].bitcast(FP8X4),
                     rhs_scale=scales["w2"][:],
                     start=True,
                     stop=True,
                 )
-                turned = keep.tile([P, N], F32, name="turned")
                 nc.scalar.activation(out=turned[:], in_=turned_ps[:], func=ACT.Identity, bias=dn_last[:], scale=-2.0)
         back = psum.tile([P, PACK, P], F32, name="back", tag="bank_1")
         for t in range(PACK):

@@ -27,6 +27,7 @@ def tile_picked_ivfpq_none_po_kernel(
     nc = tc.nc
     with ExitStack() as ctx:
         keep = ctx.enter_context(tc.tile_pool(name="keep", bufs=1))
+        shared = ctx.enter_context(tc.tile_pool(name="shared", bufs=1))
         psum = ctx.enter_context(tc.psum_pool(name="psum", bufs=1))
 
         cent_sb = keep.tile([P, V // 16], U16, name="cent_sb")
@@ -34,10 +35,8 @@ def tile_picked_ivfpq_none_po_kernel(
         own_sb = keep.tile([P, S // 16], U16, name="own_sb")
         xs = keep.tile([P, T], U8, name="xs", align_bytes=64)
         xw = keep.tile([P, T], I32, name="xw", align_bytes=64)
-        qn_sb = keep.tile([P, PACK], F32, name="qn_sb")
         dn_col = keep.tile([P, PACK], F32, name="dn_col")
         dn_sb = keep.tile([P, NEAR], F32, name="dn_sb")
-        dn_last = keep.tile([P, 1], F32, name="dn_last")
         ident = keep.tile([P, P], F32, name="ident")
         placed = {"w2": keep.tile([P, S], U8, name="placed_w2", align_bytes=64)}
         raw_w2 = [
@@ -61,10 +60,11 @@ def tile_picked_ivfpq_none_po_kernel(
 
         make_identity(nc, ident[:])
         nc.gpsimd.memset(placed["w2"][:].bitcast(I32), 0)
-        nc.gpsimd.dma_start(out=qn_sb[:], in_=qn.rearrange("(p t) o -> p (t o)", t=PACK))
-        nc.gpsimd.dma_start(out=dn_last[:], in_=dn[0:1, NEAR:].rearrange("o p -> p o"))
 
-        picked = {name: keep.tile([P, S], U8, name="picked_" + name, align_bytes=64) for name in ("w2", "w1")}
+        picked = {
+            "w2": shared.tile([P, S], U8, name="picked_w2", offset=0, align_bytes=64),
+            "w1": keep.tile([P, V], U8, name="picked_w1", align_bytes=64),
+        }
         nc.vector.tensor_copy(picked["w2"][:], xs[:].indirect(offs_sb[:]))
         nc.vector.tensor_copy(picked["w1"][:], xs[:].indirect(cent_sb[:]))
 
@@ -129,6 +129,10 @@ def tile_picked_ivfpq_none_po_kernel(
         placed["w1"] = keep.tile([P, V], U8, name="placed_w1", tag="stage_1", align_bytes=64)
         nc.gpsimd.memset(placed["w1"][:].bitcast(I32), 0)
         place("w1")
+        qn_sb = shared.tile([P, PACK], F32, name="qn_sb", offset=0, align_bytes=64)
+        dn_last = shared.tile([P, 1], F32, name="dn_last", offset=64, align_bytes=64)
+        nc.sync.dma_start(out=qn_sb[:], in_=qn.rearrange("(p t) o -> p (t o)", t=PACK))
+        nc.sync.dma_start(out=dn_last[:], in_=dn[0:1, NEAR:].rearrange("o p -> p o"))
 
         for pair in range(2):
             dn_ps = psum.tile([P, 2, P], F32, name="dn_ps", tag="bank_%d" % (6 + pair))
@@ -192,10 +196,8 @@ def tile_picked_ivfpq_none_po_kernel(
         y_near = keep.tile([P, PACK, NEAR], F32, name="y_near")
         y_last = keep.tile([P, PACK, P], F32, name="y_last")
         y = [y_near[:, :, stretches[0]], y_near[:, :, stretches[1]], y_last[:]]
-        rounded = [
-            keep.tile([P, cols.stop - cols.start, PACK], BF16, name="rounded_%d" % cols.start, align_bytes=64)
-            for cols in stretches
-        ]
+        rounded = [keep.tile([P, S // 2, PACK], BF16, name="rounded_%d" % h, align_bytes=64) for h in range(2)]
+        rounded_parts = [rounded[0][:], rounded[1][:, :P, :], rounded[1][:, P:, :]]
 
         def look_up(t, cols):
             nc.vector.tensor_tensor(
@@ -210,7 +212,7 @@ def tile_picked_ivfpq_none_po_kernel(
 
         def round_y(copy, index):
             copy(
-                out=rounded[index][:].rearrange("p (c i) t -> p c t i", i=4),
+                out=rounded_parts[index].rearrange("p (c i) t -> p c t i", i=4),
                 in_=y[index].rearrange("p t (c i) -> p c t i", i=4),
             )
 
@@ -226,7 +228,7 @@ def tile_picked_ivfpq_none_po_kernel(
             if t % 2:
                 store(y_last, stretches[2], t - 1, t + 1)
         round_y(nc.vector.tensor_copy, 2)
-        for index, cols in enumerate(stretches):
+        for index, cols in enumerate(halves):
             nc.vector.quantize_mx(
                 out=y_words[:, cols].bitcast(FP8X4),
                 scales=y_scales[:, cols],

@@ -18,7 +18,7 @@ ACT = mybir.ActivationFunctionType
 
 P = 128
 PACK = 4
-NEAR = S - P
+HALF = S // 2
 
 
 def tile_picked_ivfpq_none_po_kernel(
@@ -35,38 +35,39 @@ def tile_picked_ivfpq_none_po_kernel(
         own_sb = keep.tile([P, S // 16], U16, name="own_sb")
         xs = keep.tile([P, T], U8, name="xs", align_bytes=64)
         xw = keep.tile([P, T], I32, name="xw", align_bytes=64)
-        dn_col = keep.tile([P, PACK], F32, name="dn_col")
-        dn_sb = keep.tile([P, NEAR], F32, name="dn_sb")
+        qn_sb = keep.tile([P, PACK], F32, name="qn_sb")
         ident = keep.tile([P, P], F32, name="ident")
-        placed = {"w2": keep.tile([P, S], U8, name="placed_w2", align_bytes=64)}
-        raw_w2 = [
-            keep.tile([P, PACK, N // 2], F32, name="raw_w2", tag="stage_%d" % h, align_bytes=64) for h in range(2)
+        placed = {"w1": keep.tile([P, V], U8, name="placed_w1", align_bytes=64)}
+        stage = PACK * (N // 2) * 4
+        raw_w1 = [
+            shared.tile([P, PACK, N // 2], F32, name="raw_w1_0", offset=stage, align_bytes=64),
+            shared.tile([P, PACK, N // 2], F32, name="raw_w1_1", offset=2 * stage, align_bytes=64),
         ]
-        raw_w1 = [keep.tile([P, PACK, N // 2], F32, name="raw_w1_0")]
 
         def load_weights(raw, columns):
             nc.sync.dma_start(out=raw[:], in_=columns.rearrange("(p j) c -> p j c", j=PACK))
 
         nc.vector.memset(xs[:].bitcast(I32), 0)
-        load_weights(raw_w2[0], w2[:, : N // 2])
-        nc.sync.dma_start(offs_sb[:], offs)
+        load_weights(raw_w1[0], w1[:, : N // 2])
         nc.sync.dma_start(cent_sb[:], cent)
+        nc.sync.dma_start(offs_sb[:], offs)
         nc.sync.dma_start(own_sb[:], own)
         nc.sync.dma_start(out=xs[0:P:8, :].bitcast(I32), in_=x_scales[0].bitcast(I32))
-        nc.scalar.dma_start(out=dn_col[:], in_=dn[0:1, :].rearrange("o (p u) -> p (o u)", u=PACK))
-        load_weights(raw_w2[1], w2[:, N // 2 :])
+        load_weights(raw_w1[1], w1[:, N // 2 :])
         nc.sync.dma_start(out=xw[:], in_=x_words[0].rearrange("p n t -> p (n t)").bitcast(I32))
-        load_weights(raw_w1[0], w1[:, : N // 2])
+        nc.sync.dma_start(out=qn_sb[:], in_=qn.rearrange("(p t) o -> p (t o)", t=PACK))
+        raw_w2 = [shared.tile([P, PACK, N // 2], F32, name="raw_w2_0", offset=0, align_bytes=64)]
+        load_weights(raw_w2[0], w2[:, : N // 2])
 
         make_identity(nc, ident[:])
-        nc.gpsimd.memset(placed["w2"][:].bitcast(I32), 0)
+        nc.gpsimd.memset(placed["w1"][:].bitcast(I32), 0)
 
         picked = {
-            "w2": shared.tile([P, S], U8, name="picked_w2", offset=0, align_bytes=64),
             "w1": keep.tile([P, V], U8, name="picked_w1", align_bytes=64),
+            "w2": keep.tile([P, S], U8, name="picked_w2", align_bytes=64),
         }
-        nc.vector.tensor_copy(picked["w2"][:], xs[:].indirect(offs_sb[:]))
         nc.vector.tensor_copy(picked["w1"][:], xs[:].indirect(cent_sb[:]))
+        nc.vector.tensor_copy(picked["w2"][:], xs[:].indirect(offs_sb[:]))
 
         def place(name):
             for r in range(4):
@@ -74,29 +75,28 @@ def tile_picked_ivfpq_none_po_kernel(
                     out=placed[name][r:P:32, :].bitcast(I32), in_=picked[name][8 * r : P : 32, :].bitcast(I32)
                 )
 
-        place("w2")
+        place("w1")
 
         grouped, codes, scales = {}, {}, {}
-        for name in ("w2", "w1"):
-            grouped[name] = keep.tile([P, PACK, P, PACK], BF16, name="grouped", tag="grouped_" + name, align_bytes=64)
+        grouped["w1"] = shared.tile([P, PACK, P, PACK], BF16, name="grouped_w1", offset=4 * stage, align_bytes=64)
+        grouped["w2"] = keep.tile([P, PACK, P, PACK], BF16, name="grouped", tag="grouped_w2", align_bytes=64)
+        for name in ("w1", "w2"):
             codes[name] = keep.tile([P, N], U32, name="codes_" + name, align_bytes=64)
             scales[name] = keep.tile([P, N], U8, name="scales_" + name, align_bytes=64)
 
-        def round_weights(name, raw):
-            for half, deals in ((0, slice(0, PACK)), (1, slice(0, 2)), (1, slice(2, PACK))):
-                rows = slice(half * P // 2, (half + 1) * P // 2)
-                nc.scalar.copy(
-                    out=grouped[name][:, deals, rows, :].rearrange("p t m j -> p m j t"),
-                    in_=raw[half][:].rearrange("p j (m t) -> p m j t", t=PACK)[:, :, :, deals],
-                )
+        def round_weights(copy, name, raw, half, deals):
+            rows = slice(half * P // 2, (half + 1) * P // 2)
+            copy(
+                out=grouped[name][:, deals, rows, :].rearrange("p t m j -> p m j t"),
+                in_=raw[half][:].rearrange("p j (m t) -> p m j t", t=PACK)[:, :, :, deals],
+            )
 
-        def quantize_weights(name):
-            for first, last in ((0, 1), (1, 2), (2, PACK)):
-                nc.vector.quantize_mx(
-                    out=codes[name][:, first * P : last * P].bitcast(FP8X4),
-                    scales=scales[name][:, first * P : last * P],
-                    in_=grouped[name][:, first:last, :, :].rearrange("p t m j -> p (t m j)"),
-                )
+        def quantize_weights(name, first, last):
+            nc.vector.quantize_mx(
+                out=codes[name][:, first * P : last * P].bitcast(FP8X4),
+                scales=scales[name][:, first * P : last * P],
+                in_=grouped[name][:, first:last, :, :].rearrange("p t m j -> p (t m j)"),
+            )
 
         def product(acc, name, t, words, cols):
             deal = slice(t * P, (t + 1) * P)
@@ -110,124 +110,131 @@ def tile_picked_ivfpq_none_po_kernel(
                 stop=True,
             )
 
-        halves = [slice(0, S // 2), slice(S // 2, S)]
-        stretches = [slice(0, S // 2), slice(S // 2, NEAR), slice(NEAR, S)]
-        rest = {}
+        for half in range(2):
+            round_weights(nc.scalar.copy, "w1", raw_w1, half, slice(0, PACK))
+        quantize_weights("w1", 0, PACK)
 
-        def add_norms(t):
-            acc = psum.tile([P, NEAR], F32, name="acc", tag="bank_%d" % t)
-            for part in stretches[:2]:
-                product(acc[:, part], "w2", t, vec_words, part)
-            nc.vector.scalar_tensor_tensor(
-                out=rest[t], in0=acc[:], scalar=-2.0, in1=dn_sb[:], op0=ALU.mult, op1=ALU.add
-            )
+        raw_w2.append(shared.tile([P, PACK, N // 2], F32, name="raw_w2_1", offset=stage, align_bytes=64))
+        load_weights(raw_w2[1], w2[:, N // 2 :])
+        placed["w2"] = shared.tile([P, S], U8, name="placed_w2", offset=2 * stage, align_bytes=64)
+        dn_sb = shared.tile([P, HALF], F32, name="dn_sb", offset=2 * stage + 512, align_bytes=64)
+        dn_col = shared.tile([P, 2], F32, name="dn_col", offset=2 * stage + 2048, align_bytes=64)
+        nc.gpsimd.memset(placed["w2"][:].bitcast(I32), 0)
+        place("w2")
+        nc.sync.dma_start(out=dn_sb[:], in_=dn[:, :HALF])
+        with nc.allow_non_contiguous_dma(reason="one value of dn a partition and block"):
+            nc.sync.dma_start(out=dn_col[:], in_=dn[0:1, HALF:].rearrange("o (b p) -> p (o b)", p=P))
 
-        round_weights("w2", raw_w2)
-        quantize_weights("w2")
-        raw_w1.append(keep.tile([P, PACK, N // 2], F32, name="raw_w1_1", tag="stage_0", align_bytes=64))
-        load_weights(raw_w1[1], w1[:, N // 2 :])
-        placed["w1"] = keep.tile([P, V], U8, name="placed_w1", tag="stage_1", align_bytes=64)
-        nc.gpsimd.memset(placed["w1"][:].bitcast(I32), 0)
-        place("w1")
-        qn_sb = shared.tile([P, PACK], F32, name="qn_sb", offset=0, align_bytes=64)
-        dn_last = shared.tile([P, 1], F32, name="dn_last", offset=64, align_bytes=64)
-        nc.sync.dma_start(out=qn_sb[:], in_=qn.rearrange("(p t) o -> p (t o)", t=PACK))
-        nc.sync.dma_start(out=dn_last[:], in_=dn[0:1, NEAR:].rearrange("o p -> p o"))
+        cent_words = shared.tile([P, V], U32, name="cent_words", offset=4 * stage, align_bytes=64)
+        vec_words = shared.tile([P, S], U32, name="vec_words", offset=4 * stage + 4 * V, align_bytes=64)
+        nc.vector.tensor_copy(cent_words[:], xw[:].bitcast(U32).indirect(cent_sb[:]))
+        nc.vector.tensor_copy(vec_words[:], xw[:].bitcast(U32).indirect(offs_sb[:]))
 
-        for pair in range(2):
-            dn_ps = psum.tile([P, 2, P], F32, name="dn_ps", tag="bank_%d" % (6 + pair))
-            for u in range(2):
-                column = dn_col[:, 2 * pair + u : 2 * pair + u + 1]
-                nc.tensor.transpose(dn_ps[:, u, :], column.to_broadcast([P, P]), ident[:])
-            nc.scalar.activation(
-                out=dn_sb[:].rearrange("m (p u) -> m p u", u=PACK)[:, :, 2 * pair : 2 * pair + 2],
-                in_=dn_ps[:, :, : NEAR // PACK].rearrange("m u p -> m p u"),
-                func=ACT.Identity,
-            )
-
-        picked_words = keep.tile([P, S + V], U32, name="picked_words", tag="grouped_w2", align_bytes=64)
-        vec_words, cent_words = picked_words[:, :S], picked_words[:, S:]
-        nc.vector.tensor_copy(vec_words, xw[:].bitcast(U32).indirect(offs_sb[:]))
-        nc.vector.tensor_copy(cent_words, xw[:].bitcast(U32).indirect(cent_sb[:]))
-
-        early = keep.tile([P, 2, NEAR], F32, name="early")
-        rest[0], rest[1] = early[:, 0, :], early[:, 1, :]
-        add_norms(0)
-        add_norms(1)
-        round_weights("w1", raw_w1)
-        quantize_weights("w1")
-        late = keep.tile([P, 2, NEAR], F32, name="late", tag="stage_0", align_bytes=64)
-        rest[2], rest[3] = late[:, 0, :], late[:, 1, :]
-        turned = keep.tile([P, N], F32, name="turned")
-        add_norms(2)
-        add_norms(3)
+        round_weights(nc.scalar.copy, "w2", raw_w2, 0, slice(0, PACK))
         c_rows = []
         for t in range(PACK):
-            c_t = keep.tile([P, V], F32, name="c_%d" % t)
-            for index, cols in enumerate(halves if t == 0 else [slice(0, V)]):
-                acc = psum.tile([P, cols.stop - cols.start], F32, name="acc", tag="bank_%d" % (4 + t - 4 * index))
-                product(acc[:], "w1", t, cent_words, cols)
-                nc.scalar.activation(
-                    out=c_t[:, cols], in_=acc[:], func=ACT.Identity, bias=qn_sb[:, t : t + 1], scale=-2.0
-                )
+            if t == 0:
+                c_t = shared.tile([P, V], F32, name="c_0", offset=0, align_bytes=64)
+            else:
+                c_t = keep.tile([P, V], F32, name="c_%d" % t)
+            acc = psum.tile([P, V], F32, name="acc", tag="bank_%d" % t)
+            product(acc[:], "w1", t, cent_words, slice(0, V))
+            nc.scalar.activation(out=c_t[:], in_=acc[:], func=ACT.Identity, bias=qn_sb[:, t : t + 1], scale=-2.0)
             c_rows.append(c_t)
-            if t == 1:
-                turned_ps = psum.tile([P, N], F32, name="turned_ps", tag="bank_4")
+
+        pairs = [slice(0, 2), slice(2, PACK)]
+        for pair in pairs:
+            round_weights(nc.vector.tensor_copy, "w2", raw_w2, 1, pair)
+        for pair in pairs:
+            quantize_weights("w2", pair.start, pair.stop)
+
+        blocks = [slice(HALF, HALF + P), slice(HALF + P, S)]
+        back = []
+        for b, cols in enumerate(blocks):
+            turned_ps = psum.tile([P, N], F32, name="turned_ps", tag="bank_%d" % (6 + b))
+            for pair in pairs:
+                rows = slice(pair.start * P, pair.stop * P)
                 nc.tensor.matmul_mx(
-                    out=turned_ps[:],
-                    lhsT=vec_words[:, NEAR:].bitcast(FP8X4),
-                    lhsT_scale=placed["w2"][:, NEAR:],
-                    rhs=codes["w2"][:].bitcast(FP8X4),
-                    rhs_scale=scales["w2"][:],
+                    out=turned_ps[:, rows],
+                    lhsT=vec_words[:, cols].bitcast(FP8X4),
+                    lhsT_scale=placed["w2"][:, cols],
+                    rhs=codes["w2"][:, rows].bitcast(FP8X4),
+                    rhs_scale=scales["w2"][:, rows],
                     start=True,
                     stop=True,
                 )
-                nc.scalar.activation(out=turned[:], in_=turned_ps[:], func=ACT.Identity, bias=dn_last[:], scale=-2.0)
-        back = psum.tile([P, PACK, P], F32, name="back", tag="bank_1")
-        for t in range(PACK):
-            nc.tensor.transpose(back[:, t, :], turned[:, t * P : (t + 1) * P], ident[:])
-        rest_last = keep.tile([P, PACK, P], F32, name="rest_last")
-        nc.scalar.copy(out=rest_last[:], in_=back[:])
+            turned = keep.tile([P, N], F32, name="turned_%d" % b)
+            nc.scalar.activation(
+                out=turned[:], in_=turned_ps[:], func=ACT.Identity, bias=dn_col[:, b : b + 1], scale=-2.0
+            )
+            back.append((turned, psum.tile([P, PACK, P], F32, name="back", tag="bank_%d" % b)))
+        near_ps = []
+        for index, pair in enumerate(pairs):
+            acc = psum.tile([P, 2, HALF], F32, name="near_ps", tag="bank_%d" % (4 + index))
+            for t in range(pair.start, pair.stop):
+                product(acc[:, t - pair.start, :], "w2", t, vec_words, slice(0, HALF))
+            near_ps.append(acc)
+        for turned, bank in back:
+            for t in range(PACK):
+                nc.tensor.transpose(bank[:, t, :], turned[:, t * P : (t + 1) * P], ident[:])
 
         y_words = keep.tile([P, S], I32, name="y_words", align_bytes=64)
         y_scales = keep.tile([P, S], U8, name="y_scales", align_bytes=64)
         out_rows = out_0.rearrange("(p t) j -> p t j", t=PACK)
         out_words = out_1[0].rearrange("p n t -> p (n t)").bitcast(I32)
-        y_near = keep.tile([P, PACK, NEAR], F32, name="y_near")
-        y_last = keep.tile([P, PACK, P], F32, name="y_last")
-        y = [y_near[:, :, stretches[0]], y_near[:, :, stretches[1]], y_last[:]]
-        rounded = [keep.tile([P, S // 2, PACK], BF16, name="rounded_%d" % h, align_bytes=64) for h in range(2)]
-        rounded_parts = [rounded[0][:], rounded[1][:, :P, :], rounded[1][:, P:, :]]
+        fetched_near = keep.tile([P, PACK, HALF], F32, name="fetched_near", tag="grouped_w2", align_bytes=64)
+        fetched_far = shared.tile([P, PACK, HALF], F32, name="fetched_far", offset=2 * stage + 2048, align_bytes=64)
+        y_near = keep.tile([P, PACK, HALF], F32, name="y_near")
+        y_far = [keep.tile([P, PACK, P], F32, name="y_far_%d" % b) for b in range(2)]
+        rounded = [keep.tile([P, HALF, PACK], BF16, name="rounded_%d" % h, align_bytes=64) for h in range(2)]
 
-        def look_up(t, cols):
-            nc.vector.tensor_tensor(
-                y_near[:, t, cols] if cols.stop <= NEAR else y_last[:, t, :],
-                c_rows[t][:].indirect(own_sb[:, cols.start // 16 : cols.stop // 16]),
-                rest[t][:, cols] if cols.stop <= NEAR else rest_last[:, t, :],
-                ALU.add,
+        def offsets(cols):
+            return own_sb[:, cols.start // 16 : cols.stop // 16]
+
+        def fetch_far(t, cols):
+            nc.scalar.activation(
+                out=fetched_far[:, t, cols.start - HALF : cols.stop - HALF],
+                in_=c_rows[t][:].indirect(offsets(cols)),
+                func=ACT.Copy,
             )
 
-        def store(values, cols, first, last):
-            nc.sync.dma_start(out=out_rows[:, first:last, cols], in_=values[:, first:last, :])
-
-        def round_y(copy, index):
+        def round_y(copy, target, values):
             copy(
-                out=rounded_parts[index].rearrange("p (c i) t -> p c t i", i=4),
-                in_=y[index].rearrange("p t (c i) -> p c t i", i=4),
+                out=target.rearrange("p (c i) t -> p c t i", i=4),
+                in_=values.rearrange("p t (c i) -> p c t i", i=4),
             )
 
         for t in range(PACK):
-            for cols in [slice(0, NEAR)] if t < PACK - 1 else stretches[:2]:
-                look_up(t, cols)
-            if t > 0:
-                store(y_near, slice(0, NEAR), 0 if t == 1 else t, t + 1)
-        round_y(nc.scalar.copy, 0)
-        round_y(nc.scalar.copy, 1)
-        for t in range(PACK):
-            look_up(t, stretches[2])
-            if t % 2:
-                store(y_last, stretches[2], t - 1, t + 1)
-        round_y(nc.vector.tensor_copy, 2)
+            nc.vector.tensor_tensor(
+                fetched_near[:, t, :], c_rows[t][:].indirect(offsets(slice(0, HALF))), dn_sb[:], ALU.add
+            )
+        for index, pair in enumerate(pairs):
+            nc.vector.scalar_tensor_tensor(
+                out=y_near[:, pair, :],
+                in0=near_ps[index][:],
+                scalar=-2.0,
+                in1=fetched_near[:, pair, :],
+                op0=ALU.mult,
+                op1=ALU.add,
+            )
+            nc.sync.dma_start(out=out_rows[:, pair, :HALF], in_=y_near[:, pair, :])
+        fetch_far(0, slice(HALF, S))
+        fetch_far(1, slice(HALF, S))
+        for cols in blocks:
+            fetch_far(2, cols)
+            fetch_far(3, cols)
+
+        def add_far(b):
+            nc.vector.tensor_tensor(y_far[b][:], back[b][1][:], fetched_far[:, :, b * P : (b + 1) * P], ALU.add)
+            nc.sync.dma_start(out=out_rows[:, :, blocks[b]], in_=y_far[b][:])
+
+        add_far(0)
+        round_y(nc.vector.tensor_copy, rounded[0][:, :P, :], y_near[:, :, :P])
+        add_far(1)
+        round_y(nc.scalar.copy, rounded[0][:, P:, :], y_near[:, :, P:])
+        round_y(nc.scalar.copy, rounded[1][:, :P, :], y_far[0][:])
+        round_y(nc.vector.tensor_copy, rounded[1][:, P:, :], y_far[1][:])
+        halves = [slice(0, HALF), slice(HALF, S)]
         for index, cols in enumerate(halves):
             nc.vector.quantize_mx(
                 out=y_words[:, cols].bitcast(FP8X4),

@@ -56,8 +56,6 @@ def tile_picked_ivfpq_none_po_kernel(
         load_weights(raw_w1[1], w1[:, N // 2 :])
         nc.sync.dma_start(out=xw[:], in_=x_words[0].rearrange("p n t -> p (n t)").bitcast(I32))
         nc.sync.dma_start(out=qn_sb[:], in_=qn.rearrange("(p t) o -> p (t o)", t=PACK))
-        raw_w2 = [shared.tile([P, PACK, N // 2], F32, name="raw_w2_0", offset=0, align_bytes=64)]
-        load_weights(raw_w2[0], w2[:, : N // 2])
 
         make_identity(nc, ident[:])
         nc.gpsimd.memset(placed["w1"][:].bitcast(I32), 0)
@@ -114,37 +112,44 @@ def tile_picked_ivfpq_none_po_kernel(
             round_weights(nc.scalar.copy, "w1", raw_w1, half, slice(0, PACK))
         quantize_weights("w1", 0, PACK)
 
-        raw_w2.append(shared.tile([P, PACK, N // 2], F32, name="raw_w2_1", offset=stage, align_bytes=64))
-        load_weights(raw_w2[1], w2[:, N // 2 :])
+        raw_w2 = shared.tile([P, PACK, N], F32, name="raw_w2", offset=0, align_bytes=64)
+        load_weights(raw_w2, w2)
         placed["w2"] = shared.tile([P, S], U8, name="placed_w2", offset=2 * stage, align_bytes=64)
         dn_sb = shared.tile([P, HALF], F32, name="dn_sb", offset=2 * stage + 512, align_bytes=64)
-        dn_col = shared.tile([P, 2], F32, name="dn_col", offset=2 * stage + 2048, align_bytes=64)
+        fetched_far = shared.tile([P, PACK, HALF], F32, name="fetched_far", offset=2 * stage + 2048, align_bytes=64)
+        dn_col = [fetched_far[:, 2, b * P : b * P + 1] for b in range(2)]
         nc.gpsimd.memset(placed["w2"][:].bitcast(I32), 0)
         place("w2")
         nc.sync.dma_start(out=dn_sb[:], in_=dn[:, :HALF])
-        with nc.allow_non_contiguous_dma(reason="one value of dn a partition and block"):
-            nc.sync.dma_start(out=dn_col[:], in_=dn[0:1, HALF:].rearrange("o (b p) -> p (o b)", p=P))
+        for b in range(2):
+            nc.sync.dma_start(out=dn_col[b], in_=dn[0:1, HALF + b * P : HALF + (b + 1) * P].rearrange("o p -> p o"))
 
         cent_words = shared.tile([P, V], U32, name="cent_words", offset=4 * stage, align_bytes=64)
         vec_words = shared.tile([P, S], U32, name="vec_words", offset=4 * stage + 4 * V, align_bytes=64)
-        nc.vector.tensor_copy(cent_words[:], xw[:].bitcast(U32).indirect(cent_sb[:]))
+        halves = [slice(0, HALF), slice(HALF, S)]
+        for cols in halves:
+            nc.vector.tensor_copy(
+                cent_words[:, cols], xw[:].bitcast(U32).indirect(cent_sb[:, cols.start // 16 : cols.stop // 16])
+            )
         nc.vector.tensor_copy(vec_words[:], xw[:].bitcast(U32).indirect(offs_sb[:]))
 
-        round_weights(nc.scalar.copy, "w2", raw_w2, 0, slice(0, PACK))
         c_rows = []
         for t in range(PACK):
-            if t == 0:
-                c_t = shared.tile([P, V], F32, name="c_0", offset=0, align_bytes=64)
-            else:
-                c_t = keep.tile([P, V], F32, name="c_%d" % t)
-            acc = psum.tile([P, V], F32, name="acc", tag="bank_%d" % t)
-            product(acc[:], "w1", t, cent_words, slice(0, V))
-            nc.scalar.activation(out=c_t[:], in_=acc[:], func=ACT.Identity, bias=qn_sb[:, t : t + 1], scale=-2.0)
+            c_t = keep.tile([P, V], F32, name="c_%d" % t)
+            for index, cols in enumerate(halves if t == 0 else [slice(0, V)]):
+                acc = psum.tile([P, cols.stop - cols.start], F32, name="acc", tag="bank_%d" % (t + 4 * index))
+                product(acc[:], "w1", t, cent_words, cols)
+                nc.scalar.activation(
+                    out=c_t[:, cols], in_=acc[:], func=ACT.Identity, bias=qn_sb[:, t : t + 1], scale=-2.0
+                )
             c_rows.append(c_t)
 
         pairs = [slice(0, 2), slice(2, PACK)]
         for pair in pairs:
-            round_weights(nc.vector.tensor_copy, "w2", raw_w2, 1, pair)
+            nc.vector.tensor_copy(
+                out=grouped["w2"][:, pair, :, :].rearrange("p t m j -> p m j t"),
+                in_=raw_w2[:].rearrange("p j (m t) -> p m j t", t=PACK)[:, :, :, pair],
+            )
         for pair in pairs:
             quantize_weights("w2", pair.start, pair.stop)
 
@@ -165,7 +170,7 @@ def tile_picked_ivfpq_none_po_kernel(
                 )
             turned = keep.tile([P, N], F32, name="turned_%d" % b)
             nc.scalar.activation(
-                out=turned[:], in_=turned_ps[:], func=ACT.Identity, bias=dn_col[:, b : b + 1], scale=-2.0
+                out=turned[:], in_=turned_ps[:], func=ACT.Identity, bias=dn_col[b], scale=-2.0
             )
             back.append((turned, psum.tile([P, PACK, P], F32, name="back", tag="bank_%d" % b)))
         near_ps = []
@@ -183,7 +188,6 @@ def tile_picked_ivfpq_none_po_kernel(
         out_rows = out_0.rearrange("(p t) j -> p t j", t=PACK)
         out_words = out_1[0].rearrange("p n t -> p (n t)").bitcast(I32)
         fetched_near = keep.tile([P, PACK, HALF], F32, name="fetched_near", tag="grouped_w2", align_bytes=64)
-        fetched_far = shared.tile([P, PACK, HALF], F32, name="fetched_far", offset=2 * stage + 2048, align_bytes=64)
         y_near = keep.tile([P, PACK, HALF], F32, name="y_near")
         y_far = [keep.tile([P, PACK, P], F32, name="y_far_%d" % b) for b in range(2)]
         rounded = [keep.tile([P, HALF, PACK], BF16, name="rounded_%d" % h, align_bytes=64) for h in range(2)]
@@ -229,12 +233,10 @@ def tile_picked_ivfpq_none_po_kernel(
             nc.sync.dma_start(out=out_rows[:, :, blocks[b]], in_=y_far[b][:])
 
         add_far(0)
-        round_y(nc.vector.tensor_copy, rounded[0][:, :P, :], y_near[:, :, :P])
         add_far(1)
-        round_y(nc.scalar.copy, rounded[0][:, P:, :], y_near[:, :, P:])
+        round_y(nc.scalar.copy, rounded[0][:], y_near[:])
         round_y(nc.scalar.copy, rounded[1][:, :P, :], y_far[0][:])
         round_y(nc.vector.tensor_copy, rounded[1][:, P:, :], y_far[1][:])
-        halves = [slice(0, HALF), slice(HALF, S)]
         for index, cols in enumerate(halves):
             nc.vector.quantize_mx(
                 out=y_words[:, cols].bitcast(FP8X4),

@@ -56,6 +56,8 @@ def tile_picked_ivfpq_none_po_kernel(
         load_weights(raw_w1[1], w1[:, N // 2 :])
         nc.sync.dma_start(out=xw[:], in_=x_words[0].rearrange("p n t -> p (n t)").bitcast(I32))
         nc.sync.dma_start(out=qn_sb[:], in_=qn.rearrange("(p t) o -> p (t o)", t=PACK))
+        raw_w2 = [shared.tile([P, PACK, N // 2], F32, name="raw_w2_0", offset=0, align_bytes=64)]
+        load_weights(raw_w2[0], w2[:, : N // 2])
 
         make_identity(nc, ident[:])
         nc.gpsimd.memset(placed["w1"][:].bitcast(I32), 0)
@@ -112,12 +114,15 @@ def tile_picked_ivfpq_none_po_kernel(
             round_weights(nc.scalar.copy, "w1", raw_w1, half, slice(0, PACK))
         quantize_weights("w1", 0, PACK)
 
-        raw_w2 = shared.tile([P, PACK, N], F32, name="raw_w2", offset=0, align_bytes=64)
-        load_weights(raw_w2, w2)
+        raw_w2.append(shared.tile([P, PACK, N // 2], F32, name="raw_w2_1", offset=stage, align_bytes=64))
+        load_weights(raw_w2[1], w2[:, N // 2 :])
         placed["w2"] = shared.tile([P, S], U8, name="placed_w2", offset=2 * stage, align_bytes=64)
         dn_sb = shared.tile([P, HALF], F32, name="dn_sb", offset=2 * stage + 512, align_bytes=64)
-        fetched_far = shared.tile([P, PACK, HALF], F32, name="fetched_far", offset=2 * stage + 2048, align_bytes=64)
-        dn_col = [fetched_far[:, 2, b * P : b * P + 1] for b in range(2)]
+        far_at = [3 * stage - 64 - stage // 2, 3 * stage - 64]
+        dn_col = [
+            shared.tile([P, 16], F32, name="dn_col_0", offset=far_at[1] - 32)[:, 0:1],
+            shared.tile([P, 1], F32, name="dn_col_1", offset=2 * stage + 1600)[:],
+        ]
         nc.gpsimd.memset(placed["w2"][:].bitcast(I32), 0)
         place("w2")
         nc.sync.dma_start(out=dn_sb[:], in_=dn[:, :HALF])
@@ -127,36 +132,33 @@ def tile_picked_ivfpq_none_po_kernel(
         cent_words = shared.tile([P, V], U32, name="cent_words", offset=4 * stage, align_bytes=64)
         vec_words = shared.tile([P, S], U32, name="vec_words", offset=4 * stage + 4 * V, align_bytes=64)
         halves = [slice(0, HALF), slice(HALF, S)]
-        for cols in halves:
-            nc.vector.tensor_copy(
-                cent_words[:, cols], xw[:].bitcast(U32).indirect(cent_sb[:, cols.start // 16 : cols.stop // 16])
-            )
+        nc.vector.tensor_copy(cent_words[:], xw[:].bitcast(U32).indirect(cent_sb[:]))
         nc.vector.tensor_copy(vec_words[:], xw[:].bitcast(U32).indirect(offs_sb[:]))
 
+        round_weights(nc.scalar.copy, "w2", raw_w2, 0, slice(0, PACK))
         c_rows = []
         for t in range(PACK):
-            c_t = keep.tile([P, V], F32, name="c_%d" % t)
-            for index, cols in enumerate(halves if t == 0 else [slice(0, V)]):
-                acc = psum.tile([P, cols.stop - cols.start], F32, name="acc", tag="bank_%d" % (t + 4 * index))
-                product(acc[:], "w1", t, cent_words, cols)
-                nc.scalar.activation(
-                    out=c_t[:, cols], in_=acc[:], func=ACT.Identity, bias=qn_sb[:, t : t + 1], scale=-2.0
-                )
+            if t == 0:
+                c_t = shared.tile([P, V], F32, name="c_0", offset=0, align_bytes=64)
+            else:
+                c_t = keep.tile([P, V], F32, name="c_%d" % t)
+            acc = psum.tile([P, V], F32, name="acc", tag="bank_%d" % t)
+            product(acc[:], "w1", t, cent_words, slice(0, V))
+            nc.scalar.activation(out=c_t[:], in_=acc[:], func=ACT.Identity, bias=qn_sb[:, t : t + 1], scale=-2.0)
             c_rows.append(c_t)
 
         pairs = [slice(0, 2), slice(2, PACK)]
         for pair in pairs:
-            nc.vector.tensor_copy(
-                out=grouped["w2"][:, pair, :, :].rearrange("p t m j -> p m j t"),
-                in_=raw_w2[:].rearrange("p j (m t) -> p m j t", t=PACK)[:, :, :, pair],
-            )
+            round_weights(nc.vector.tensor_copy, "w2", raw_w2, 1, pair)
         for pair in pairs:
             quantize_weights("w2", pair.start, pair.stop)
 
         blocks = [slice(HALF, HALF + P), slice(HALF + P, S)]
-        back = []
+        turned = [keep.tile([P, N], F32, name="turned_%d" % b) for b in range(2)]
+        turned_banks = []
         for b, cols in enumerate(blocks):
             turned_ps = psum.tile([P, N], F32, name="turned_ps", tag="bank_%d" % (6 + b))
+            turned_banks.append(turned_ps)
             for pair in pairs:
                 rows = slice(pair.start * P, pair.stop * P)
                 nc.tensor.matmul_mx(
@@ -168,36 +170,41 @@ def tile_picked_ivfpq_none_po_kernel(
                     start=True,
                     stop=True,
                 )
-            turned = keep.tile([P, N], F32, name="turned_%d" % b)
-            nc.scalar.activation(
-                out=turned[:], in_=turned_ps[:], func=ACT.Identity, bias=dn_col[b], scale=-2.0
-            )
-            back.append((turned, psum.tile([P, PACK, P], F32, name="back", tag="bank_%d" % b)))
+        nc.scalar.activation(out=turned[0][:], in_=turned_banks[0][:], func=ACT.Identity, bias=dn_col[0], scale=-2.0)
+        nc.vector.tensor_scalar(
+            out=turned[1][:], in0=turned_banks[1][:], scalar1=-2.0, scalar2=dn_col[1], op0=ALU.mult, op1=ALU.add
+        )
         near_ps = []
         for index, pair in enumerate(pairs):
             acc = psum.tile([P, 2, HALF], F32, name="near_ps", tag="bank_%d" % (4 + index))
             for t in range(pair.start, pair.stop):
                 product(acc[:, t - pair.start, :], "w2", t, vec_words, slice(0, HALF))
             near_ps.append(acc)
-        for turned, bank in back:
-            for t in range(PACK):
-                nc.tensor.transpose(bank[:, t, :], turned[:, t * P : (t + 1) * P], ident[:])
+        back = []
+        for index, pair in enumerate(pairs):
+            back.append(psum.tile([P, 2, HALF], F32, name="back", tag="bank_%d" % index))
+            for b in range(2):
+                for t in range(pair.start, pair.stop):
+                    nc.tensor.transpose(
+                        back[index][:, t - pair.start, b * P : (b + 1) * P], turned[b][:, t * P : (t + 1) * P], ident[:]
+                    )
 
-        y_words = keep.tile([P, S], I32, name="y_words", align_bytes=64)
         y_scales = keep.tile([P, S], U8, name="y_scales", align_bytes=64)
         out_rows = out_0.rearrange("(p t) j -> p t j", t=PACK)
         out_words = out_1[0].rearrange("p n t -> p (n t)").bitcast(I32)
         fetched_near = keep.tile([P, PACK, HALF], F32, name="fetched_near", tag="grouped_w2", align_bytes=64)
+        fetched_far = [
+            shared.tile([P, 2, HALF], F32, name="fetched_far_%d" % index, offset=at, align_bytes=64)
+            for index, at in enumerate(far_at)
+        ]
         y_near = keep.tile([P, PACK, HALF], F32, name="y_near")
-        y_far = [keep.tile([P, PACK, P], F32, name="y_far_%d" % b) for b in range(2)]
-        rounded = [keep.tile([P, HALF, PACK], BF16, name="rounded_%d" % h, align_bytes=64) for h in range(2)]
 
         def offsets(cols):
             return own_sb[:, cols.start // 16 : cols.stop // 16]
 
         def fetch_far(t, cols):
             nc.scalar.activation(
-                out=fetched_far[:, t, cols.start - HALF : cols.stop - HALF],
+                out=fetched_far[t // 2][:, t % 2, cols.start - HALF : cols.stop - HALF],
                 in_=c_rows[t][:].indirect(offsets(cols)),
                 func=ACT.Copy,
             )
@@ -209,9 +216,7 @@ def tile_picked_ivfpq_none_po_kernel(
             )
 
         for t in range(PACK):
-            nc.vector.tensor_tensor(
-                fetched_near[:, t, :], c_rows[t][:].indirect(offsets(slice(0, HALF))), dn_sb[:], ALU.add
-            )
+            nc.vector.tensor_tensor(fetched_near[:, t, :], c_rows[t][:].indirect(offsets(halves[0])), dn_sb[:], ALU.add)
         for index, pair in enumerate(pairs):
             nc.vector.scalar_tensor_tensor(
                 out=y_near[:, pair, :],
@@ -222,27 +227,41 @@ def tile_picked_ivfpq_none_po_kernel(
                 op1=ALU.add,
             )
             nc.sync.dma_start(out=out_rows[:, pair, :HALF], in_=y_near[:, pair, :])
-        fetch_far(0, slice(HALF, S))
-        fetch_far(1, slice(HALF, S))
+        y_far = keep.tile([P, PACK, HALF], F32, name="y_far", tag="grouped_w2", align_bytes=64)
+        fetch_far(0, halves[1])
+        fetch_far(1, halves[1])
         for cols in blocks:
             fetch_far(2, cols)
             fetch_far(3, cols)
 
-        def add_far(b):
-            nc.vector.tensor_tensor(y_far[b][:], back[b][1][:], fetched_far[:, :, b * P : (b + 1) * P], ALU.add)
-            nc.sync.dma_start(out=out_rows[:, :, blocks[b]], in_=y_far[b][:])
+        def add_far(index, part):
+            nc.vector.tensor_tensor(
+                y_far[:, pairs[index], part], back[index][:, :, part], fetched_far[index][:, :, part], ALU.add
+            )
 
-        add_far(0)
-        add_far(1)
-        round_y(nc.scalar.copy, rounded[0][:], y_near[:])
-        round_y(nc.scalar.copy, rounded[1][:, :P, :], y_far[0][:])
-        round_y(nc.vector.tensor_copy, rounded[1][:, P:, :], y_far[1][:])
-        for index, cols in enumerate(halves):
+        def store_far(index):
+            nc.sync.dma_start(out=out_rows[:, pairs[index], HALF:], in_=y_far[:, pairs[index], :])
+
+        def quantize_y(index):
             nc.vector.quantize_mx(
-                out=y_words[:, cols].bitcast(FP8X4),
-                scales=y_scales[:, cols],
+                out=y_words[:, halves[index]].bitcast(FP8X4),
+                scales=y_scales[:, halves[index]],
                 in_=rounded[index][:].rearrange("p c t -> p (c t)"),
             )
+
+        add_far(0, slice(0, HALF))
+        store_far(0)
+        rounded = [keep.tile([P, HALF, PACK], BF16, name="rounded_0", align_bytes=64)]
+        add_far(1, slice(0, P))
+        add_far(1, slice(P, HALF))
+        store_far(1)
+        rounded.append(shared.tile([P, HALF, PACK], BF16, name="rounded_1", offset=far_at[1] - 1024, align_bytes=64))
+        y_words = shared.tile([P, S], I32, name="y_words", offset=far_at[1] + 1024, align_bytes=64)
+        round_y(nc.scalar.copy, rounded[0][:], y_near[:])
+        round_y(nc.vector.tensor_copy, rounded[1][:, :P, :], y_far[:, :, :P])
+        round_y(nc.scalar.copy, rounded[1][:, P:, :], y_far[:, :, P:])
+        quantize_y(0)
+        quantize_y(1)
         nc.sync.dma_start(out=out_words[:, halves[0]], in_=y_words[:, halves[0]])
         nc.scalar.dma_start(out=out_words[:, halves[1]], in_=y_words[:, halves[1]])
         for q in range(4):

@@ -53,9 +53,9 @@ def tile_picked_ivfpq_none_po_kernel(
         nc.sync.dma_start(offs_sb[:], offs)
         nc.sync.dma_start(own_sb[:], own)
         nc.sync.dma_start(out=xs[0:P:8, :].bitcast(I32), in_=x_scales[0].bitcast(I32))
+        nc.scalar.dma_start(out=qn_sb[:], in_=qn.rearrange("(p t) o -> p (t o)", t=PACK))
         load_weights(raw_w1[1], w1[:, N // 2 :])
         nc.sync.dma_start(out=xw[:], in_=x_words[0].rearrange("p n t -> p (n t)").bitcast(I32))
-        nc.sync.dma_start(out=qn_sb[:], in_=qn.rearrange("(p t) o -> p (t o)", t=PACK))
         raw_w2 = [shared.tile([P, PACK, N // 2], F32, name="raw_w2_0", offset=0, align_bytes=64)]
         load_weights(raw_w2[0], w2[:, : N // 2])
 
@@ -117,17 +117,15 @@ def tile_picked_ivfpq_none_po_kernel(
         raw_w2.append(shared.tile([P, PACK, N // 2], F32, name="raw_w2_1", offset=stage, align_bytes=64))
         load_weights(raw_w2[1], w2[:, N // 2 :])
         placed["w2"] = shared.tile([P, S], U8, name="placed_w2", offset=2 * stage, align_bytes=64)
-        dn_sb = shared.tile([P, HALF], F32, name="dn_sb", offset=2 * stage + 512, align_bytes=64)
-        far_at = [3 * stage - 64 - stage // 2, 3 * stage - 64]
+        dn_sb = shared.tile([P, S], F32, name="dn_sb", offset=2 * stage + 512, align_bytes=64)
+        far_at = [3 * stage, 3 * stage + stage // 2]
         dn_col = [
             shared.tile([P, 16], F32, name="dn_col_0", offset=far_at[1] - 32)[:, 0:1],
-            shared.tile([P, 1], F32, name="dn_col_1", offset=2 * stage + 1600)[:],
+            shared.tile([P, 1], F32, name="dn_col_1", offset=2 * stage + 2624)[:],
         ]
         nc.gpsimd.memset(placed["w2"][:].bitcast(I32), 0)
         place("w2")
-        nc.sync.dma_start(out=dn_sb[:], in_=dn[:, :HALF])
-        for b in range(2):
-            nc.sync.dma_start(out=dn_col[b], in_=dn[0:1, HALF + b * P : HALF + (b + 1) * P].rearrange("o p -> p o"))
+        nc.sync.dma_start(out=dn_sb[:], in_=dn)
 
         cent_words = shared.tile([P, V], U32, name="cent_words", offset=4 * stage, align_bytes=64)
         vec_words = shared.tile([P, S], U32, name="vec_words", offset=4 * stage + 4 * V, align_bytes=64)
@@ -147,6 +145,11 @@ def tile_picked_ivfpq_none_po_kernel(
             nc.scalar.activation(out=c_t[:], in_=acc[:], func=ACT.Identity, bias=qn_sb[:, t : t + 1], scale=-2.0)
             c_rows.append(c_t)
 
+        dn_ps = psum.tile([P, 2, P], F32, name="dn_ps", tag="bank_5")
+        for b in range(2):
+            nc.tensor.transpose(dn_ps[:, b, :], dn_sb[:, HALF + b * P : HALF + (b + 1) * P], ident[:])
+            nc.scalar.copy(out=dn_col[b], in_=dn_ps[:, b, 0:1])
+
         pairs = [slice(0, 2), slice(2, PACK)]
         for pair in pairs:
             round_weights(nc.vector.tensor_copy, "w2", raw_w2, 1, pair)
@@ -154,7 +157,7 @@ def tile_picked_ivfpq_none_po_kernel(
             quantize_weights("w2", pair.start, pair.stop)
 
         blocks = [slice(HALF, HALF + P), slice(HALF + P, S)]
-        turned = [keep.tile([P, N], F32, name="turned_%d" % b) for b in range(2)]
+        turned = [keep.tile([P, N], F32, name="turned_0")]
         turned_banks = []
         for b, cols in enumerate(blocks):
             turned_ps = psum.tile([P, N], F32, name="turned_ps", tag="bank_%d" % (6 + b))
@@ -171,24 +174,12 @@ def tile_picked_ivfpq_none_po_kernel(
                     stop=True,
                 )
         nc.scalar.activation(out=turned[0][:], in_=turned_banks[0][:], func=ACT.Identity, bias=dn_col[0], scale=-2.0)
-        nc.vector.tensor_scalar(
-            out=turned[1][:], in0=turned_banks[1][:], scalar1=-2.0, scalar2=dn_col[1], op0=ALU.mult, op1=ALU.add
-        )
         near_ps = []
         for index, pair in enumerate(pairs):
             acc = psum.tile([P, 2, HALF], F32, name="near_ps", tag="bank_%d" % (4 + index))
             for t in range(pair.start, pair.stop):
                 product(acc[:, t - pair.start, :], "w2", t, vec_words, slice(0, HALF))
             near_ps.append(acc)
-        back = []
-        for index, pair in enumerate(pairs):
-            back.append(psum.tile([P, 2, HALF], F32, name="back", tag="bank_%d" % index))
-            for b in range(2):
-                for t in range(pair.start, pair.stop):
-                    nc.tensor.transpose(
-                        back[index][:, t - pair.start, b * P : (b + 1) * P], turned[b][:, t * P : (t + 1) * P], ident[:]
-                    )
-
         y_scales = keep.tile([P, S], U8, name="y_scales", align_bytes=64)
         out_rows = out_0.rearrange("(p t) j -> p t j", t=PACK)
         out_words = out_1[0].rearrange("p n t -> p (n t)").bitcast(I32)
@@ -216,7 +207,20 @@ def tile_picked_ivfpq_none_po_kernel(
             )
 
         for t in range(PACK):
-            nc.vector.tensor_tensor(fetched_near[:, t, :], c_rows[t][:].indirect(offsets(halves[0])), dn_sb[:], ALU.add)
+            nc.vector.tensor_tensor(fetched_near[:, t, :], c_rows[t][:].indirect(offsets(halves[0])), dn_sb[:, :HALF], ALU.add)
+        turned.append(shared.tile([P, N], F32, name="turned_1", offset=2 * stage - 512, align_bytes=64))
+        nc.vector.tensor_scalar(
+            out=turned[1][:], in0=turned_banks[1][:], scalar1=-2.0, scalar2=dn_col[1], op0=ALU.mult, op1=ALU.add
+        )
+        back = []
+        for index, pair in enumerate(pairs):
+            back.append(psum.tile([P, 2, HALF], F32, name="back", tag="bank_%d" % index))
+            for b in range(2):
+                for t in range(pair.start, pair.stop):
+                    nc.tensor.transpose(
+                        back[index][:, t - pair.start, b * P : (b + 1) * P], turned[b][:, t * P : (t + 1) * P], ident[:]
+                    )
+
         for index, pair in enumerate(pairs):
             nc.vector.scalar_tensor_tensor(
                 out=y_near[:, pair, :],

@@ -37,10 +37,10 @@ def tile_picked_ivfpq_none_po_kernel(
         xw = keep.tile([P, T], I32, name="xw", align_bytes=64)
         qn_sb = keep.tile([P, PACK], F32, name="qn_sb")
         ident = keep.tile([P, P], F32, name="ident")
-        placed = {"w1": keep.tile([P, V], U8, name="placed_w1", align_bytes=64)}
+        placed = {name: keep.tile([P, V], U8, name="placed_" + name, align_bytes=64) for name in ("w1", "w2")}
         stage = PACK * (N // 2) * 4
         raw_w1 = [
-            shared.tile([P, PACK, N // 2], F32, name="raw_w1_0", offset=stage, align_bytes=64),
+            shared.tile([P, PACK, N // 2], F32, name="raw_w1_0", offset=5 * stage, align_bytes=64),
             shared.tile([P, PACK, N // 2], F32, name="raw_w1_1", offset=2 * stage, align_bytes=64),
         ]
 
@@ -60,11 +60,12 @@ def tile_picked_ivfpq_none_po_kernel(
         load_weights(raw_w2[0], w2[:, : N // 2])
 
         make_identity(nc, ident[:])
-        nc.gpsimd.memset(placed["w1"][:].bitcast(I32), 0)
+        for name in ("w1", "w2"):
+            nc.vector.memset(placed[name][:].bitcast(I32), 0)
 
         picked = {
             "w1": keep.tile([P, V], U8, name="picked_w1", align_bytes=64),
-            "w2": keep.tile([P, S], U8, name="picked_w2", align_bytes=64),
+            "w2": shared.tile([P, S], U8, name="picked_w2", offset=5 * stage, align_bytes=64),
         }
         nc.vector.tensor_copy(picked["w1"][:], xs[:].indirect(cent_sb[:]))
         nc.vector.tensor_copy(picked["w2"][:], xs[:].indirect(offs_sb[:]))
@@ -114,16 +115,14 @@ def tile_picked_ivfpq_none_po_kernel(
             round_weights(nc.scalar.copy, "w1", raw_w1, half, slice(0, PACK))
         quantize_weights("w1", 0, PACK)
 
-        raw_w2.append(shared.tile([P, PACK, N // 2], F32, name="raw_w2_1", offset=stage, align_bytes=64))
+        raw_w2.append(shared.tile([P, PACK, N // 2], F32, name="raw_w2_1", offset=5 * stage + S, align_bytes=64))
         load_weights(raw_w2[1], w2[:, N // 2 :])
-        placed["w2"] = shared.tile([P, S], U8, name="placed_w2", offset=2 * stage, align_bytes=64)
         dn_sb = shared.tile([P, S], F32, name="dn_sb", offset=2 * stage + 512, align_bytes=64)
         far_at = [3 * stage, 3 * stage + stage // 2]
         dn_col = [
             shared.tile([P, 16], F32, name="dn_col_0", offset=far_at[1] - 32)[:, 0:1],
             shared.tile([P, 1], F32, name="dn_col_1", offset=2 * stage + 2624)[:],
         ]
-        nc.gpsimd.memset(placed["w2"][:].bitcast(I32), 0)
         place("w2")
         nc.sync.dma_start(out=dn_sb[:], in_=dn)
 
@@ -246,28 +245,28 @@ def tile_picked_ivfpq_none_po_kernel(
         def store_far(index):
             nc.sync.dma_start(out=out_rows[:, pairs[index], HALF:], in_=y_far[:, pairs[index], :])
 
-        def quantize_y(index):
+        def quantize_y(words, cols, values):
             nc.vector.quantize_mx(
-                out=y_words[:, halves[index]].bitcast(FP8X4),
-                scales=y_scales[:, halves[index]],
-                in_=rounded[index][:].rearrange("p c t -> p (c t)"),
+                out=words.bitcast(FP8X4), scales=y_scales[:, cols], in_=values.rearrange("p c t -> p (c t)")
             )
 
         add_far(0, slice(0, HALF))
         store_far(0)
-        rounded = [keep.tile([P, HALF, PACK], BF16, name="rounded_0", align_bytes=64)]
+        rounded = [keep.tile([P, HALF, PACK], BF16, name="rounded_0", tag="rounded", align_bytes=64)]
         add_far(1, slice(0, P))
         add_far(1, slice(P, HALF))
         store_far(1)
         rounded.append(shared.tile([P, HALF, PACK], BF16, name="rounded_1", offset=far_at[1] - 1024, align_bytes=64))
-        y_words = shared.tile([P, S], I32, name="y_words", offset=far_at[1] + 1024, align_bytes=64)
+        near_words = shared.tile([P, HALF], I32, name="near_words", offset=far_at[1] + 1024, align_bytes=64)
         round_y(nc.scalar.copy, rounded[0][:], y_near[:])
         round_y(nc.vector.tensor_copy, rounded[1][:, :P, :], y_far[:, :, :P])
         round_y(nc.scalar.copy, rounded[1][:, P:, :], y_far[:, :, P:])
-        quantize_y(0)
-        quantize_y(1)
-        nc.sync.dma_start(out=out_words[:, halves[0]], in_=y_words[:, halves[0]])
-        nc.scalar.dma_start(out=out_words[:, halves[1]], in_=y_words[:, halves[1]])
+        quantize_y(near_words[:], halves[0], rounded[0][:])
+        far_words = keep.tile([P, HALF], I32, name="far_words", tag="rounded", align_bytes=64)
+        for b, cols in enumerate(blocks):
+            quantize_y(far_words[:, b * P : (b + 1) * P], cols, rounded[1][:, b * P : (b + 1) * P, :])
+        nc.sync.dma_start(out=out_words[:, halves[0]], in_=near_words[:])
+        nc.scalar.dma_start(out=out_words[:, halves[1]], in_=far_words[:])
         for q in range(4):
             engine = nc.scalar if q % 2 else nc.sync
             engine.dma_start(

@@ -30,43 +30,43 @@ def tile_picked_ivfpq_none_po_kernel(
         shared = ctx.enter_context(tc.tile_pool(name="shared", bufs=1))
         psum = ctx.enter_context(tc.psum_pool(name="psum", bufs=1))
 
+        stage = PACK * (N // 2) * 4
         cent_sb = keep.tile([P, V // 16], U16, name="cent_sb")
         offs_sb = keep.tile([P, S // 16], U16, name="offs_sb")
         own_sb = keep.tile([P, S // 16], U16, name="own_sb")
-        xs = keep.tile([P, T], U8, name="xs", align_bytes=64)
+        xs = shared.tile([P, T], U8, name="xs", offset=stage - T // 2, align_bytes=64)
         xw = keep.tile([P, T], I32, name="xw", align_bytes=64)
         qn_sb = keep.tile([P, PACK], F32, name="qn_sb")
         ident = keep.tile([P, P], F32, name="ident")
         placed = {name: keep.tile([P, V], U8, name="placed_" + name, align_bytes=64) for name in ("w1", "w2")}
-        stage = PACK * (N // 2) * 4
-        raw_w1 = [
-            shared.tile([P, PACK, N // 2], F32, name="raw_w1_0", offset=5 * stage, align_bytes=64),
-            shared.tile([P, PACK, N // 2], F32, name="raw_w1_1", offset=2 * stage, align_bytes=64),
-        ]
+        picked = {
+            "w1": shared.tile([P, V], U8, name="picked_w1", offset=2 * stage, align_bytes=64),
+            "w2": keep.tile([P, S], U8, name="picked_w2", align_bytes=64),
+        }
+        raw = {"w1": [keep.tile([P, PACK, N // 2], F32, name="raw_w1_%d" % h, align_bytes=64) for h in range(2)]}
 
-        def load_weights(raw, columns):
-            nc.sync.dma_start(out=raw[:], in_=columns.rearrange("(p j) c -> p j c", j=PACK))
+        def load_weights(name, source, half):
+            columns = source[:, half * N // 2 : (half + 1) * N // 2]
+            nc.sync.dma_start(out=raw[name][half][:], in_=columns.rearrange("(p j) c -> p j c", j=PACK))
 
         nc.vector.memset(xs[:].bitcast(I32), 0)
-        load_weights(raw_w1[0], w1[:, : N // 2])
+        x_rows = x_words[0].rearrange("p n t -> p (n t)").bitcast(I32)
+        nc.sync.dma_start(out=xw[:, : T // 8], in_=x_rows[:, : T // 8])
         nc.sync.dma_start(cent_sb[:], cent)
         nc.sync.dma_start(offs_sb[:], offs)
-        nc.sync.dma_start(own_sb[:], own)
         nc.sync.dma_start(out=xs[0:P:8, :].bitcast(I32), in_=x_scales[0].bitcast(I32))
         nc.scalar.dma_start(out=qn_sb[:], in_=qn.rearrange("(p t) o -> p (t o)", t=PACK))
-        load_weights(raw_w1[1], w1[:, N // 2 :])
-        nc.sync.dma_start(out=xw[:], in_=x_words[0].rearrange("p n t -> p (n t)").bitcast(I32))
-        raw_w2 = [shared.tile([P, PACK, N // 2], F32, name="raw_w2_0", offset=0, align_bytes=64)]
-        load_weights(raw_w2[0], w2[:, : N // 2])
+        dn_four = keep.tile([P, PACK], F32, name="dn_four")
+        nc.scalar.dma_start(out=dn_four[:], in_=dn[0].rearrange("(p i) -> p i", i=PACK))
+        nc.sync.dma_start(out=xw[:, T // 8 :], in_=x_rows[:, T // 8 :])
+        for half in range(2):
+            load_weights("w1", w1, half)
+        nc.sync.dma_start(own_sb[:], own)
 
         make_identity(nc, ident[:])
         for name in ("w1", "w2"):
             nc.vector.memset(placed[name][:].bitcast(I32), 0)
 
-        picked = {
-            "w1": keep.tile([P, V], U8, name="picked_w1", align_bytes=64),
-            "w2": shared.tile([P, S], U8, name="picked_w2", offset=5 * stage, align_bytes=64),
-        }
         nc.vector.tensor_copy(picked["w1"][:], xs[:].indirect(cent_sb[:]))
         nc.vector.tensor_copy(picked["w2"][:], xs[:].indirect(offs_sb[:]))
 
@@ -78,25 +78,56 @@ def tile_picked_ivfpq_none_po_kernel(
 
         place("w1")
 
+        raw["w2"] = [
+            shared.tile([P, PACK, N // 2], F32, name="raw_w2_%d" % h, offset=h * stage, align_bytes=64) for h in range(2)
+        ]
+        for half in range(2):
+            load_weights("w2", w2, half)
+        place("w2")
+
+        spread_ps = psum.tile([P, PACK, P], F32, name="spread_ps", tag="bank_4")
+        dn_sb = keep.tile([P, HALF], F32, name="dn_sb")
+        dn_far = shared.tile([P, HALF], F32, name="dn_far", offset=4 * stage, align_bytes=64)
+        for i in range(PACK):
+            nc.tensor.transpose(spread_ps[:, i, :], dn_four[:, i : i + 1].to_broadcast([P, P]), ident[:])
+        for target, part in ((dn_far, slice(P // 2, P)), (dn_sb, slice(0, P // 2))):
+            nc.scalar.copy(
+                out=target[:].rearrange("m (p i) -> m p i", i=PACK), in_=spread_ps[:, :, part].rearrange("m i p -> m p i")
+            )
+        dn_ps = psum.tile([P, 2, P], F32, name="dn_ps", tag="bank_5")
+        dn_col = shared.tile([P, 2], F32, name="dn_col", offset=3 * stage)
+        for b in range(2):
+            nc.tensor.transpose(dn_ps[:, b, :], dn_far[:, b * P : (b + 1) * P], ident[:])
+        nc.scalar.copy(out=dn_col[:], in_=dn_ps[:, :, 0])
+
+        cent_words = keep.tile([P, V], U32, name="cent_words", align_bytes=64)
+        far_words = keep.tile([P, HALF], U32, name="far_words", align_bytes=64)
+        nc.vector.tensor_copy(cent_words[:], xw[:].bitcast(U32).indirect(cent_sb[:]))
+        nc.vector.tensor_copy(far_words[:], xw[:].bitcast(U32).indirect(offs_sb[:, HALF // 16 :]))
+
         grouped, codes, scales = {}, {}, {}
         grouped["w1"] = shared.tile([P, PACK, P, PACK], BF16, name="grouped_w1", offset=4 * stage, align_bytes=64)
-        grouped["w2"] = keep.tile([P, PACK, P, PACK], BF16, name="grouped", tag="grouped_w2", align_bytes=64)
+        grouped["w2"] = shared.tile([P, PACK, P, PACK], BF16, name="grouped_w2", offset=5 * stage, align_bytes=64)
         for name in ("w1", "w2"):
             codes[name] = keep.tile([P, N], U32, name="codes_" + name, align_bytes=64)
             scales[name] = keep.tile([P, N], U8, name="scales_" + name, align_bytes=64)
+        pairs = [slice(0, 2), slice(2, PACK)]
+        halves = [slice(0, HALF), slice(HALF, S)]
+        blocks = [slice(HALF, HALF + P), slice(HALF + P, S)]
 
-        def round_weights(copy, name, raw, half, deals):
+        def round_weights(copy, name, half, deals):
             rows = slice(half * P // 2, (half + 1) * P // 2)
             copy(
                 out=grouped[name][:, deals, rows, :].rearrange("p t m j -> p m j t"),
-                in_=raw[half][:].rearrange("p j (m t) -> p m j t", t=PACK)[:, :, :, deals],
+                in_=raw[name][half][:].rearrange("p j (m t) -> p m j t", t=PACK)[:, :, :, deals],
             )
 
-        def quantize_weights(name, first, last):
+        def quantize_weights(name, deals):
+            cols = slice(deals.start * P, deals.stop * P)
             nc.vector.quantize_mx(
-                out=codes[name][:, first * P : last * P].bitcast(FP8X4),
-                scales=scales[name][:, first * P : last * P],
-                in_=grouped[name][:, first:last, :, :].rearrange("p t m j -> p (t m j)"),
+                out=codes[name][:, cols].bitcast(FP8X4),
+                scales=scales[name][:, cols],
+                in_=grouped[name][:, deals, :, :].rearrange("p t m j -> p (t m j)"),
             )
 
         def product(acc, name, t, words, cols):
@@ -111,52 +142,29 @@ def tile_picked_ivfpq_none_po_kernel(
                 stop=True,
             )
 
-        for half in range(2):
-            round_weights(nc.scalar.copy, "w1", raw_w1, half, slice(0, PACK))
-        quantize_weights("w1", 0, PACK)
+        round_weights(nc.scalar.copy, "w1", 0, slice(0, PACK))
+        round_weights(nc.vector.tensor_copy, "w1", 1, pairs[0])
+        round_weights(nc.scalar.copy, "w1", 1, pairs[1])
+        for pair in pairs:
+            quantize_weights("w1", pair)
 
-        raw_w2.append(shared.tile([P, PACK, N // 2], F32, name="raw_w2_1", offset=5 * stage + S, align_bytes=64))
-        load_weights(raw_w2[1], w2[:, N // 2 :])
-        dn_sb = shared.tile([P, S], F32, name="dn_sb", offset=2 * stage + 512, align_bytes=64)
-        far_at = [3 * stage, 3 * stage + stage // 2]
-        dn_col = [
-            shared.tile([P, 16], F32, name="dn_col_0", offset=far_at[1] - 32)[:, 0:1],
-            shared.tile([P, 1], F32, name="dn_col_1", offset=2 * stage + 2624)[:],
-        ]
-        place("w2")
-        nc.sync.dma_start(out=dn_sb[:], in_=dn)
+        near_words = shared.tile([P, HALF], U32, name="near_words", offset=5 * stage - 4 * HALF, align_bytes=64)
+        nc.vector.tensor_copy(near_words[:], xw[:].bitcast(U32).indirect(offs_sb[:, : HALF // 16]))
 
-        cent_words = shared.tile([P, V], U32, name="cent_words", offset=4 * stage, align_bytes=64)
-        vec_words = shared.tile([P, S], U32, name="vec_words", offset=4 * stage + 4 * V, align_bytes=64)
-        halves = [slice(0, HALF), slice(HALF, S)]
-        nc.vector.tensor_copy(cent_words[:], xw[:].bitcast(U32).indirect(cent_sb[:]))
-        nc.vector.tensor_copy(vec_words[:], xw[:].bitcast(U32).indirect(offs_sb[:]))
-
-        round_weights(nc.scalar.copy, "w2", raw_w2, 0, slice(0, PACK))
         c_rows = []
         for t in range(PACK):
-            if t == 0:
-                c_t = shared.tile([P, V], F32, name="c_0", offset=0, align_bytes=64)
-            else:
-                c_t = keep.tile([P, V], F32, name="c_%d" % t)
+            c_t = keep.tile([P, V], F32, name="c_%d" % t)
             acc = psum.tile([P, V], F32, name="acc", tag="bank_%d" % t)
             product(acc[:], "w1", t, cent_words, slice(0, V))
             nc.scalar.activation(out=c_t[:], in_=acc[:], func=ACT.Identity, bias=qn_sb[:, t : t + 1], scale=-2.0)
             c_rows.append(c_t)
 
-        dn_ps = psum.tile([P, 2, P], F32, name="dn_ps", tag="bank_5")
-        for b in range(2):
-            nc.tensor.transpose(dn_ps[:, b, :], dn_sb[:, HALF + b * P : HALF + (b + 1) * P], ident[:])
-            nc.scalar.copy(out=dn_col[b], in_=dn_ps[:, b, 0:1])
-
-        pairs = [slice(0, 2), slice(2, PACK)]
+        round_weights(nc.vector.tensor_copy, "w2", 0, slice(0, PACK))
         for pair in pairs:
-            round_weights(nc.vector.tensor_copy, "w2", raw_w2, 1, pair)
+            round_weights(nc.vector.tensor_copy, "w2", 1, pair)
         for pair in pairs:
-            quantize_weights("w2", pair.start, pair.stop)
+            quantize_weights("w2", pair)
 
-        blocks = [slice(HALF, HALF + P), slice(HALF + P, S)]
-        turned = [keep.tile([P, N], F32, name="turned_0")]
         turned_banks = []
         for b, cols in enumerate(blocks):
             turned_ps = psum.tile([P, N], F32, name="turned_ps", tag="bank_%d" % (6 + b))
@@ -165,38 +173,37 @@ def tile_picked_ivfpq_none_po_kernel(
                 rows = slice(pair.start * P, pair.stop * P)
                 nc.tensor.matmul_mx(
                     out=turned_ps[:, rows],
-                    lhsT=vec_words[:, cols].bitcast(FP8X4),
+                    lhsT=far_words[:, b * P : (b + 1) * P].bitcast(FP8X4),
                     lhsT_scale=placed["w2"][:, cols],
                     rhs=codes["w2"][:, rows].bitcast(FP8X4),
                     rhs_scale=scales["w2"][:, rows],
                     start=True,
                     stop=True,
                 )
-        nc.scalar.activation(out=turned[0][:], in_=turned_banks[0][:], func=ACT.Identity, bias=dn_col[0], scale=-2.0)
         near_ps = []
         for index, pair in enumerate(pairs):
             acc = psum.tile([P, 2, HALF], F32, name="near_ps", tag="bank_%d" % (4 + index))
             for t in range(pair.start, pair.stop):
-                product(acc[:, t - pair.start, :], "w2", t, vec_words, slice(0, HALF))
+                product(acc[:, t - pair.start, :], "w2", t, near_words, slice(0, HALF))
             near_ps.append(acc)
+
         y_scales = keep.tile([P, S], U8, name="y_scales", align_bytes=64)
         out_rows = out_0.rearrange("(p t) j -> p t j", t=PACK)
         out_words = out_1[0].rearrange("p n t -> p (n t)").bitcast(I32)
-        fetched_near = keep.tile([P, PACK, HALF], F32, name="fetched_near", tag="grouped_w2", align_bytes=64)
+        fetched_near = shared.tile([P, PACK, HALF], F32, name="fetched_near", offset=5 * stage, align_bytes=64)
         fetched_far = [
-            shared.tile([P, 2, HALF], F32, name="fetched_far_%d" % index, offset=at, align_bytes=64)
-            for index, at in enumerate(far_at)
+            keep.tile([P, 2, HALF], F32, name="fetched_far_0"),
+            shared.tile([P, 2, HALF], F32, name="fetched_far_1", offset=3 * stage),
         ]
         y_near = keep.tile([P, PACK, HALF], F32, name="y_near")
+        y_far = keep.tile([P, PACK, HALF], F32, name="y_far")
 
         def offsets(cols):
             return own_sb[:, cols.start // 16 : cols.stop // 16]
 
-        def fetch_far(t, cols):
+        def fetch_far(t):
             nc.scalar.activation(
-                out=fetched_far[t // 2][:, t % 2, cols.start - HALF : cols.stop - HALF],
-                in_=c_rows[t][:].indirect(offsets(cols)),
-                func=ACT.Copy,
+                out=fetched_far[t // 2][:, t % 2, :], in_=c_rows[t][:].indirect(offsets(halves[1])), func=ACT.Copy
             )
 
         def round_y(copy, target, values):
@@ -206,11 +213,17 @@ def tile_picked_ivfpq_none_po_kernel(
             )
 
         for t in range(PACK):
-            nc.vector.tensor_tensor(fetched_near[:, t, :], c_rows[t][:].indirect(offsets(halves[0])), dn_sb[:, :HALF], ALU.add)
-        turned.append(shared.tile([P, N], F32, name="turned_1", offset=2 * stage - 512, align_bytes=64))
-        nc.vector.tensor_scalar(
-            out=turned[1][:], in0=turned_banks[1][:], scalar1=-2.0, scalar2=dn_col[1], op0=ALU.mult, op1=ALU.add
-        )
+            nc.vector.tensor_tensor(fetched_near[:, t, :], c_rows[t][:].indirect(offsets(halves[0])), dn_sb[:], ALU.add)
+        fetch_far(0)
+        fetch_far(1)
+        turned = []
+        for b in range(2):
+            turned.append(keep.tile([P, N], F32, name="turned_%d" % b))
+            nc.scalar.activation(
+                out=turned[b][:], in_=turned_banks[b][:], func=ACT.Identity, bias=dn_col[:, b : b + 1], scale=-2.0
+            )
+        fetch_far(2)
+        fetch_far(3)
         back = []
         for index, pair in enumerate(pairs):
             back.append(psum.tile([P, 2, HALF], F32, name="back", tag="bank_%d" % index))
@@ -230,43 +243,26 @@ def tile_picked_ivfpq_none_po_kernel(
                 op1=ALU.add,
             )
             nc.sync.dma_start(out=out_rows[:, pair, :HALF], in_=y_near[:, pair, :])
-        y_far = keep.tile([P, PACK, HALF], F32, name="y_far", tag="grouped_w2", align_bytes=64)
-        fetch_far(0, halves[1])
-        fetch_far(1, halves[1])
-        for cols in blocks:
-            fetch_far(2, cols)
-            fetch_far(3, cols)
+        for index, pair in enumerate(pairs):
+            nc.vector.tensor_tensor(y_far[:, pair, :], back[index][:], fetched_far[index][:], ALU.add)
+            nc.sync.dma_start(out=out_rows[:, pair, HALF:], in_=y_far[:, pair, :])
 
-        def add_far(index, part):
-            nc.vector.tensor_tensor(
-                y_far[:, pairs[index], part], back[index][:, :, part], fetched_far[index][:, :, part], ALU.add
-            )
-
-        def store_far(index):
-            nc.sync.dma_start(out=out_rows[:, pairs[index], HALF:], in_=y_far[:, pairs[index], :])
+        rounded = [keep.tile([P, HALF, PACK], BF16, name="rounded_%d" % h, align_bytes=64) for h in range(2)]
+        y_words = [keep.tile([P, HALF], I32, name="y_words_%d" % h, align_bytes=64) for h in range(2)]
+        round_y(nc.scalar.copy, rounded[0][:], y_near[:])
+        round_y(nc.vector.tensor_copy, rounded[1][:, :P, :], y_far[:, :, :P])
+        round_y(nc.scalar.copy, rounded[1][:, P:, :], y_far[:, :, P:])
 
         def quantize_y(words, cols, values):
             nc.vector.quantize_mx(
                 out=words.bitcast(FP8X4), scales=y_scales[:, cols], in_=values.rearrange("p c t -> p (c t)")
             )
 
-        add_far(0, slice(0, HALF))
-        store_far(0)
-        rounded = [keep.tile([P, HALF, PACK], BF16, name="rounded_0", tag="rounded", align_bytes=64)]
-        add_far(1, slice(0, P))
-        add_far(1, slice(P, HALF))
-        store_far(1)
-        rounded.append(shared.tile([P, HALF, PACK], BF16, name="rounded_1", offset=far_at[1] - 1024, align_bytes=64))
-        near_words = shared.tile([P, HALF], I32, name="near_words", offset=far_at[1] + 1024, align_bytes=64)
-        round_y(nc.scalar.copy, rounded[0][:], y_near[:])
-        round_y(nc.vector.tensor_copy, rounded[1][:, :P, :], y_far[:, :, :P])
-        round_y(nc.scalar.copy, rounded[1][:, P:, :], y_far[:, :, P:])
-        quantize_y(near_words[:], halves[0], rounded[0][:])
-        far_words = keep.tile([P, HALF], I32, name="far_words", tag="rounded", align_bytes=64)
+        quantize_y(y_words[0][:], halves[0], rounded[0][:])
         for b, cols in enumerate(blocks):
-            quantize_y(far_words[:, b * P : (b + 1) * P], cols, rounded[1][:, b * P : (b + 1) * P, :])
-        nc.sync.dma_start(out=out_words[:, halves[0]], in_=near_words[:])
-        nc.scalar.dma_start(out=out_words[:, halves[1]], in_=far_words[:])
+            quantize_y(y_words[1][:, b * P : (b + 1) * P], cols, rounded[1][:, b * P : (b + 1) * P, :])
+        nc.sync.dma_start(out=out_words[:, halves[0]], in_=y_words[0][:])
+        nc.scalar.dma_start(out=out_words[:, halves[1]], in_=y_words[1][:])
         for q in range(4):
             engine = nc.scalar if q % 2 else nc.sync
             engine.dma_start(

@@ -43,7 +43,12 @@ def tile_picked_ivfpq_none_po_kernel(
             "w1": shared.tile([P, V], U8, name="picked_w1", offset=2 * stage, align_bytes=64),
             "w2": keep.tile([P, S], U8, name="picked_w2", align_bytes=64),
         }
-        raw = {"w1": [keep.tile([P, PACK, N // 2], F32, name="raw_w1_%d" % h, align_bytes=64) for h in range(2)]}
+        raw = {
+            "w1": [
+                keep.tile([P, PACK, N // 2], F32, name="raw_w1_0", align_bytes=64),
+                shared.tile([P, PACK, N // 2], F32, name="raw_w1_1", offset=6 * stage, align_bytes=64),
+            ]
+        }
 
         def load_weights(name, source, half):
             columns = source[:, half * N // 2 : (half + 1) * N // 2]
@@ -55,12 +60,12 @@ def tile_picked_ivfpq_none_po_kernel(
         nc.sync.dma_start(cent_sb[:], cent)
         nc.sync.dma_start(offs_sb[:], offs)
         nc.sync.dma_start(out=xs[0:P:8, :].bitcast(I32), in_=x_scales[0].bitcast(I32))
-        nc.scalar.dma_start(out=qn_sb[:], in_=qn.rearrange("(p t) o -> p (t o)", t=PACK))
         dn_four = keep.tile([P, PACK], F32, name="dn_four")
         nc.scalar.dma_start(out=dn_four[:], in_=dn[0].rearrange("(p i) -> p i", i=PACK))
         nc.sync.dma_start(out=xw[:, T // 8 :], in_=x_rows[:, T // 8 :])
         for half in range(2):
             load_weights("w1", w1, half)
+        nc.sync.dma_start(out=qn_sb[:], in_=qn.rearrange("(p t) o -> p (t o)", t=PACK))
         nc.sync.dma_start(own_sb[:], own)
 
         make_identity(nc, ident[:])
@@ -145,10 +150,10 @@ def tile_picked_ivfpq_none_po_kernel(
         round_weights(nc.scalar.copy, "w1", 0, slice(0, PACK))
         round_weights(nc.vector.tensor_copy, "w1", 1, pairs[0])
         round_weights(nc.scalar.copy, "w1", 1, pairs[1])
-        for pair in pairs:
-            quantize_weights("w1", pair)
+        quantize_weights("w1", slice(0, 1))
+        quantize_weights("w1", slice(1, PACK))
 
-        near_words = shared.tile([P, HALF], U32, name="near_words", offset=5 * stage - 4 * HALF, align_bytes=64)
+        near_words = shared.tile([P, HALF], U32, name="near_words", offset=6 * stage, align_bytes=64)
         nc.vector.tensor_copy(near_words[:], xw[:].bitcast(U32).indirect(offs_sb[:, : HALF // 16]))
 
         c_rows = []
@@ -190,7 +195,7 @@ def tile_picked_ivfpq_none_po_kernel(
         y_scales = keep.tile([P, S], U8, name="y_scales", align_bytes=64)
         out_rows = out_0.rearrange("(p t) j -> p t j", t=PACK)
         out_words = out_1[0].rearrange("p n t -> p (n t)").bitcast(I32)
-        fetched_near = shared.tile([P, PACK, HALF], F32, name="fetched_near", offset=5 * stage, align_bytes=64)
+        fetched_near = shared.tile([P, PACK, HALF], F32, name="fetched_near", offset=stage, align_bytes=64)
         fetched_far = [
             keep.tile([P, 2, HALF], F32, name="fetched_far_0"),
             shared.tile([P, 2, HALF], F32, name="fetched_far_1", offset=3 * stage),

@@ -60,12 +60,12 @@ def tile_picked_ivfpq_none_po_kernel(
         nc.sync.dma_start(cent_sb[:], cent)
         nc.sync.dma_start(offs_sb[:], offs)
         nc.sync.dma_start(out=xs[0:P:8, :].bitcast(I32), in_=x_scales[0].bitcast(I32))
+        nc.scalar.dma_start(out=qn_sb[:], in_=qn.rearrange("(p t) o -> p (t o)", t=PACK))
         dn_four = keep.tile([P, PACK], F32, name="dn_four")
         nc.scalar.dma_start(out=dn_four[:], in_=dn[0].rearrange("(p i) -> p i", i=PACK))
         nc.sync.dma_start(out=xw[:, T // 8 :], in_=x_rows[:, T // 8 :])
         for half in range(2):
             load_weights("w1", w1, half)
-        nc.sync.dma_start(out=qn_sb[:], in_=qn.rearrange("(p t) o -> p (t o)", t=PACK))
         nc.sync.dma_start(own_sb[:], own)
 
         make_identity(nc, ident[:])

@@ -100,10 +100,11 @@ def tile_picked_ivfpq_none_po_kernel(
                 out=target[:].rearrange("m (p i) -> m p i", i=PACK), in_=spread_ps[:, :, part].rearrange("m i p -> m p i")
             )
         dn_ps = psum.tile([P, 2, P], F32, name="dn_ps", tag="bank_5")
-        dn_col = shared.tile([P, 2], F32, name="dn_col", offset=3 * stage)
+        dn_col = [shared.tile([P, 1], F32, name="dn_col_0", offset=3 * stage), keep.tile([P, 1], F32, name="dn_col_1")]
         for b in range(2):
             nc.tensor.transpose(dn_ps[:, b, :], dn_far[:, b * P : (b + 1) * P], ident[:])
-        nc.scalar.copy(out=dn_col[:], in_=dn_ps[:, :, 0])
+        for b in range(2):
+            nc.scalar.copy(out=dn_col[b][:], in_=dn_ps[:, b, 0:1])
 
         cent_words = keep.tile([P, V], U32, name="cent_words", align_bytes=64)
         far_words = keep.tile([P, HALF], U32, name="far_words", align_bytes=64)
@@ -225,7 +226,7 @@ def tile_picked_ivfpq_none_po_kernel(
         for b in range(2):
             turned.append(keep.tile([P, N], F32, name="turned_%d" % b))
             nc.scalar.activation(
-                out=turned[b][:], in_=turned_banks[b][:], func=ACT.Identity, bias=dn_col[:, b : b + 1], scale=-2.0
+                out=turned[b][:], in_=turned_banks[b][:], func=ACT.Identity, bias=dn_col[b][:], scale=-2.0
             )
         fetch_far(2)
         fetch_far(3)
@@ -253,7 +254,10 @@ def tile_picked_ivfpq_none_po_kernel(
             nc.sync.dma_start(out=out_rows[:, pair, HALF:], in_=y_far[:, pair, :])
 
         rounded = [keep.tile([P, HALF, PACK], BF16, name="rounded_%d" % h, align_bytes=64) for h in range(2)]
-        y_words = [keep.tile([P, HALF], I32, name="y_words_%d" % h, align_bytes=64) for h in range(2)]
+        y_words = [
+            shared.tile([P, HALF], I32, name="y_words_0", offset=3 * stage, align_bytes=64),
+            keep.tile([P, HALF], I32, name="y_words_1", align_bytes=64),
+        ]
         round_y(nc.scalar.copy, rounded[0][:], y_near[:])
         round_y(nc.vector.tensor_copy, rounded[1][:, :P, :], y_far[:, :, :P])
         round_y(nc.scalar.copy, rounded[1][:, P:, :], y_far[:, :, P:])

@@ -250,7 +250,10 @@ def tile_picked_ivfpq_none_po_kernel(
             )
             nc.sync.dma_start(out=out_rows[:, pair, :HALF], in_=y_near[:, pair, :])
         for index, pair in enumerate(pairs):
-            nc.vector.tensor_tensor(y_far[:, pair, :], back[index][:], fetched_far[index][:], ALU.add)
+            for part in [slice(0, HALF)] if index == 0 else [slice(0, P), slice(P, HALF)]:
+                nc.vector.tensor_tensor(
+                    y_far[:, pair, part], back[index][:, :, part], fetched_far[index][:, :, part], ALU.add
+                )
             nc.sync.dma_start(out=out_rows[:, pair, HALF:], in_=y_far[:, pair, :])
 
         rounded = [keep.tile([P, HALF, PACK], BF16, name="rounded_%d" % h, align_bytes=64) for h in range(2)]
@@ -259,8 +262,10 @@ def tile_picked_ivfpq_none_po_kernel(
             keep.tile([P, HALF], I32, name="y_words_1", align_bytes=64),
         ]
         round_y(nc.scalar.copy, rounded[0][:], y_near[:])
+        cut = 3 * HALF // 4
         round_y(nc.vector.tensor_copy, rounded[1][:, :P, :], y_far[:, :, :P])
-        round_y(nc.scalar.copy, rounded[1][:, P:, :], y_far[:, :, P:])
+        round_y(nc.vector.tensor_copy, rounded[1][:, P:cut, :], y_far[:, :, P:cut])
+        round_y(nc.scalar.copy, rounded[1][:, cut:, :], y_far[:, :, cut:])
 
         def quantize_y(words, cols, values):
             nc.vector.quantize_mx(
@@ -268,8 +273,7 @@ def tile_picked_ivfpq_none_po_kernel(
             )
 
         quantize_y(y_words[0][:], halves[0], rounded[0][:])
-        for b, cols in enumerate(blocks):
-            quantize_y(y_words[1][:, b * P : (b + 1) * P], cols, rounded[1][:, b * P : (b + 1) * P, :])
+        quantize_y(y_words[1][:], halves[1], rounded[1][:])
         nc.sync.dma_start(out=out_words[:, halves[0]], in_=y_words[0][:])
         nc.scalar.dma_start(out=out_words[:, halves[1]], in_=y_words[1][:])
         for q in range(4):

@@ -257,10 +257,7 @@ def tile_picked_ivfpq_none_po_kernel(
             nc.sync.dma_start(out=out_rows[:, pair, HALF:], in_=y_far[:, pair, :])
 
         rounded = [keep.tile([P, HALF, PACK], BF16, name="rounded_%d" % h, align_bytes=64) for h in range(2)]
-        y_words = [
-            shared.tile([P, HALF], I32, name="y_words_0", offset=3 * stage, align_bytes=64),
-            keep.tile([P, HALF], I32, name="y_words_1", align_bytes=64),
-        ]
+        y_words = shared.tile([P, S], I32, name="y_words", offset=3 * stage, align_bytes=64)
         round_y(nc.scalar.copy, rounded[0][:], y_near[:])
         cut = 3 * HALF // 4
         round_y(nc.vector.tensor_copy, rounded[1][:, :P, :], y_far[:, :, :P])
@@ -272,10 +269,9 @@ def tile_picked_ivfpq_none_po_kernel(
                 out=words.bitcast(FP8X4), scales=y_scales[:, cols], in_=values.rearrange("p c t -> p (c t)")
             )
 
-        quantize_y(y_words[0][:], halves[0], rounded[0][:])
-        quantize_y(y_words[1][:], halves[1], rounded[1][:])
-        nc.sync.dma_start(out=out_words[:, halves[0]], in_=y_words[0][:])
-        nc.scalar.dma_start(out=out_words[:, halves[1]], in_=y_words[1][:])
+        quantize_y(y_words[:, halves[0]], halves[0], rounded[0][:])
+        quantize_y(y_words[:, halves[1]], halves[1], rounded[1][:])
+        nc.sync.dma_start(out=out_words, in_=y_words[:])
         for q in range(4):
             engine = nc.scalar if q % 2 else nc.sync
             engine.dma_start(

@@ -81,13 +81,13 @@ def tile_picked_ivfpq_none_po_kernel(
                     out=placed[name][r:P:32, :].bitcast(I32), in_=picked[name][8 * r : P : 32, :].bitcast(I32)
                 )
 
-        place("w1")
-
         raw["w2"] = [
-            shared.tile([P, PACK, N // 2], F32, name="raw_w2_%d" % h, offset=h * stage, align_bytes=64) for h in range(2)
+            keep.tile([P, PACK, N // 2], F32, name="raw_w2_0", align_bytes=64),
+            shared.tile([P, PACK, N // 2], F32, name="raw_w2_1", offset=stage, align_bytes=64),
         ]
-        for half in range(2):
-            load_weights("w2", w2, half)
+        load_weights("w2", w2, 0)
+        place("w1")
+        load_weights("w2", w2, 1)
         place("w2")
 
         spread_ps = psum.tile([P, PACK, P], F32, name="spread_ps", tag="bank_4")
@@ -113,7 +113,6 @@ def tile_picked_ivfpq_none_po_kernel(
 
         grouped, codes, scales = {}, {}, {}
         grouped["w1"] = shared.tile([P, PACK, P, PACK], BF16, name="grouped_w1", offset=4 * stage, align_bytes=64)
-        grouped["w2"] = shared.tile([P, PACK, P, PACK], BF16, name="grouped_w2", offset=5 * stage, align_bytes=64)
         for name in ("w1", "w2"):
             codes[name] = keep.tile([P, N], U32, name="codes_" + name, align_bytes=64)
             scales[name] = keep.tile([P, N], U8, name="scales_" + name, align_bytes=64)
@@ -157,6 +156,10 @@ def tile_picked_ivfpq_none_po_kernel(
         near_words = shared.tile([P, HALF], U32, name="near_words", offset=6 * stage, align_bytes=64)
         nc.vector.tensor_copy(near_words[:], xw[:].bitcast(U32).indirect(offs_sb[:, : HALF // 16]))
 
+        grouped["w2"] = shared.tile([P, PACK, P, PACK], BF16, name="grouped_w2", offset=6 * stage + 4 * HALF, align_bytes=64)
+        round_weights(nc.scalar.copy, "w2", 0, pairs[0])
+        round_weights(nc.vector.tensor_copy, "w2", 0, pairs[1])
+
         c_rows = []
         for t in range(PACK):
             c_t = keep.tile([P, V], F32, name="c_%d" % t)
@@ -165,7 +168,6 @@ def tile_picked_ivfpq_none_po_kernel(
             nc.scalar.activation(out=c_t[:], in_=acc[:], func=ACT.Identity, bias=qn_sb[:, t : t + 1], scale=-2.0)
             c_rows.append(c_t)
 
-        round_weights(nc.vector.tensor_copy, "w2", 0, slice(0, PACK))
         for pair in pairs:
             round_weights(nc.vector.tensor_copy, "w2", 1, pair)
         for pair in pairs:

@@ -45,7 +45,7 @@ def tile_picked_ivfpq_none_po_kernel(
         }
         raw = {
             "w1": [
-                keep.tile([P, PACK, N // 2], F32, name="raw_w1_0", align_bytes=64),
+                shared.tile([P, PACK, N // 2], F32, name="raw_w1_0", offset=5 * stage, align_bytes=64),
                 shared.tile([P, PACK, N // 2], F32, name="raw_w1_1", offset=6 * stage, align_bytes=64),
             ]
         }
@@ -150,11 +150,10 @@ def tile_picked_ivfpq_none_po_kernel(
         round_weights(nc.scalar.copy, "w1", 0, slice(0, PACK))
         round_weights(nc.vector.tensor_copy, "w1", 1, pairs[0])
         round_weights(nc.scalar.copy, "w1", 1, pairs[1])
+        near_words = shared.tile([P, HALF], U32, name="near_words", offset=5 * stage, align_bytes=64)
+        nc.vector.tensor_copy(near_words[:], xw[:].bitcast(U32).indirect(offs_sb[:, : HALF // 16]))
         quantize_weights("w1", slice(0, 1))
         quantize_weights("w1", slice(1, PACK))
-
-        near_words = shared.tile([P, HALF], U32, name="near_words", offset=6 * stage, align_bytes=64)
-        nc.vector.tensor_copy(near_words[:], xw[:].bitcast(U32).indirect(offs_sb[:, : HALF // 16]))
 
         grouped["w2"] = shared.tile([P, PACK, P, PACK], BF16, name="grouped_w2", offset=6 * stage + 4 * HALF, align_bytes=64)
         round_weights(nc.scalar.copy, "w2", 0, pairs[0])

@@ -66,7 +66,6 @@ def tile_picked_ivfpq_none_po_kernel(
         nc.sync.dma_start(out=xw[:, T // 8 :], in_=x_rows[:, T // 8 :])
         for half in range(2):
             load_weights("w1", w1, half)
-        nc.sync.dma_start(own_sb[:], own)
 
         make_identity(nc, ident[:])
         for name in ("w1", "w2"):
@@ -88,6 +87,7 @@ def tile_picked_ivfpq_none_po_kernel(
         load_weights("w2", w2, 0)
         place("w1")
         load_weights("w2", w2, 1)
+        nc.sync.dma_start(own_sb[:], own)
         place("w2")
 
         spread_ps = psum.tile([P, PACK, P], F32, name="spread_ps", tag="bank_4")
@@ -155,9 +155,31 @@ def tile_picked_ivfpq_none_po_kernel(
         quantize_weights("w1", slice(0, 1))
         quantize_weights("w1", slice(1, PACK))
 
-        grouped["w2"] = shared.tile([P, PACK, P, PACK], BF16, name="grouped_w2", offset=6 * stage + 4 * HALF, align_bytes=64)
-        round_weights(nc.scalar.copy, "w2", 0, pairs[0])
-        round_weights(nc.vector.tensor_copy, "w2", 0, pairs[1])
+        def prepare_w2(half, copies):
+            rounded_w2 = []
+            for index, pair in enumerate(pairs):
+                rounded_w2.append(
+                    shared.tile(
+                        [P, 2, P // 2, PACK],
+                        BF16,
+                        name="rounded_w2_%d_%d" % (half, index),
+                        offset=6 * stage + index * stage // 4,
+                        align_bytes=64,
+                    )
+                )
+                copies[index](
+                    out=rounded_w2[index][:].rearrange("p t m j -> p m j t"),
+                    in_=raw["w2"][half][:].rearrange("p j (m t) -> p m j t", t=PACK)[:, :, :, pair],
+                )
+            for t in range(PACK):
+                cols = slice(t * P + half * P // 2, t * P + (half + 1) * P // 2)
+                nc.vector.quantize_mx(
+                    out=codes["w2"][:, cols].bitcast(FP8X4),
+                    scales=scales["w2"][:, cols],
+                    in_=rounded_w2[t // 2][:, t % 2].rearrange("p m j -> p (m j)"),
+                )
+
+        prepare_w2(0, [nc.scalar.copy, nc.vector.tensor_copy])
 
         c_rows = []
         for t in range(PACK):
@@ -167,10 +189,7 @@ def tile_picked_ivfpq_none_po_kernel(
             nc.scalar.activation(out=c_t[:], in_=acc[:], func=ACT.Identity, bias=qn_sb[:, t : t + 1], scale=-2.0)
             c_rows.append(c_t)
 
-        for pair in pairs:
-            round_weights(nc.vector.tensor_copy, "w2", 1, pair)
-        for pair in pairs:
-            quantize_weights("w2", pair)
+        prepare_w2(1, [nc.vector.tensor_copy, nc.vector.tensor_copy])
 
         turned_banks = []
         for b, cols in enumerate(blocks):

@@ -106,6 +106,9 @@ def tile_picked_ivfpq_none_po_kernel(
         for b in range(2):
             nc.scalar.copy(out=dn_col[b][:], in_=dn_ps[:, b, 0:1])
 
+        qn_first = shared.tile([P, 1], F32, name="qn_first", offset=7 * stage)
+        nc.scalar.copy(out=qn_first[:], in_=qn_sb[:, 0:1])
+
         cent_words = keep.tile([P, V], U32, name="cent_words", align_bytes=64)
         far_words = keep.tile([P, HALF], U32, name="far_words", align_bytes=64)
         nc.vector.tensor_copy(cent_words[:], xw[:].bitcast(U32).indirect(cent_sb[:]))
@@ -155,41 +158,51 @@ def tile_picked_ivfpq_none_po_kernel(
         quantize_weights("w1", slice(0, 1))
         quantize_weights("w1", slice(1, PACK))
 
-        def prepare_w2(half, copies):
-            rounded_w2 = []
-            for index, pair in enumerate(pairs):
-                rounded_w2.append(
-                    shared.tile(
-                        [P, 2, P // 2, PACK],
-                        BF16,
-                        name="rounded_w2_%d_%d" % (half, index),
-                        offset=6 * stage + index * stage // 4,
-                        align_bytes=64,
-                    )
-                )
-                copies[index](
-                    out=rounded_w2[index][:].rearrange("p t m j -> p m j t"),
+        def round_w2(half, copies):
+            rounded_w2 = shared.tile(
+                [P, PACK, P // 2, PACK], BF16, name="rounded_w2_%d" % half, offset=(6 + half) * stage, align_bytes=64
+            )
+            for copy, pair in zip(copies, pairs):
+                copy(
+                    out=rounded_w2[:, pair].rearrange("p t m j -> p m j t"),
                     in_=raw["w2"][half][:].rearrange("p j (m t) -> p m j t", t=PACK)[:, :, :, pair],
                 )
+            return rounded_w2
+
+        def quantize_w2(half, rounded_w2):
             for t in range(PACK):
                 cols = slice(t * P + half * P // 2, t * P + (half + 1) * P // 2)
                 nc.vector.quantize_mx(
                     out=codes["w2"][:, cols].bitcast(FP8X4),
                     scales=scales["w2"][:, cols],
-                    in_=rounded_w2[t // 2][:, t % 2].rearrange("p m j -> p (m j)"),
+                    in_=rounded_w2[:, t].rearrange("p m j -> p (m j)"),
                 )
 
-        prepare_w2(0, [nc.scalar.copy, nc.vector.tensor_copy])
+        quantize_w2(0, round_w2(0, [nc.scalar.copy, nc.vector.tensor_copy]))
 
         c_rows = []
         for t in range(PACK):
             c_t = keep.tile([P, V], F32, name="c_%d" % t)
-            acc = psum.tile([P, V], F32, name="acc", tag="bank_%d" % t)
-            product(acc[:], "w1", t, cent_words, slice(0, V))
-            nc.scalar.activation(out=c_t[:], in_=acc[:], func=ACT.Identity, bias=qn_sb[:, t : t + 1], scale=-2.0)
+            parts = [(slice(0, V), t, qn_sb[:, t : t + 1])]
+            if t == 0:
+                parts = [(slice(0, V // 2), 0, qn_first[:]), (slice(V // 2, V), 6, qn_sb[:, 0:1])]
+            for cols, bank, norm in parts:
+                acc = psum.tile([P, cols.stop - cols.start], F32, name="acc", tag="bank_%d" % bank)
+                product(acc[:], "w1", t, cent_words, cols)
+                nc.scalar.activation(out=c_t[:, cols], in_=acc[:], func=ACT.Identity, bias=norm, scale=-2.0)
             c_rows.append(c_t)
 
-        prepare_w2(1, [nc.vector.tensor_copy, nc.vector.tensor_copy])
+        def offsets(cols):
+            return own_sb[:, cols.start // 16 : cols.stop // 16]
+
+        fetched_near = keep.tile([P, PACK, HALF], F32, name="fetched_near")
+
+        def fetch_near(t):
+            nc.vector.tensor_tensor(fetched_near[:, t, :], c_rows[t][:].indirect(offsets(halves[0])), dn_sb[:], ALU.add)
+
+        last_rounded = round_w2(1, [nc.vector.tensor_copy, nc.vector.tensor_copy])
+        fetch_near(0)
+        quantize_w2(1, last_rounded)
 
         turned_banks = []
         for b, cols in enumerate(blocks):
@@ -216,16 +229,12 @@ def tile_picked_ivfpq_none_po_kernel(
         y_scales = keep.tile([P, S], U8, name="y_scales", align_bytes=64)
         out_rows = out_0.rearrange("(p t) j -> p t j", t=PACK)
         out_words = out_1[0].rearrange("p n t -> p (n t)").bitcast(I32)
-        fetched_near = shared.tile([P, PACK, HALF], F32, name="fetched_near", offset=stage, align_bytes=64)
         fetched_far = [
             keep.tile([P, 2, HALF], F32, name="fetched_far_0"),
             shared.tile([P, 2, HALF], F32, name="fetched_far_1", offset=3 * stage),
         ]
         y_near = keep.tile([P, PACK, HALF], F32, name="y_near")
         y_far = keep.tile([P, PACK, HALF], F32, name="y_far")
-
-        def offsets(cols):
-            return own_sb[:, cols.start // 16 : cols.stop // 16]
 
         def fetch_far(t):
             nc.scalar.activation(
@@ -238,8 +247,8 @@ def tile_picked_ivfpq_none_po_kernel(
                 in_=values.rearrange("p t (c i) -> p c t i", i=4),
             )
 
-        for t in range(PACK):
-            nc.vector.tensor_tensor(fetched_near[:, t, :], c_rows[t][:].indirect(offsets(halves[0])), dn_sb[:], ALU.add)
+        for t in range(1, PACK):
+            fetch_near(t)
         fetch_far(0)
         fetch_far(1)
         turned = []

@@ -19,6 +19,7 @@ ACT = mybir.ActivationFunctionType
 P = 128
 PACK = 4
 HALF = S // 2
+APART = 32 * 1024
 
 
 def tile_picked_ivfpq_none_po_kernel(
@@ -28,6 +29,7 @@ def tile_picked_ivfpq_none_po_kernel(
     with ExitStack() as ctx:
         keep = ctx.enter_context(tc.tile_pool(name="keep", bufs=1))
         shared = ctx.enter_context(tc.tile_pool(name="shared", bufs=1))
+        windows = ctx.enter_context(tc.tile_pool(name="windows", bufs=1))
         psum = ctx.enter_context(tc.psum_pool(name="psum", bufs=1))
 
         stage = PACK * (N // 2) * 4
@@ -35,7 +37,7 @@ def tile_picked_ivfpq_none_po_kernel(
         offs_sb = keep.tile([P, S // 16], U16, name="offs_sb")
         own_sb = keep.tile([P, S // 16], U16, name="own_sb")
         xs = shared.tile([P, T], U8, name="xs", offset=stage - T // 2, align_bytes=64)
-        xw = keep.tile([P, T], I32, name="xw", align_bytes=64)
+        xw = windows.tile([P, T], I32, name="xw", offset=APART, align_bytes=64)
         qn_sb = keep.tile([P, PACK], F32, name="qn_sb")
         ident = keep.tile([P, P], F32, name="ident")
         placed = {name: keep.tile([P, V], U8, name="placed_" + name, align_bytes=64) for name in ("w1", "w2")}
@@ -182,7 +184,7 @@ def tile_picked_ivfpq_none_po_kernel(
 
         c_rows = []
         for t in range(PACK):
-            c_t = keep.tile([P, V], F32, name="c_%d" % t)
+            c_t = windows.tile([P, V], F32, name="c_%d" % t, offset=APART * (t + 1) + 4 * T, align_bytes=64)
             parts = [(slice(0, V), t, qn_sb[:, t : t + 1])]
             if t == 0:
                 parts = [(slice(0, V // 2), 0, qn_first[:]), (slice(V // 2, V), 6, qn_sb[:, 0:1])]

@@ -19,7 +19,6 @@ ACT = mybir.ActivationFunctionType
 P = 128
 PACK = 4
 HALF = S // 2
-APART = 32 * 1024
 
 
 def tile_picked_ivfpq_none_po_kernel(
@@ -29,7 +28,6 @@ def tile_picked_ivfpq_none_po_kernel(
     with ExitStack() as ctx:
         keep = ctx.enter_context(tc.tile_pool(name="keep", bufs=1))
         shared = ctx.enter_context(tc.tile_pool(name="shared", bufs=1))
-        windows = ctx.enter_context(tc.tile_pool(name="windows", bufs=1))
         psum = ctx.enter_context(tc.psum_pool(name="psum", bufs=1))
 
         stage = PACK * (N // 2) * 4
@@ -37,7 +35,7 @@ def tile_picked_ivfpq_none_po_kernel(
         offs_sb = keep.tile([P, S // 16], U16, name="offs_sb")
         own_sb = keep.tile([P, S // 16], U16, name="own_sb")
         xs = shared.tile([P, T], U8, name="xs", offset=stage - T // 2, align_bytes=64)
-        xw = windows.tile([P, T], I32, name="xw", offset=APART, align_bytes=64)
+        xw = keep.tile([P, T], I32, name="xw", align_bytes=64)
         qn_sb = keep.tile([P, PACK], F32, name="qn_sb")
         ident = keep.tile([P, P], F32, name="ident")
         placed = {name: keep.tile([P, V], U8, name="placed_" + name, align_bytes=64) for name in ("w1", "w2")}
@@ -86,8 +84,8 @@ def tile_picked_ivfpq_none_po_kernel(
             keep.tile([P, PACK, N // 2], F32, name="raw_w2_0", align_bytes=64),
             shared.tile([P, PACK, N // 2], F32, name="raw_w2_1", offset=stage, align_bytes=64),
         ]
-        load_weights("w2", w2, 0)
         place("w1")
+        load_weights("w2", w2, 0)
         load_weights("w2", w2, 1)
         nc.sync.dma_start(own_sb[:], own)
         place("w2")
@@ -108,9 +106,6 @@ def tile_picked_ivfpq_none_po_kernel(
         for b in range(2):
             nc.scalar.copy(out=dn_col[b][:], in_=dn_ps[:, b, 0:1])
 
-        qn_first = shared.tile([P, 1], F32, name="qn_first", offset=7 * stage)
-        nc.scalar.copy(out=qn_first[:], in_=qn_sb[:, 0:1])
-
         cent_words = keep.tile([P, V], U32, name="cent_words", align_bytes=64)
         far_words = keep.tile([P, HALF], U32, name="far_words", align_bytes=64)
         nc.vector.tensor_copy(cent_words[:], xw[:].bitcast(U32).indirect(cent_sb[:]))
@@ -125,11 +120,11 @@ def tile_picked_ivfpq_none_po_kernel(
         halves = [slice(0, HALF), slice(HALF, S)]
         blocks = [slice(HALF, HALF + P), slice(HALF + P, S)]
 
-        def round_weights(copy, name, half, deals):
-            rows = slice(half * P // 2, (half + 1) * P // 2)
+        def round_weights(copy, name, half, deals, rows):
+            placed_rows = slice(half * P // 2 + rows.start, half * P // 2 + rows.stop)
             copy(
-                out=grouped[name][:, deals, rows, :].rearrange("p t m j -> p m j t"),
-                in_=raw[name][half][:].rearrange("p j (m t) -> p m j t", t=PACK)[:, :, :, deals],
+                out=grouped[name][:, deals, placed_rows, :].rearrange("p t m j -> p m j t"),
+                in_=raw[name][half][:].rearrange("p j (m t) -> p m j t", t=PACK)[:, rows, :, deals],
             )
 
         def quantize_weights(name, deals):
@@ -152,27 +147,29 @@ def tile_picked_ivfpq_none_po_kernel(
                 stop=True,
             )
 
-        round_weights(nc.scalar.copy, "w1", 0, slice(0, PACK))
-        round_weights(nc.vector.tensor_copy, "w1", 1, pairs[0])
-        round_weights(nc.scalar.copy, "w1", 1, pairs[1])
-        near_words = shared.tile([P, HALF], U32, name="near_words", offset=5 * stage, align_bytes=64)
-        nc.vector.tensor_copy(near_words[:], xw[:].bitcast(U32).indirect(offs_sb[:, : HALF // 16]))
+        all_rows, low_rows, high_rows = slice(0, P // 2), slice(0, P // 4), slice(P // 4, P // 2)
+        round_weights(nc.scalar.copy, "w1", 0, slice(0, PACK), all_rows)
+        for pair in pairs:
+            round_weights(nc.vector.tensor_copy, "w1", 1, pair, low_rows)
+            round_weights(nc.scalar.copy, "w1", 1, pair, high_rows)
         quantize_weights("w1", slice(0, 1))
         quantize_weights("w1", slice(1, PACK))
+        near_words = shared.tile([P, HALF], U32, name="near_words", offset=6 * stage + stage // 2, align_bytes=64)
+        nc.vector.tensor_copy(near_words[:], xw[:].bitcast(U32).indirect(offs_sb[:, : HALF // 16]))
 
-        def round_w2(half, copies):
+        def round_w2(half, shares):
             rounded_w2 = shared.tile(
                 [P, PACK, P // 2, PACK], BF16, name="rounded_w2_%d" % half, offset=(6 + half) * stage, align_bytes=64
             )
-            for copy, pair in zip(copies, pairs):
+            for copy, deals, rows in shares:
                 copy(
-                    out=rounded_w2[:, pair].rearrange("p t m j -> p m j t"),
-                    in_=raw["w2"][half][:].rearrange("p j (m t) -> p m j t", t=PACK)[:, :, :, pair],
+                    out=rounded_w2[:, deals, rows].rearrange("p t m j -> p m j t"),
+                    in_=raw["w2"][half][:].rearrange("p j (m t) -> p m j t", t=PACK)[:, rows, :, deals],
                 )
             return rounded_w2
 
-        def quantize_w2(half, rounded_w2):
-            for t in range(PACK):
+        def quantize_w2(half, rounded_w2, deals):
+            for t in deals:
                 cols = slice(t * P + half * P // 2, t * P + (half + 1) * P // 2)
                 nc.vector.quantize_mx(
                     out=codes["w2"][:, cols].bitcast(FP8X4),
@@ -180,14 +177,18 @@ def tile_picked_ivfpq_none_po_kernel(
                     in_=rounded_w2[:, t].rearrange("p m j -> p (m j)"),
                 )
 
-        quantize_w2(0, round_w2(0, [nc.scalar.copy, nc.vector.tensor_copy]))
+        first_shares = [
+            (nc.vector.tensor_copy, pairs[0], all_rows),
+            (nc.vector.tensor_copy, pairs[1], all_rows),
+        ]
+        quantize_w2(0, round_w2(0, first_shares), range(PACK))
 
         c_rows = []
         for t in range(PACK):
-            c_t = windows.tile([P, V], F32, name="c_%d" % t, offset=APART * (t + 1) + 4 * T, align_bytes=64)
+            c_t = keep.tile([P, V], F32, name="c_%d" % t, align_bytes=64)
             parts = [(slice(0, V), t, qn_sb[:, t : t + 1])]
             if t == 0:
-                parts = [(slice(0, V // 2), 0, qn_first[:]), (slice(V // 2, V), 6, qn_sb[:, 0:1])]
+                parts = [(slice(0, V // 2), 0, qn_sb[:, 0:1]), (slice(V // 2, V), 6, qn_sb[:, 0:1])]
             for cols, bank, norm in parts:
                 acc = psum.tile([P, cols.stop - cols.start], F32, name="acc", tag="bank_%d" % bank)
                 product(acc[:], "w1", t, cent_words, cols)
@@ -202,9 +203,9 @@ def tile_picked_ivfpq_none_po_kernel(
         def fetch_near(t):
             nc.vector.tensor_tensor(fetched_near[:, t, :], c_rows[t][:].indirect(offsets(halves[0])), dn_sb[:], ALU.add)
 
-        last_rounded = round_w2(1, [nc.vector.tensor_copy, nc.vector.tensor_copy])
+        last_rounded = round_w2(1, [(nc.vector.tensor_copy, pair, all_rows) for pair in pairs])
         fetch_near(0)
-        quantize_w2(1, last_rounded)
+        quantize_w2(1, last_rounded, range(PACK))
 
         turned_banks = []
         for b, cols in enumerate(blocks):

@@ -19,6 +19,7 @@ ACT = mybir.ActivationFunctionType
 P = 128
 PACK = 4
 HALF = S // 2
+LINE = 256
 
 
 def tile_picked_ivfpq_none_po_kernel(
@@ -34,19 +35,19 @@ def tile_picked_ivfpq_none_po_kernel(
         cent_sb = keep.tile([P, V // 16], U16, name="cent_sb")
         offs_sb = keep.tile([P, S // 16], U16, name="offs_sb")
         own_sb = keep.tile([P, S // 16], U16, name="own_sb")
-        xs = shared.tile([P, T], U8, name="xs", offset=stage - T // 2, align_bytes=64)
-        xw = keep.tile([P, T], I32, name="xw", align_bytes=64)
+        xs = shared.tile([P, T], U8, name="xs", offset=stage - T // 2, align_bytes=LINE)
+        xw = keep.tile([P, T], I32, name="xw", align_bytes=LINE)
         qn_sb = keep.tile([P, PACK], F32, name="qn_sb")
-        ident = keep.tile([P, P], F32, name="ident")
-        placed = {name: keep.tile([P, V], U8, name="placed_" + name, align_bytes=64) for name in ("w1", "w2")}
+        ident = keep.tile([P, P], F32, name="ident", align_bytes=LINE)
+        placed = {name: keep.tile([P, V], U8, name="placed_" + name, align_bytes=LINE) for name in ("w1", "w2")}
         picked = {
-            "w1": shared.tile([P, V], U8, name="picked_w1", offset=2 * stage, align_bytes=64),
-            "w2": keep.tile([P, S], U8, name="picked_w2", align_bytes=64),
+            "w1": shared.tile([P, V], U8, name="picked_w1", offset=2 * stage, align_bytes=LINE),
+            "w2": keep.tile([P, S], U8, name="picked_w2", align_bytes=LINE),
         }
         raw = {
             "w1": [
-                shared.tile([P, PACK, N // 2], F32, name="raw_w1_0", offset=5 * stage, align_bytes=64),
-                shared.tile([P, PACK, N // 2], F32, name="raw_w1_1", offset=6 * stage, align_bytes=64),
+                shared.tile([P, PACK, N // 2], F32, name="raw_w1_0", offset=5 * stage, align_bytes=LINE),
+                shared.tile([P, PACK, N // 2], F32, name="raw_w1_1", offset=6 * stage, align_bytes=LINE),
             ]
         }
 
@@ -81,8 +82,8 @@ def tile_picked_ivfpq_none_po_kernel(
                 )
 
         raw["w2"] = [
-            keep.tile([P, PACK, N // 2], F32, name="raw_w2_0", align_bytes=64),
-            shared.tile([P, PACK, N // 2], F32, name="raw_w2_1", offset=stage, align_bytes=64),
+            keep.tile([P, PACK, N // 2], F32, name="raw_w2_0", align_bytes=LINE),
+            shared.tile([P, PACK, N // 2], F32, name="raw_w2_1", offset=stage, align_bytes=LINE),
         ]
         place("w1")
         load_weights("w2", w2, 0)
@@ -91,8 +92,8 @@ def tile_picked_ivfpq_none_po_kernel(
         place("w2")
 
         spread_ps = psum.tile([P, PACK, P], F32, name="spread_ps", tag="bank_4")
-        dn_sb = keep.tile([P, HALF], F32, name="dn_sb")
-        dn_far = shared.tile([P, HALF], F32, name="dn_far", offset=4 * stage, align_bytes=64)
+        dn_sb = keep.tile([P, HALF], F32, name="dn_sb", align_bytes=LINE)
+        dn_far = shared.tile([P, HALF], F32, name="dn_far", offset=4 * stage, align_bytes=LINE)
         for i in range(PACK):
             nc.tensor.transpose(spread_ps[:, i, :], dn_four[:, i : i + 1].to_broadcast([P, P]), ident[:])
         for target, part in ((dn_far, slice(P // 2, P)), (dn_sb, slice(0, P // 2))):
@@ -106,16 +107,16 @@ def tile_picked_ivfpq_none_po_kernel(
         for b in range(2):
             nc.scalar.copy(out=dn_col[b][:], in_=dn_ps[:, b, 0:1])
 
-        cent_words = keep.tile([P, V], U32, name="cent_words", align_bytes=64)
-        far_words = keep.tile([P, HALF], U32, name="far_words", align_bytes=64)
+        cent_words = keep.tile([P, V], U32, name="cent_words", align_bytes=LINE)
+        far_words = keep.tile([P, HALF], U32, name="far_words", align_bytes=LINE)
         nc.vector.tensor_copy(cent_words[:], xw[:].bitcast(U32).indirect(cent_sb[:]))
         nc.vector.tensor_copy(far_words[:], xw[:].bitcast(U32).indirect(offs_sb[:, HALF // 16 :]))
 
         grouped, codes, scales = {}, {}, {}
-        grouped["w1"] = shared.tile([P, PACK, P, PACK], BF16, name="grouped_w1", offset=4 * stage, align_bytes=64)
+        grouped["w1"] = shared.tile([P, PACK, P, PACK], BF16, name="grouped_w1", offset=4 * stage, align_bytes=LINE)
         for name in ("w1", "w2"):
-            codes[name] = keep.tile([P, N], U32, name="codes_" + name, align_bytes=64)
-            scales[name] = keep.tile([P, N], U8, name="scales_" + name, align_bytes=64)
+            codes[name] = keep.tile([P, N], U32, name="codes_" + name, align_bytes=LINE)
+            scales[name] = keep.tile([P, N], U8, name="scales_" + name, align_bytes=LINE)
         pairs = [slice(0, 2), slice(2, PACK)]
         halves = [slice(0, HALF), slice(HALF, S)]
         blocks = [slice(HALF, HALF + P), slice(HALF + P, S)]
@@ -154,12 +155,12 @@ def tile_picked_ivfpq_none_po_kernel(
             round_weights(nc.scalar.copy, "w1", 1, pair, high_rows)
         quantize_weights("w1", slice(0, 1))
         quantize_weights("w1", slice(1, PACK))
-        near_words = shared.tile([P, HALF], U32, name="near_words", offset=6 * stage + stage // 2, align_bytes=64)
+        near_words = shared.tile([P, HALF], U32, name="near_words", offset=6 * stage + stage // 2, align_bytes=LINE)
         nc.vector.tensor_copy(near_words[:], xw[:].bitcast(U32).indirect(offs_sb[:, : HALF // 16]))
 
         def round_w2(half, shares):
             rounded_w2 = shared.tile(
-                [P, PACK, P // 2, PACK], BF16, name="rounded_w2_%d" % half, offset=(6 + half) * stage, align_bytes=64
+                [P, PACK, P // 2, PACK], BF16, name="rounded_w2_%d" % half, offset=(6 + half) * stage, align_bytes=LINE
             )
             for copy, deals, rows in shares:
                 copy(
@@ -185,7 +186,7 @@ def tile_picked_ivfpq_none_po_kernel(
 
         c_rows = []
         for t in range(PACK):
-            c_t = keep.tile([P, V], F32, name="c_%d" % t, align_bytes=64)
+            c_t = keep.tile([P, V], F32, name="c_%d" % t, align_bytes=LINE)
             parts = [(slice(0, V), t, qn_sb[:, t : t + 1])]
             if t == 0:
                 parts = [(slice(0, V // 2), 0, qn_sb[:, 0:1]), (slice(V // 2, V), 6, qn_sb[:, 0:1])]
@@ -198,7 +199,7 @@ def tile_picked_ivfpq_none_po_kernel(
         def offsets(cols):
             return own_sb[:, cols.start // 16 : cols.stop // 16]
 
-        fetched_near = keep.tile([P, PACK, HALF], F32, name="fetched_near")
+        fetched_near = keep.tile([P, PACK, HALF], F32, name="fetched_near", align_bytes=LINE)
 
         def fetch_near(t):
             nc.vector.tensor_tensor(fetched_near[:, t, :], c_rows[t][:].indirect(offsets(halves[0])), dn_sb[:], ALU.add)
@@ -229,15 +230,15 @@ def tile_picked_ivfpq_none_po_kernel(
                 product(acc[:, t - pair.start, :], "w2", t, near_words, slice(0, HALF))
             near_ps.append(acc)
 
-        y_scales = keep.tile([P, S], U8, name="y_scales", align_bytes=64)
+        y_scales = keep.tile([P, S], U8, name="y_scales", align_bytes=LINE)
         out_rows = out_0.rearrange("(p t) j -> p t j", t=PACK)
         out_words = out_1[0].rearrange("p n t -> p (n t)").bitcast(I32)
         fetched_far = [
-            keep.tile([P, 2, HALF], F32, name="fetched_far_0"),
+            keep.tile([P, 2, HALF], F32, name="fetched_far_0", align_bytes=LINE),
             shared.tile([P, 2, HALF], F32, name="fetched_far_1", offset=3 * stage),
         ]
-        y_near = keep.tile([P, PACK, HALF], F32, name="y_near")
-        y_far = keep.tile([P, PACK, HALF], F32, name="y_far")
+        y_near = keep.tile([P, PACK, HALF], F32, name="y_near", align_bytes=LINE)
+        y_far = keep.tile([P, PACK, HALF], F32, name="y_far", align_bytes=LINE)
 
         def fetch_far(t):
             nc.scalar.activation(
@@ -256,7 +257,7 @@ def tile_picked_ivfpq_none_po_kernel(
         fetch_far(1)
         turned = []
         for b in range(2):
-            turned.append(keep.tile([P, N], F32, name="turned_%d" % b))
+            turned.append(keep.tile([P, N], F32, name="turned_%d" % b, align_bytes=LINE))
             nc.scalar.activation(
                 out=turned[b][:], in_=turned_banks[b][:], func=ACT.Identity, bias=dn_col[b][:], scale=-2.0
             )
@@ -288,8 +289,8 @@ def tile_picked_ivfpq_none_po_kernel(
                 )
             nc.sync.dma_start(out=out_rows[:, pair, HALF:], in_=y_far[:, pair, :])
 
-        rounded = [keep.tile([P, HALF, PACK], BF16, name="rounded_%d" % h, align_bytes=64) for h in range(2)]
-        y_words = shared.tile([P, S], I32, name="y_words", offset=3 * stage, align_bytes=64)
+        rounded = [keep.tile([P, HALF, PACK], BF16, name="rounded_%d" % h, align_bytes=LINE) for h in range(2)]
+        y_words = shared.tile([P, S], I32, name="y_words", offset=3 * stage, align_bytes=LINE)
         round_y(nc.scalar.copy, rounded[0][:], y_near[:])
         cut = 3 * HALF // 4
         round_y(nc.vector.tensor_copy, rounded[1][:, :P, :], y_far[:, :, :P])

@@ -196,6 +196,10 @@ def tile_picked_ivfpq_none_po_kernel(
                 nc.scalar.activation(out=c_t[:, cols], in_=acc[:], func=ACT.Identity, bias=norm, scale=-2.0)
             c_rows.append(c_t)
 
+        idle = psum.tile([P, 3 * P], F32, name="idle", tag="bank_7")
+        product(idle[:, : 2 * P], "w1", 3, cent_words, slice(0, 2 * P))
+        product(idle[:, 2 * P :], "w1", 3, cent_words, slice(2 * P, 3 * P))
+
         def offsets(cols):
             return own_sb[:, cols.start // 16 : cols.stop // 16]
 

@@ -310,8 +310,7 @@ def tile_picked_ivfpq_none_po_kernel(
         quantize_y(y_words[:, halves[1]], halves[1], rounded[1][:])
         nc.sync.dma_start(out=out_words, in_=y_words[:])
         for q in range(4):
-            engine = nc.scalar if q % 2 else nc.sync
-            engine.dma_start(
+            nc.scalar.dma_start(
                 out=out_2[0][4 * q : 4 * q + 4, :].bitcast(I32),
                 in_=y_scales[32 * q : 32 * q + 4, :].bitcast(I32),
             )

from contextlib import ExitStack

import concourse.mybir as mybir
from concourse.masks import make_identity

K, T, S, V, N = 512, 2048, 512, 512, 512
FLOPS = 2 * K * N * (V + S)

F32 = mybir.dt.float32
BF16 = mybir.dt.bfloat16
I32 = mybir.dt.int32
U32 = mybir.dt.uint32
U16 = mybir.dt.uint16
U8 = mybir.dt.uint8
FP8X4 = mybir.dt.float8_e4m3fn_x4
ALU = mybir.AluOpType
ACT = mybir.ActivationFunctionType

P = 128
PACK = 4
HALF = S // 2
LINE = 256


def tile_picked_ivfpq_none_po_kernel(
    tc, x_words, x_scales, w1, w2, dn, qn, offs, cent, own, out_0, out_1, out_2
):
    nc = tc.nc
    with ExitStack() as ctx:
        keep = ctx.enter_context(tc.tile_pool(name="keep", bufs=1))
        shared = ctx.enter_context(tc.tile_pool(name="shared", bufs=1))
        psum = ctx.enter_context(tc.psum_pool(name="psum", bufs=1))

        stage = PACK * (N // 2) * 4
        cent_sb = keep.tile([P, V // 16], U16, name="cent_sb")
        offs_sb = keep.tile([P, S // 16], U16, name="offs_sb")
        own_sb = keep.tile([P, S // 16], U16, name="own_sb")
        xs = shared.tile([P, T], U8, name="xs", offset=stage - T // 2, align_bytes=LINE)
        xw = keep.tile([P, T], I32, name="xw", align_bytes=LINE)
        qn_sb = keep.tile([P, PACK], F32, name="qn_sb")
        ident = keep.tile([P, P], F32, name="ident", align_bytes=LINE)
        placed = {name: keep.tile([P, V], U8, name="placed_" + name, align_bytes=LINE) for name in ("w1", "w2")}
        picked = {
            "w1": shared.tile([P, V], U8, name="picked_w1", offset=2 * stage, align_bytes=LINE),
            "w2": keep.tile([P, S], U8, name="picked_w2", align_bytes=LINE),
        }
        raw = {
            "w1": [
                shared.tile([P, PACK, N // 2], F32, name="raw_w1_0", offset=5 * stage, align_bytes=LINE),
                shared.tile([P, PACK, N // 2], F32, name="raw_w1_1", offset=6 * stage, align_bytes=LINE),
            ]
        }

        def load_weights(name, source, half):
            columns = source[:, half * N // 2 : (half + 1) * N // 2]
            nc.sync.dma_start(out=raw[name][half][:], in_=columns.rearrange("(p j) c -> p j c", j=PACK))

        nc.vector.memset(xs[:].bitcast(I32), 0)
        x_rows = x_words[0].rearrange("p n t -> p (n t)").bitcast(I32)
        nc.sync.dma_start(out=xw[:, : T // 8], in_=x_rows[:, : T // 8])
        nc.sync.dma_start(cent_sb[:], cent)
        nc.sync.dma_start(offs_sb[:], offs)
        nc.sync.dma_start(out=xs[0:P:8, :].bitcast(I32), in_=x_scales[0].bitcast(I32))
        nc.scalar.dma_start(out=qn_sb[:], in_=qn.rearrange("(p t) o -> p (t o)", t=PACK))
        dn_four = keep.tile([P, PACK], F32, name="dn_four")
        nc.scalar.dma_start(out=dn_four[:], in_=dn[0].rearrange("(p i) -> p i", i=PACK))
        nc.sync.dma_start(out=xw[:, T // 8 :], in_=x_rows[:, T // 8 :])
        for half in range(2):
            load_weights("w1", w1, half)

        make_identity(nc, ident[:])
        for name in ("w1", "w2"):
            nc.vector.memset(placed[name][:].bitcast(I32), 0)

        nc.vector.tensor_copy(picked["w1"][:], xs[:].indirect(cent_sb[:]))
        nc.vector.tensor_copy(picked["w2"][:], xs[:].indirect(offs_sb[:]))

        def place(name):
            for r in range(4):
                nc.sync.dma_start(
                    out=placed[name][r:P:32, :].bitcast(I32), in_=picked[name][8 * r : P : 32, :].bitcast(I32)
                )

        raw["w2"] = [
            keep.tile([P, PACK, N // 2], F32, name="raw_w2_0", align_bytes=LINE),
            shared.tile([P, PACK, N // 2], F32, name="raw_w2_1", offset=stage, align_bytes=LINE),
        ]
        place("w1")
        load_weights("w2", w2, 0)
        load_weights("w2", w2, 1)
        nc.sync.dma_start(own_sb[:], own)
        place("w2")

        spread_ps = psum.tile([P, PACK, P], F32, name="spread_ps", tag="bank_4")
        dn_sb = keep.tile([P, HALF], F32, name="dn_sb", align_bytes=LINE)
        dn_far = shared.tile([P, HALF], F32, name="dn_far", offset=4 * stage, align_bytes=LINE)
        for i in range(PACK):
            nc.tensor.transpose(spread_ps[:, i, :], dn_four[:, i : i + 1].to_broadcast([P, P]), ident[:])
        for target, part in ((dn_far, slice(P // 2, P)), (dn_sb, slice(0, P // 2))):
            nc.scalar.copy(
                out=target[:].rearrange("m (p i) -> m p i", i=PACK), in_=spread_ps[:, :, part].rearrange("m i p -> m p i")
            )
        dn_ps = psum.tile([P, 2, P], F32, name="dn_ps", tag="bank_5")
        dn_col = [shared.tile([P, 1], F32, name="dn_col_0", offset=3 * stage), keep.tile([P, 1], F32, name="dn_col_1")]
        for b in range(2):
            nc.tensor.transpose(dn_ps[:, b, :], dn_far[:, b * P : (b + 1) * P], ident[:])
        for b in range(2):
            nc.scalar.copy(out=dn_col[b][:], in_=dn_ps[:, b, 0:1])

        cent_words = keep.tile([P, V], U32, name="cent_words", align_bytes=LINE)
        far_words = keep.tile([P, HALF], U32, name="far_words", align_bytes=LINE)
        nc.vector.tensor_copy(cent_words[:], xw[:].bitcast(U32).indirect(cent_sb[:]))
        nc.vector.tensor_copy(far_words[:], xw[:].bitcast(U32).indirect(offs_sb[:, HALF // 16 :]))

        grouped, codes, scales = {}, {}, {}
        grouped["w1"] = shared.tile([P, PACK, P, PACK], BF16, name="grouped_w1", offset=4 * stage, align_bytes=LINE)
        for name in ("w1", "w2"):
            codes[name] = keep.tile([P, N], U32, name="codes_" + name, align_bytes=LINE)
            scales[name] = keep.tile([P, N], U8, name="scales_" + name, align_bytes=LINE)
        pairs = [slice(0, 2), slice(2, PACK)]
        halves = [slice(0, HALF), slice(HALF, S)]
        blocks = [slice(HALF, HALF + P), slice(HALF + P, S)]

        def round_weights(copy, name, half, deals, rows):
            placed_rows = slice(half * P // 2 + rows.start, half * P // 2 + rows.stop)
            copy(
                out=grouped[name][:, deals, placed_rows, :].rearrange("p t m j -> p m j t"),
                in_=raw[name][half][:].rearrange("p j (m t) -> p m j t", t=PACK)[:, rows, :, deals],
            )

        def quantize_weights(name, deals):
            cols = slice(deals.start * P, deals.stop * P)
            nc.vector.quantize_mx(
                out=codes[name][:, cols].bitcast(FP8X4),
                scales=scales[name][:, cols],
                in_=grouped[name][:, deals, :, :].rearrange("p t m j -> p (t m j)"),
            )

        def product(acc, name, t, words, cols):
            deal = slice(t * P, (t + 1) * P)
            nc.tensor.matmul_mx(
                out=acc,
                lhsT=codes[name][:, deal].bitcast(FP8X4),
                lhsT_scale=scales[name][:, deal],
                rhs=words[:, cols].bitcast(FP8X4),
                rhs_scale=placed[name][:, cols],
                start=True,
                stop=True,
            )

        all_rows, low_rows, high_rows = slice(0, P // 2), slice(0, P // 4), slice(P // 4, P // 2)
        round_weights(nc.scalar.copy, "w1", 0, slice(0, PACK), all_rows)
        for pair in pairs:
            round_weights(nc.vector.tensor_copy, "w1", 1, pair, low_rows)
            round_weights(nc.scalar.copy, "w1", 1, pair, high_rows)
        quantize_weights("w1", slice(0, 1))
        quantize_weights("w1", slice(1, PACK))
        near_words = shared.tile([P, HALF], U32, name="near_words", offset=6 * stage + stage // 2, align_bytes=LINE)
        nc.vector.tensor_copy(near_words[:], xw[:].bitcast(U32).indirect(offs_sb[:, : HALF // 16]))

        def round_w2(half, shares):
            rounded_w2 = shared.tile(
                [P, PACK, P // 2, PACK], BF16, name="rounded_w2_%d" % half, offset=(6 + half) * stage, align_bytes=LINE
            )
            for copy, deals, rows in shares:
                copy(
                    out=rounded_w2[:, deals, rows].rearrange("p t m j -> p m j t"),
                    in_=raw["w2"][half][:].rearrange("p j (m t) -> p m j t", t=PACK)[:, rows, :, deals],
                )
            return rounded_w2

        def quantize_w2(half, rounded_w2, deals):
            for t in deals:
                cols = slice(t * P + half * P // 2, t * P + (half + 1) * P // 2)
                nc.vector.quantize_mx(
                    out=codes["w2"][:, cols].bitcast(FP8X4),
                    scales=scales["w2"][:, cols],
                    in_=rounded_w2[:, t].rearrange("p m j -> p (m j)"),
                )

        first_shares = [
            (nc.vector.tensor_copy, pairs[0], all_rows),
            (nc.vector.tensor_copy, pairs[1], all_rows),
        ]
        quantize_w2(0, round_w2(0, first_shares), range(PACK))

        c_rows = []
        for t in range(PACK):
            c_t = keep.tile([P, V], F32, name="c_%d" % t, align_bytes=LINE)
            parts = [(slice(0, V), t, qn_sb[:, t : t + 1])]
            if t == 0:
                parts = [(slice(0, V // 2), 0, qn_sb[:, 0:1]), (slice(V // 2, V), 6, qn_sb[:, 0:1])]
            for cols, bank, norm in parts:
                acc = psum.tile([P, cols.stop - cols.start], F32, name="acc", tag="bank_%d" % bank)
                product(acc[:], "w1", t, cent_words, cols)
                nc.scalar.activation(out=c_t[:, cols], in_=acc[:], func=ACT.Identity, bias=norm, scale=-2.0)
            c_rows.append(c_t)

        idle = psum.tile([P, 3 * P], F32, name="idle", tag="bank_7")
        product(idle[:, : 2 * P], "w1", 3, cent_words, slice(0, 2 * P))
        product(idle[:, 2 * P :], "w1", 3, cent_words, slice(2 * P, 3 * P))

        def offsets(cols):
            return own_sb[:, cols.start // 16 : cols.stop // 16]

        fetched_near = keep.tile([P, PACK, HALF], F32, name="fetched_near", align_bytes=LINE)

        def fetch_near(t):
            nc.vector.tensor_tensor(fetched_near[:, t, :], c_rows[t][:].indirect(offsets(halves[0])), dn_sb[:], ALU.add)

        last_rounded = round_w2(1, [(nc.vector.tensor_copy, pair, all_rows) for pair in pairs])
        fetch_near(0)
        quantize_w2(1, last_rounded, range(PACK))

        turned_banks = []
        for b, cols in enumerate(blocks):
            turned_ps = psum.tile([P, N], F32, name="turned_ps", tag="bank_%d" % (6 + b))
            turned_banks.append(turned_ps)
            for pair in pairs:
                rows = slice(pair.start * P, pair.stop * P)
                nc.tensor.matmul_mx(
                    out=turned_ps[:, rows],
                    lhsT=far_words[:, b * P : (b + 1) * P].bitcast(FP8X4),
                    lhsT_scale=placed["w2"][:, cols],
                    rhs=codes["w2"][:, rows].bitcast(FP8X4),
                    rhs_scale=scales["w2"][:, rows],
                    start=True,
                    stop=True,
                )
        near_ps = []
        for index, pair in enumerate(pairs):
            acc = psum.tile([P, 2, HALF], F32, name="near_ps", tag="bank_%d" % (4 + index))
            for t in range(pair.start, pair.stop):
                product(acc[:, t - pair.start, :], "w2", t, near_words, slice(0, HALF))
            near_ps.append(acc)

        y_scales = keep.tile([P, S], U8, name="y_scales", align_bytes=LINE)
        out_rows = out_0.rearrange("(p t) j -> p t j", t=PACK)
        out_words = out_1[0].rearrange("p n t -> p (n t)").bitcast(I32)
        fetched_far = [
            keep.tile([P, 2, HALF], F32, name="fetched_far_0", align_bytes=LINE),
            shared.tile([P, 2, HALF], F32, name="fetched_far_1", offset=3 * stage),
        ]
        y_near = keep.tile([P, PACK, HALF], F32, name="y_near", align_bytes=LINE)
        y_far = keep.tile([P, PACK, HALF], F32, name="y_far", align_bytes=LINE)

        def fetch_far(t):
            nc.scalar.activation(
                out=fetched_far[t // 2][:, t % 2, :], in_=c_rows[t][:].indirect(offsets(halves[1])), func=ACT.Copy
            )

        def round_y(copy, target, values):
            copy(
                out=target.rearrange("p (c i) t -> p c t i", i=4),
                in_=values.rearrange("p t (c i) -> p c t i", i=4),
            )

        for t in range(1, PACK):
            fetch_near(t)
        fetch_far(0)
        fetch_far(1)
        turned = []
        for b in range(2):
            turned.append(keep.tile([P, N], F32, name="turned_%d" % b, align_bytes=LINE))
            nc.scalar.activation(
                out=turned[b][:], in_=turned_banks[b][:], func=ACT.Identity, bias=dn_col[b][:], scale=-2.0
            )
        fetch_far(2)
        fetch_far(3)
        back = []
        for index, pair in enumerate(pairs):
            back.append(psum.tile([P, 2, HALF], F32, name="back", tag="bank_%d" % index))
            for b in range(2):
                for t in range(pair.start, pair.stop):
                    nc.tensor.transpose(
                        back[index][:, t - pair.start, b * P : (b + 1) * P], turned[b][:, t * P : (t + 1) * P], ident[:]
                    )

        for index, pair in enumerate(pairs):
            nc.vector.scalar_tensor_tensor(
                out=y_near[:, pair, :],
                in0=near_ps[index][:],
                scalar=-2.0,
                in1=fetched_near[:, pair, :],
                op0=ALU.mult,
                op1=ALU.add,
            )
            nc.sync.dma_start(out=out_rows[:, pair, :HALF], in_=y_near[:, pair, :])
        for index, pair in enumerate(pairs):
            for part in [slice(0, HALF)] if index == 0 else [slice(0, P), slice(P, HALF)]:
                nc.vector.tensor_tensor(
                    y_far[:, pair, part], back[index][:, :, part], fetched_far[index][:, :, part], ALU.add
                )
            nc.sync.dma_start(out=out_rows[:, pair, HALF:], in_=y_far[:, pair, :])

        rounded = [keep.tile([P, HALF, PACK], BF16, name="rounded_%d" % h, align_bytes=LINE) for h in range(2)]
        y_words = shared.tile([P, S], I32, name="y_words", offset=3 * stage, align_bytes=LINE)
        round_y(nc.scalar.copy, rounded[0][:], y_near[:])
        cut = 3 * HALF // 4
        round_y(nc.vector.tensor_copy, rounded[1][:, :P, :], y_far[:, :, :P])
        round_y(nc.vector.tensor_copy, rounded[1][:, P:cut, :], y_far[:, :, P:cut])
        round_y(nc.scalar.copy, rounded[1][:, cut:, :], y_far[:, :, cut:])

        def quantize_y(words, cols, values):
            nc.vector.quantize_mx(
                out=words.bitcast(FP8X4), scales=y_scales[:, cols], in_=values.rearrange("p c t -> p (c t)")
            )

        quantize_y(y_words[:, halves[0]], halves[0], rounded[0][:])
        quantize_y(y_words[:, halves[1]], halves[1], rounded[1][:])
        nc.sync.dma_start(out=out_words, in_=y_words[:])
        for q in range(4):
            nc.scalar.dma_start(
                out=out_2[0][4 * q : 4 * q + 4, :].bitcast(I32),
                in_=y_scales[32 * q : 32 * q + 4, :].bitcast(I32),
            )
